import numpy as np, ml_dtypes
CORES = [16,17,18,19,32,33,34,35]
N = 8
BF = ml_dtypes.bfloat16
def gentries(a):
    return np.ascontiguousarray(a.reshape(8, 16, -1).transpose(0, 2, 1)).reshape(8, -1)
def gtable(e):
    e = np.asarray(e); return np.ascontiguousarray(e.reshape(8, -1, 16).transpose(0, 2, 1)).reshape(128, -1).astype(np.int32)
V, R, M, RO, P, H, CAP, NEED = 4096, 2816, 2, 3, 4, 2, 128, 9
S, TOP = V // N, 2 ** 20 - 1
def parts(rng):
    base = rng.integers(0, 2 ** 20, (1, 8, 16, 1)); amp = np.exp2(10 + 7 * rng.random((N, 8, 1, R)))
    x = np.clip(base + amp * rng.standard_normal((N, 8, 16, R)), 0, TOP).astype(np.int64)
    t = (np.exp2(14 + 3.5 * rng.random((N, 8, 1, 1))) * (0.5 + rng.random((N, 8, 16, 1)))).astype(np.int64)
    lv = rng.integers(0, V, (N, 8, P, R)); lv = np.where(rng.random((N, 8, 1, R)) < 0.5, np.sort(lv, axis=2), lv)
    cd = rng.integers(0, R, (N, 8, RO, M, V))
    return x, t, lv, cd
def pack(x, t, lv, cd):
    return {"px": np.ascontiguousarray(x.reshape(N, 128, R)).astype(np.int32), "th": np.ascontiguousarray(t.reshape(N, 128, 1)).astype(np.int32),
            "ray": np.stack([gtable(a.reshape(8, -1)) for a in lv]), "cand": np.stack([gtable(a.reshape(8, -1)) for a in cd])}
def setup_inputs(rng):
    return pack(*parts(rng))
def setup_inputs_room(rng):
    x, t, lv, cd = parts(rng); h = R // 8
    t = rng.integers(2 ** 14, 2 ** 15, (N, 8, 16, 1)); x = rng.integers(2 ** 18, 2 ** 19, (1, 8, 16, 1)) + rng.integers(0, 2 ** 13, (N, 8, 16, R))
    inc = np.zeros((8, V), bool); own = np.arange(V) // S
    for o in range(N):
        for g in range(8):
            n = int(rng.choice(np.array([0, 1, CAP - 1, CAP, CAP + 1, S]))); last = o == N - 1 and g < 4
            if o == 0: n = (CAP, CAP + 1, S, CAP - 1, 1, 0, CAP, CAP + 1)[g]
            if last: n = (CAP, 1, CAP - 1, CAP)[g]
            s = rng.permutation(S)[:n]
            if last and not np.any(s == S - 1): s[0] = S - 1
            inc[g, o * S + s] = True
    for a in range(N):
        for g in range(8):
            o = rng.permutation(R); hot, watch, calm = o[:h], o[h:2 * h], o[h:]
            m = np.argsort(rng.random((16, h)), axis=0) < rng.integers(NEED, 17, h)
            x[a, g][:, hot] += m * (rng.choice(np.array([-1, 1]), h) * rng.integers(2 ** 16, 2 ** 17, h))
            lv[a, g, 0, o[:2 * h]] = V - 1; cd[a, g, 0] = rng.choice(calm, (M, V))
            for who, back in ((hot, 1), (watch, 2)):
                v = np.flatnonzero(inc[g] & ((own + back) % N == a))
                cd[a, g, 0, rng.integers(0, M, len(v)), v] = rng.choice(who, len(v))
    return pack(x, t, lv, cd)
def setup_inputs_ties(rng):
    x, t, lv, cd = parts(rng); n = min(R // 8, S)
    base = rng.choice(np.array([0, 2 ** 19, TOP]), 8); base[0] = 0; base[1] = TOP; base[2] = 2 ** 19; sg = np.where(base > 2 ** 19, -1, 1)
    t = rng.choice(np.array([0, 1, 1000, 2 ** 18, 2 ** 19 - 8]), (N, 8, 1, 1)) + rng.integers(0, 3, (N, 8, 16, 1))
    x = np.tile(base.reshape(1, 8, 1, 1), (N, 1, 16, R))
    for a in range(N):
        for g in range(8):
            o = rng.permutation(R); hot, watch, calm = o[:n], o[n:2 * n], o[n:]; b, e = (a - 1) % N, (a - 2) % N
            m = (np.argsort(rng.random((16, n)), axis=0) < rng.choice(np.array([NEED - 1, NEED, 16]), n)).astype(np.int64)
            x[a, g][:, hot] = base[g] + sg[g] * (t[b, g] + m)
            v = b * S + rng.permutation(S)[:n]
            lv[a, g, 0, hot] = np.where(rng.random(n) < 0.4, v, np.where(rng.random(n) < 0.5, V - 1, np.maximum(v - 1, 0)))
            lv[a, g, 0, watch] = V - 1
            cd[a, g, 0] = rng.choice(calm, (M, V)); cd[a, g, 0, 0, v] = hot
            cd[a, g, 0, M - 1, e * S:(e + 1) * S] = rng.choice(watch, S)
    return pack(x, t, lv, cd)
def setup_inputs_alike(rng):
    x, t, lv, cd = parts(rng)
    cd[:, ::4] = rng.choice(np.array([0, R - 1, R // 2, 5]), (N, 2, RO, M, V)); cd[:, 3] = cd[:, 3][:, :, :1]
    lv[:, 1::2] = lv[:, 1::2, :1]
    lv[:, 2] = rng.choice(np.array([0, V - 1]), (N, P, R)); lv[:, 6] = rng.integers(0, 16, (N, P, R))
    return pack(x, t, lv, cd)
def setup_inputs_dim(rng):
    x, t, lv, cd = parts(rng); q = rng.permutation(N); k = int(rng.integers(0, 7)); o = int(q[1])
    lv[:, k] = lv[:, k] // 2; lv[q[0], :7] = rng.integers(0, 4, (7, P, R)); t[o] = TOP; t[q[2]] = 0
    for a, pixel in ((int(q[0]), 0), (int(q[3]), TOP)):
        s = rng.permutation(R)[:R // 16]; x[a, 7][:, s] = pixel; lv[a, 7, 0, s] = V - 1
        cd[a, 7, 0, 0, o * S:(o + 1) * S] = rng.choice(s, S)
    return pack(x, t, lv, cd)
def setup_inputs_spread(rng):
    x, t, lv, cd = parts(rng)
    t = np.minimum(np.exp2(10 + 10 * rng.random((N, 8, 16, 1))).astype(np.int64), TOP)
    x = np.minimum((np.exp2(20 * rng.random((N, 8, 1, R))) * rng.random((N, 8, 16, R))).astype(np.int64), TOP)
    return pack(x, t, lv, cd)
def check_inputs(d):
    bad = []
    for k, lo, hi in (("px", 0, TOP), ("th", 0, TOP), ("ray", 0, V - 1), ("cand", 0, R - 1)):
        if np.min(d[k]) < lo or np.max(d[k]) > hi: bad.append("range of " + k)
    return bad
def reference(px, th, ray, cand):
    x = px.astype(np.int64).reshape(N, 8, 16, R); t = th.astype(np.int64).reshape(N, 8, 16, 1)
    lv = np.stack([gentries(a) for a in ray]).astype(np.int64).reshape(N, 8, P, R)
    cd = np.stack([gentries(a) for a in cand]).astype(np.int64).reshape(N, 8, RO, M, V)
    c = np.zeros((N, 8, R), np.int64); number = np.arange(V)
    for rnd in range(RO):
        w = np.take_along_axis(lv, c[:, :, None, :], 2)[:, :, 0]
        lo = np.full((8, 16, V), TOP + 1, np.int64); hi = np.full((8, 16, V), -1, np.int64)
        for a in range(N):
            for m in range(M):
                ix = cd[a, :, rnd, m]
                sees = (number <= np.take_along_axis(w[a], ix, 1))[:, None, :]
                v = np.take_along_axis(x[a], ix[:, None, :], 2)
                lo = np.minimum(lo, np.where(sees, v, TOP + 1)); hi = np.maximum(hi, np.where(sees, v, -1))
        carved = np.zeros((8, V), bool)
        for o in range(N):
            far = (hi[:, :, o * S:(o + 1) * S] - lo[:, :, o * S:(o + 1) * S] > t[o]).astype(np.int64)
            odd = np.add.reduce(far, axis=1) >= NEED
            carved[:, o * S:(o + 1) * S] = odd & (np.add.accumulate(odd.astype(np.int64), axis=1) <= CAP)
        for step in range(H):
            w = np.take_along_axis(lv, c[:, :, None, :], 2)[:, :, 0]
            nx, nc = [], []
            for a in range(N):
                gone = np.take_along_axis(carved, w[a], 1); e = np.take_along_axis(lo, w[a][:, None, :], 2)
                nx.append(np.where(gone[:, None, :], np.clip(x[a] + ((x[a] - e) >> 2), 0, TOP), x[a]))
                nc.append(np.minimum(c[a] + gone.astype(np.int64), P - 1))
            x = np.stack(nx); c = np.stack(nc)
    yc = np.stack([gtable(c[a]) for a in range(N)])
    return {"yx": x.reshape(N, 128, R).astype(np.float32), "yc": yc.astype(np.float32)}

@@ -1,0 +1,519 @@
+from concourse.bass import DstId, RemoteDMATransfer
+from concourse.mybir import dt, AluOpType, AxisListType, ActivationFunctionType
+
+A = AluOpType
+F = ActivationFunctionType
+R, V, TOP, BIG = 2816, 4096, 2 ** 20 - 1, 2 ** 22
+U = 4096.0
+NC = 4
+PIECES = ((0, 96), (96, 176))
+KB = 3
+SCHED = "L00s L01v X0 L10s X1 L11v M0 Z0 M1 L20s V0 L21v Z1 L30s L31v M2 V1 Z2 M3 V2 Z3 V3 R03 R34"
+f32, i32, u16, f16, b16 = "float32", "int32", "uint16", "float16", "bfloat16"
+SCRATCH = {n: ("sbuf", [128] + list(sh), d) for n, sh, d in (
+    ("sta", (2, 8, 4, 8), i32), ("stb", (4, 8, 4, 8), i32), ("stc", (4, 8, 4, 8), i32), ("str", (704,), i32),
+    ("sth", (1,), i32), ("sth2", (2,), i32), ("ls0", (512,), u16), ("ls1", (2048,), u16),
+    ("lsr", (712,), u16), ("ll1", (2048,), u16), ("llr", (712,), u16), ("om", (512,), u16),
+    ("ia", (128,), i32), ("ib", (128,), i32), ("ic", (128,), i32), ("id", (128,), i32), ("ie", (128,), i32),
+    ("ig", (128,), i32), ("es", (3, 128), f32), ("io2", (64,), i32), ("io3", (64,), i32),
+    ("uk", (16, 128), f16), ("dkb", (16, 128), b16), ("ob", (128,), b16), ("ni", (128,), b16),
+    ("pmx", (128,), f32), ("ones", (512,), b16), ("six", (128,), b16), ("vt", (4096,), f32),
+    ("vp", (64,), b16), ("nth", (1,), f32), ("thf", (4,), f32),
+    ("xi", (2816,), i32), ("xf", (2824,), f32), ("xl", (2824,), f32), ("w", (2816,), f32), ("wf", (176,), f32),
+    ("wu", (176,), u16), ("w16", (176,), f16), ("cur", (176,), f32), ("dl", (528,), f32), ("q1", (352,), f32),
+    ("q2", (176,), f32), ("eq", (528,), f32), ("pr", (528,), f32), ("cfin", (176,), f32),
+    ("cf", (512,), f32), ("wg0", (1024,), b16), ("wg1", (1024,), b16), ("mk0", (1024,), b16), ("mk1", (1024,), b16),
+    ("sm", (256,), f32), ("oo", (512,), u16), ("zb0", (1024,), f32), ("zb1", (1024,), f32), ("hb0", (1024,), f32),
+    ("hb1", (1024,), f32), ("lb0", (1024,), f32), ("lb1", (1024,), f32), ("zz", (8, 4, 2, 128), f32), ("hs", (512,), f32),
+    ("fe", (512,), f32), ("far", (512,), b16), ("inc", (512,), b16), ("cum", (512,), f32), ("pc", (512,), b16),
+    ("et", (512,), f32), ("ea", (4096,), f32), ("ag", (2816,), f32), ("sg", (2816,), b16), ("tq", (176,), f32))}
+SCRATCH.update({n: ("dram", list(sh), d) for n, sh, d in (
+    ("l0d", (8, 128, 64), u16), ("l0r", (8, 128, 64), u16), ("l1d", (8, 128, 256), u16), ("l1r", (8, 128, 256), u16),
+    ("lrd", (8, 128, 89), u16), ("lrr", (8, 128, 89), u16), ("pxd", (16, 128, 176), i32), ("pxr", (16, 128, 176), i32),
+    ("rb", (4, 128, 176), i32), ("ro0", (4, 128, 96), f32), ("od0", (16, 128, 96), f32), ("or0", (16, 128, 96), f32),
+    ("ro1", (4, 128, 80), f32), ("od1", (16, 128, 80), f32), ("or1", (16, 128, 80), f32),
+    ("cd", (8, 128, 22), f32), ("cr", (8, 128, 22), f32))})
+SCRATCH.update({n: ("psum", [128, k], f32) for n, k in (("pb", 3072), ("pw", 512), ("pv", 512))})
+PSUM = ["pb%d" % k for k in range(6)] + ["pw", "pv"]
+SEMAPHORES = (["v", "s", "t", "gc", "lsem", "l0a", "l1a", "lra", "ca", "rbi", "ro0i", "ro1i", "rlo"]
+              + [n + str(q) for n in ("pxa", "oa", "ob") for q in range(8)] + [n + str(c) for n in ("rg", "rk") for c in range(NC)]
+              + ["ea0", "ea1", "dst", "dst1", "dl0", "dl1", "dpx", "dpy", "dlb", "dlc", "dxi", "dod0", "dod1", "dcd", "dy", "dz",
+                 "dlr", "dlq"])
+
+
+def layout(T, topo):
+    lay = []
+    for r, c in enumerate(T.cores):
+        mine = [q for q, d in enumerate(T.cores) if topo.chip(d) == topo.chip(c)]
+        far = [q for q in range(len(T.cores)) if q not in mine]
+        other = [d for d in topo.cores_of(c) if topo.die(d) != topo.die(c)]
+        lay.append(([q for q in mine if q != r], far, other[mine.index(r)]))
+    return lay
+
+
+def two(engines, n):
+    return [(1 << engines[2 * k]) | (1 << engines[2 * k + 1]) for k in range(n)]
+
+
+def transfer(topo, dst, mask, src, out, sem):
+    rid, pid, _ = topo.addr(dst)
+    return RemoteDMATransfer(dst_ids=[DstId(rid=rid, pnc=pid)], dma_engine_mask=mask, remote_sem=sem, src=src, dst=out)
+
+
+def relay_program(g, core, T, topo, r, far):
+    masks = two(topo.engines(core, T.cores[far[0]]), len(far))
+    n = 2 * len(far)
+    for s, src, dst, to in (("rbi", T.rb, T.pxr, "pxa"), ("ro0i", T.ro0, T.or0, "oa"), ("ro1i", T.ro1, T.or1, "ob")):
+        g.wait_ge(T.sem[s], n)
+        g.remote_dma_fused([transfer(topo, T.cores[q], masks[k], src[k], dst[2 * r + 1], T.sem[to + str(r)])
+                            for k, q in enumerate(far)], local_sem=T.sem.rlo)
+    g.wait_ge(T.sem.rlo, 3 * n)
+
+
+def rank_program(g, core, T, topo):
+    lay = layout(T, topo)
+    rank = T.rank_of(core)
+    if rank is None:
+        for r, (near, far, rel) in enumerate(lay):
+            if rel == core:
+                relay_program(g, core, T, topo, r, far)
+        return
+    near, far, rel = lay[rank]
+    sem = T.sem
+    queue = {"v": g.vector, "s": g.scalar, "t": g.tensor, "y": g.sync, "g": g}
+    own = {"v": "v", "s": "s", "t": "t", "g": "gc"}
+    cnt, seen, wr, rd = {}, {}, {}, {}
+
+    def waits(q, deps):
+        need = {}
+        for s, n in deps:
+            need[s] = max(need.get(s, 0), n)
+        for s in need:
+            if seen.get((q, s), 0) < need[s]:
+                queue[q].wait_ge(sem[s], need[s])
+                seen[(q, s)] = need[s]
+
+    def deps_of(q, reads, writes):
+        d = []
+        for k in reads + writes:
+            d += wr.get(k, [])
+        for k in writes:
+            d += rd.get(k, {}).items()
+        for k in reads:
+            if k in PSUM:
+                d += [(s, n) for s, n in rd.get(k, {}).items() if s != own.get(q)]
+        return d
+
+    def done(tag, reads, writes):
+        for k in reads:
+            rd.setdefault(k, {})[tag[0]] = tag[1]
+        for k in writes:
+            wr[k] = [tag]
+            rd[k] = {}
+
+    calls = {"mm": g.tensor.matmul, "acts": g.scalar.activation, "act": g.scalar.activation, "iota": g.iota,
+             "copy": g.vector.tensor_copy, "tt": g.vector.tensor_tensor, "ts": g.vector.tensor_scalar, "set": g.vector.memset,
+             "scan": g.vector.tensor_tensor_scan}
+
+    def op(q, name, args, reads, writes, **kw):
+        waits(q, deps_of(q, reads, writes))
+        s = own[q]
+        for a in args if name in ("mm", "acts") else [args]:
+            ins = calls[name](*a, **kw)
+        cnt[s] = cnt.get(s, 0) + 1
+        ins.then_inc(sem[s], 1)
+        done((s, cnt[s]), reads, writes)
+
+    def vts(out, in0, s1, s2, ops, reads, writes):
+        op("v", "ts", (out, in0, s1, s2) + ops, reads, writes)
+
+    def dma(q, pairs, s, reads, writes):
+        waits(q, deps_of(q, reads, writes))
+        for o, i in pairs:
+            queue[q].dma_start(o, i).then_inc(sem[s], 16)
+        cnt[s] = cnt.get(s, 0) + 16 * len(pairs)
+        done((s, cnt[s]), reads, writes)
+
+    def arrives(s, n, key):
+        cnt[s] = cnt.get(s, 0) + n
+        wr[key] = [(s, cnt[s])]
+
+    nf, nn = len(far), len(near)
+    off = topo.engines(core, T.cores[far[0]])
+    rest = [e for e in topo.engines(core, T.cores[near[0]]) if e not in off]
+
+    def send(moves, reads):
+        waits("g", deps_of("g", reads, []))
+        g.remote_dma_fused([transfer(topo, d, m, a, b, sem[s]) for d, m, a, b, s in moves], local_sem=sem.lsem)
+        cnt["lsem"] = cnt.get("lsem", 0) + 2 * len(moves)
+
+    def to_far(src, dst, s):
+        return [(T.cores[q], m, src(q), dst, s) for q, m in zip(far, two(off, nf))]
+
+    def to_relay(src, via, vsem):
+        return [(rel, m, src(q), via[k], vsem) for k, (q, m) in enumerate(zip(far, two(rest, nf)))]
+
+    def to_near(src, dst, s, engines):
+        return [(T.cores[q], m, src(q), dst, s) for q, m in zip(near, two(engines, nn))]
+
+    def to_all(src, dst, s):
+        return to_far(lambda q: src[q], dst[rank], s) + to_near(lambda q: src[q], dst[rank], s, rest)
+
+    def halves(src, dst, s, via, vsem, kf, kn):
+        s = s + str(rank)
+        send(to_relay(lambda q: src[2 * q + 1], via, vsem) + to_far(lambda q: src[2 * q], dst[2 * rank], s), kf)
+        send(to_near(lambda q: src[2 * q], dst[2 * rank], s, rest) + to_near(lambda q: src[2 * q + 1], dst[2 * rank + 1], s, off), kn)
+
+    lo, hi = 16 * rank, 16 * rank + 16
+    npc = range(len(PIECES))
+    others = [(a, b) for a, b in ((0, rank), (rank + 1, 8)) if b > a]
+
+    def land(q, dst, src, mine, s, reads, key):
+        dma(q, [(dst[16 * a:16 * b, :], src[a:b]) for a, b in others] + [(dst[lo:hi, :], mine[lo:hi, :])], s, reads, [key])
+
+    dma("y", [(T.sta[:], T.cand[:, 0:512]), (T["str"][:], T.ray[:]), (T.sth[:], T.th[:])], "dst", [], ["sta", "str", "sth"])
+    fa, fb = far[0], far[-1] + 1
+    na, nb = min(near + [rank]), max(near + [rank]) + 1
+    dma("y", [(T.pxd[2 * fa:2 * fb], T.px[16 * fa:16 * fb, :])], "dpx", [], ["pxdf"])
+    dma("y", [(T.pxd[2 * na:2 * nb], T.px[16 * na:16 * nb, :])], "dpy", [], ["pxdn"])
+    dma("y", [(T.stb[:], T.cand[:, 512:1536]), (T.xi[lo:hi, :], T.px[lo:hi, :])], "dst1", [], ["stb", "xi.own"])
+    op("g", "iota", (T.ia[:], [[-16, 8], [0, 16]], 0, 1), [], ["ia"])
+    op("g", "iota", (T.ib[:], [[-16000, 8], [-999, 16]], 0, 1000), [], ["ib"])
+    op("g", "iota", (T.vt[:, 0:1024], [[512, 8], [1, 128]], -2048, 0), [], ["vt0"], allow_small_or_imprecise_dtypes=True)
+    op("g", "iota", (T.ie[:], [[-1, 128]], 0, 1), [], ["ie"])
+    op("g", "iota", (T.io2[:], [[0, 8], [16, 8]], -64, 0), [], ["io2"])
+    op("g", "iota", (T.io3[:], [[0, 64]], 0, 1), [], ["io3"])
+    op("g", "iota", (T["id"][:], [[-1, 16], [-16, 8]], 0, 1), [], ["id"])
+    op("g", "iota", (T.ic[:], [[0, 16], [1, 8]], 1024, -1), [], ["ic"])
+    op("g", "iota", (T.ig[:], [[0, 8], [-8, 16]], 0, 1), [], ["ig"])
+    halves(T.pxd, T.pxr, "pxa", T.rb, "rbi", ["pxdf"], ["pxdn"])
+    for k in range(16):
+        vts(T.uk[:, k, :], T.ia[:], float(k), None, (A.is_equal,), ["ia"], ["uk" if k == 15 else "uk.%d" % k])
+    w16k, wfk, curk = ["w16.%d" % p for p in npc], ["wf%d" % p for p in npc], ["cur%d" % p for p in npc]
+    vts(T.w16[:], T["str"][:, 0:176], -2048.0, None, (A.add,), ["str"], w16k)
+    for m in range(2):
+        for c in range(NC):
+            k = c * 128 + m * 64
+            op("v", "copy", (T.ls0[:, k:k + 64], T.sta[:, m, :, c, :]), ["sta"], ["ls0.%d" % k])
+    ls0k = ["ls0.%d" % k for k in range(0, 512, 64)]
+    for k in range(16):
+        vts(T.dkb[:, k, :], T.ib[:], float(k), -U, (A.is_equal, A.mult), ["ib"], ["dkb" if k == 15 else "dkb.%d" % k])
+    vts(T.io3[:], T.io3[:], 15, None, (A.bitwise_and,), ["io3"], ["io3"])
+    vts(T.ni[:], T.ie[:], 0.0, -0.25, (A.is_equal, A.mult), ["ie"], ["ni"])
+    op("v", "tt", (T.io2[:], T.io2[:], T.io3[:], A.add), ["io2", "io3"], ["io2"])
+    op("v", "set", (T.six[:], 64.0), [], ["six"])
+    vts(T.vp[:], T.io2[:], -4 * U, None, (A.mult,), ["io2"], ["vp"])
+
+    def constants():
+        op("v", "set", (T.lsr[:, 704:712], 0), [], ["lsr"])
+        vts(T.sth2[:, 0:1], T.sth[:], 10, None, (A.arith_shift_right,), ["sth"], ["sth2a"])
+        vts(T.sth2[:, 1:2], T.sth[:], 1023, None, (A.bitwise_and,), ["sth"], ["sth2b"])
+        op("v", "copy", (T.lsr[:, 0:704], T["str"][:]), ["str"], ["lsr.r"])
+        op("v", "copy", (T.lsr[:, 704:706], T.sth2[:]), ["sth2a", "sth2b"], ["lsr"])
+        dma("s", [(T.lrd[:], T.lsr[:])], "dlr", ["lsr", "lsr.r"], ["lrd"])
+        vts(T.ic[:], T.ic[:], 7, None, (A.bitwise_and,), ["ic"], ["ic"])
+        vts(T.pmx[:], T["id"][:], 0.0, None, (A.is_equal,), ["id"], ["pmx"])
+        op("v", "set", (T.ones[:], 1.0), [], ["ones"])
+        vts(T.ob[:], T.ic[:], 0.0, None, (A.is_equal,), ["ic"], ["ob"])
+        op("v", "set", (T.xl[:, 2816:2824], float(BIG)), [], ["xls"])
+        op("v", "set", (T.xf[:, 2816:2824], float(-BIG)), [], ["xfs"])
+        op("v", "set", (T.cur[:], 0.0), [], curk)
+        for b in range(KB):
+            vts(T.es[:, b, :], T.ig[:], float(b), None, (A.is_equal,), ["ig"], ["es" if b == KB - 1 else "es.%d" % b])
+
+    def later_lists():
+        vts(T.stc[:], T.stb[:], 4, None, (A.arith_shift_right,), ["stb"], ["stc"])
+        for half in range(2):
+            for m in range(4):
+                for c in range(NC):
+                    k = half * 1024 + (m // 2) * 512 + c * 128 + (m % 2) * 64
+                    op("v", "copy", (T.ls1[:, k:k + 64], T.stb[:, m, :, c, :]), ["stb"], ["ls1.%d" % k])
+            if half == 0:
+                vts(T.stb[:], T.stb[:], 15, None, (A.bitwise_and,), ["stb"], ["stb"])
+                vts(T.stb[:], T.stb[:], 176.0, None, (A.mult,), ["stb"], ["stb"])
+                op("v", "tt", (T.stb[:], T.stb[:], T.stc[:], A.add), ["stb", "stc"], ["stb"])
+        ls1k = ["ls1.%d" % k for k in range(0, 2048, 64)]
+        dma("y", [(T.l1d[:], T.ls1[:])], "dlc", ls1k, ["l1d"])
+        send(to_all(T.l1d, T.l1r, "l1a"), ["l1d"])
+        arrives("l1a", 14, "l1r")
+        land("y", T.ll1, T.l1r, T.ls1, "dl1", ["l1r"] + ls1k, "ll1")
+
+    def thresholds():
+        op("v", "copy", (T.thf[:, 0:2], T.llr[:, 704:706]), ["llr"], ["thf"])
+        vts(T.thf[:, 2:3], T.thf[:, 0:1], 1024.0, None, (A.mult,), ["thf"], ["thf2"])
+        op("v", "tt", (T.thf[:, 3:4], T.thf[:, 2:3], T.thf[:, 1:2], A.add), ["thf", "thf2"], ["thf3"])
+        op("t", "mm", [(T.pb[:, 2048:2049], T.pmx[:], T.thf[:, 3:4], True, True)], ["pmx", "thf3"], ["pb4"])
+        vts(T.nth[:], T.pb[:, 2048:2049], -1.0, None, (A.mult,), ["pb4"], ["nth"])
+
+    for q in near + far:
+        arrives("pxa%d" % q, 4, "pxr%d" % q)
+        dma("y", [(T.xi[16 * q:16 * q + 16, :], T.pxr[2 * q:2 * q + 2])], "dxi", ["pxr%d" % q], ["xi.%d" % q])
+    xik = ["xi.own", "xi.%d" % far[-1]]
+    wk = ["w%d" % b for b in range(8)]
+
+    def unpack(t, ns):
+        for n in ns:
+            a, b = (512 * n, min(512 * n + 512, R)) if t == 0 else (352 * n, 352 * n + 352)
+            ps, key = ((T.pw, "pw"), (T.pv, "pv"))[n % 2]
+            if t == 0:
+                mm = [(ps[:, k:b - a:16], T.uk[:, k, :], T.w16[:, a // 16:b // 16], True, True) for k in range(16)]
+            else:
+                mm = [(ps[:, 176 * k:176 * k + 176], T.uk[:, 2 * n + k, :], T.w16[:], True, True) for k in range(2)]
+            op("t", "mm", mm, ["uk"] + w16k, [key])
+            op("s", "act", (T.w[:, a:b], ps[:, 0:b - a], F.Copy), [key], [wk[n]])
+
+    def lists(t, where=0):
+        return (T.ls0, 0, ls0k) if t == 0 else (T.ll1, 512 * (t - 1) + 1024 * where, ["ll1"])
+
+    def prepare(t):
+        buf, base, key = lists(t)
+        op("v", "copy", (T.cf[:], buf[:, base:base + 512]), key, ["cf"])
+
+    turn = {"s": 0, "v": 0}
+
+    def look(t, c, m, q):
+        buf, base, key = lists(t, 1)
+        k = base + c * 128 + m * 64
+        out, ok = T.pb[:, 512 * c + 64 * m:512 * c + 64 * m + 64], "pb%d" % c
+        turn[q] ^= 1
+        if q == "s":
+            wg, wgk = (T.wg0, T.wg1)[turn[q]], "wg%d" % turn[q]
+            op("s", "acts", [(wg[:, 128 * b:128 * b + 128], T.w[:, 0:R].indirect(buf[:, k + 8 * b:k + 8 * b + 8]), F.Copy,
+                              float(2048 - 64 - 512 * b - 128 * c)) for b in range(8)], key + wk, [wgk])
+            op("t", "mm", [(out, T.ni[:], T.vp[:], True, False)]
+               + [(out, T.dkb[:, i, :], wg[:, i:1024:16], False, i == 15) for i in range(16)], ["dkb", "ni", "vp", wgk], [ok])
+        else:
+            mk, mkk = (T.mk0, T.mk1)[turn[q]], "mk%d" % turn[q]
+            op("v", "tt", (mk[:], T.w[:, 0:R].indirect(buf[:, k:k + 64]), T.vt[:, c * 1024:c * 1024 + 1024], A.is_ge),
+               key + ["vt%d" % c] + wk, [mkk])
+            op("t", "mm", [(out, T.six[0:1, :], T.six[0:1, 0:64], True, False)]
+               + [(out, T.dkb[:, i, :], mk[:, i:1024:16], False, i == 15) for i in range(16)], ["dkb", "six", mkk], [ok])
+
+    def mask(c):
+        d, e, k = slice(c * 128, c * 128 + 128), slice(c % 2 * 128, c % 2 * 128 + 128), "sm%d" % (c % 2)
+        op("v", "tt", (T.sm[:, e], T.pb[:, 512 * c:512 * c + 128], T.cf[:, d], A.max), ["pb%d" % c, "cf"], [k])
+        vts(T.oo[:, d], T.sm[:, e], float(R), None, (A.min,), [k], ["oo%d" % c])
+
+    xfk = ["xf%d" % p for p in npc] + ["xfs"]
+    xlk = ["xl%d" % p for p in npc] + ["xls"]
+
+    def masked(t, c):
+        return (T.om, "om") if t == 0 else (T.oo, "oo%d" % c)
+
+    def see0(c, t=1):
+        e, d = c % 2, slice(c * 128, c * 128 + 64)
+        o, ok = masked(t, c)
+        za = T.ag[:, 1024 * e:1024 * e + 1024]
+        op("s", "act", (za, T.xf[:, 0:2824].indirect(o[:, d]), F.Copy), [ok] + xfk, ["za%d" % e, "ag0", "agh", "ag1"])
+        op("s", "act", ((T.zb0, T.zb1)[e][:], za, F.Abs), ["za%d" % e], ["zb%d" % e])
+
+    def see1(c, t=1):
+        e, d = c % 2, slice(c * 128 + 64, c * 128 + 128)
+        o, ok = masked(t, c)
+        za, zb, hb, lb = T.ag[:, 1024 * e:1024 * e + 1024], (T.zb0, T.zb1)[e], (T.hb0, T.hb1)[e], (T.lb0, T.lb1)[e]
+        op("v", "tt", (hb[:], T.xf[:, 0:2824].indirect(o[:, d]), za, A.max), [ok, "za%d" % e] + xfk, ["hb%d" % e])
+        dma("y", [(T.zz[:, a, c, 0, :], hb[16 * a:16 * a + 16, :]) for a in range(8)], "rg%d" % c, ["hb%d" % e], ["zh%d" % c])
+        op("v", "tt", (lb[:], T.xl[:, 0:2824].indirect(o[:, d]), zb[:], A.min), [ok, "zb%d" % e] + xlk, ["lb%d" % e])
+        dma("y", [(T.zz[:, a, c, 1, :], lb[16 * a:16 * a + 16, :]) for a in range(8)], "rk%d" % c, ["lb%d" % e], ["zl%d" % c])
+
+    def reduce(c0, c1):
+        for a in range(1, 8):
+            for j, o, z in ((0, A.max, "zh"), (1, A.min, "zl")):
+                b = 2048 + 512 * j
+                acc, key = T.pb[:, b + 128 * c0:b + 128 * c1], "pb%d" % (4 + j)
+                src = [z + str(c) for c in range(c0, c1)]
+                if a == 1:
+                    op("s", "act", (acc, T.zz[:, 0, c0:c1, j, :], F.Copy), src, [key])
+                op("v", "tt", (acc, acc, T.zz[:, a, c0:c1, j, :], o), src + [key], [key])
+
+    def carve():
+        op("s", "act", (T.hs[:], T.pb[:, 2048:2560], F.Identity, T.nth[:]), ["pb4", "nth"], ["hs"])
+        op("v", "tt", (T.far[:], T.hs[:], T.pb[:, 2560:3072], A.is_gt), ["hs", "pb5"], ["far"])
+        op("s", "act", (T.fe[:], T.pb[:, 2560:3072], F.Copy, -0.375, -0.25), ["pb5"], ["fe"])
+        op("t", "mm", [(T.pw[:], T.ob[:], T.far[:], True, True)], ["ob", "far"], ["pw"])
+        vts(T.inc[:], T.pw[:], 9.0, None, (A.is_ge,), ["pw"], ["inc"])
+        op("v", "scan", (T.cum[:], T.inc[:], T.inc[:], 0.0, A.add, A.max), ["inc"], ["cum"])
+        op("v", "tt", (T.pv[:], T.inc[:], T.fe[:], A.mult), ["inc", "fe"], ["pv"])
+        vts(T.pc[:], T.cum[:], 128.0, None, (A.is_le,), ["cum"], ["pc"])
+        op("v", "tt", (T.et[:], T.pc[:], T.pv[:], A.mult), ["pc", "pv"], ["et"])
+        pairs = [(T.ea[16 * a:16 * a + 16, 512 * b:512 * b + 512], T.et[b:128:8, :]) for b in range(KB, 8) for a in range(8)]
+        n = len(pairs) * 5 // 8
+        dma("y", pairs[:n], "ea0", ["et"], ["eaa"])
+        dma("s", pairs[n:], "ea1", ["et"], ["eab"])
+        for b in range(KB):
+            d = slice(512 * b, 512 * b + 512)
+            op("t", "mm", [(T.pb[:, d], T.es[:, b, :], T.et[:], True, True)], ["es", "et"], ["pb%d" % b])
+            op("s", "act", (T.ea[:, d], T.pb[:, d], F.Copy), ["pb%d" % b], ["eac"])
+
+    dl = T.dl
+
+    def places(t):
+        if t == 0:
+            op("v", "copy", (T.eq[:], T.llr[:, 176:704]), ["llr"], ["eq0", "eq1", "eq2"])
+            op("v", "tt", (T.pr[:, 0:176], T.eq[:, 0:176], T.wf[:], A.subtract), ["eq0"] + wfk, ["pr.0"])
+            op("v", "tt", (T.pr[:, 176:528], T.eq[:, 176:528], T.eq[:, 0:352], A.subtract), ["eq0"], ["pr"])
+            vts(dl[:], T.pr[:], 1.0 / U, None, (A.mult,), ["pr.0", "pr"], ["dl"])
+            return
+        for k in range(3):
+            vts(T.eq[:, k * 176:k * 176 + 176], T.cur[:], U * k, None, (A.is_equal,), curk, ["eq%d" % k])
+        op("v", "tt", (T.pr[:], T.eq[:], dl[:], A.mult), ["eq0", "eq1", "eq2", "dl"], ["pr"])
+        op("v", "tt", (T.q1[:, 176:352], T.pr[:, 0:176], T.pr[:, 176:352], A.add), ["pr"], ["q1t"])
+        op("v", "tt", (T.q1[:, 0:176], T.q1[:, 176:352], T.pr[:, 352:528], A.add), ["pr", "q1t"], ["q1"])
+        op("v", "tt", (T.pr[:, 0:352], T.eq[:, 0:352], dl[:, 176:528], A.mult), ["eq0", "eq1", "dl"], ["pr"])
+        op("v", "tt", (T.q2[:], T.pr[:, 0:176], T.pr[:, 176:352], A.add), ["pr"], ["q2"])
+
+    pgs = ((T.pw, "pw"), (T.pv, "pv"))
+
+    def span(p):
+        return 16 * PIECES[p][0], 16 * PIECES[p][1]
+
+    def banks(p):
+        a, b = span(p)
+        return [(k, 512 * k, min(512 * k + 512, R)) for k in range(a // 512, (b + 511) // 512)]
+
+    def agk(p):
+        return ["ag0", "agh"] if p == 0 else ["ag1"]
+
+    def gather(p, q):
+        a, b = span(p)
+        h = (a + b) // 2
+        parts = (("v", a, h, ["agh"]), ("s", h, b, ["ag0"])) if q == "vs" else ((q, a, b, agk(p)),)
+        for q, x, y, keys in parts:
+            args = (T.ag[:, x:y], T.ea[:, 0:V].indirect(T.wu[:, x // 16:y // 16]))
+            op(q, "act" if q == "s" else "copy", args + ((F.Copy,) if q == "s" else ()), ["eaa", "eab", "eac", "wu%d" % p], keys)
+
+    def sign(p):
+        a, b = span(p)
+        op("s", "act", (T.sg[:, a:b], T.ag[:, a:b], F.Sign), agk(p), ["sg%d" % p])
+
+    def pack(p):
+        a, b = PIECES[p]
+        ps, key = pgs[p]
+        op("t", "mm", [(ps[:, a:b], T.dkb[:, k, :], T.sg[:, 16 * a + k:16 * b:16], k == 0, k == 15) for k in range(16)],
+           ["dkb", "sg%d" % p], [key])
+
+    def spread(p, ks=slice(0, 6)):
+        for k, x, y in banks(p)[ks]:
+            op("t", "mm", [(T.pb[:, x:y], T.ones[0:1, 0:128], T.ones[0:1, 0:y - x], True, False),
+                           (T.pb[:, x:y], T.ni[:], T.sg[:, x:y], False, True)], ["ni", "ones", "sg%d" % p], ["pb%d" % k])
+
+    def small(p, t, step, last):
+        a, b = PIECES[p]
+        ps, key = pgs[p]
+        if t == 0:
+            q, qk = dl[:, 176 * step + a:176 * step + b], "dl"
+        else:
+            q, qk = (T.q1[:, a:b], "q1") if step == 0 else (T.q2[:, a:b], "q2")
+        wfp, tqp = ["wf%d" % p], ["tq%d" % p]
+        if not last:
+            op("v", "tt", (T.tq[:, a:b], ps[:, a:b], q, A.mult), [key, qk], tqp)
+            op("v", "tt", (T.wf[:, a:b], T.wf[:, a:b], T.tq[:, a:b], A.add), wfp + tqp, wfp)
+            if step == 1:
+                vts(T.w16[:, a:b], T.wf[:, a:b], -2048.0, None, (A.add,), wfp, ["w16.%d" % p])
+            op("v", "copy", (T.wu[:, a:b], T.wf[:, a:b]), wfp, ["wu%d" % p])
+        op("v", "tt", (T.cur[:, a:b], ps[:, a:b], T.cur[:, a:b], A.add), [key, "cur%d" % p], ["cur%d" % p])
+
+    def move(p, part):
+        a, b = span(p)
+        pk = ["pb%d" % k for k, _, _ in banks(p)]
+        if part == 0:
+            for k, x, y in banks(p):
+                op("v", "tt", (T.pb[:, x:y], T.xf[:, x:y], T.pb[:, x:y], A.mult), ["pb%d" % k, "xf%d" % p], ["pb%d" % k])
+        elif part == 1:
+            op("v", "tt", (T.xi[:, a:b], T.pb[:, a:b], T.ag[:, a:b], A.add), pk + agk(p), ["xi%d" % p])
+        else:
+            vts(T.xf[:, a:b], T.xi[:, a:b], 0.0, float(TOP), (A.max, A.min), ["xi%d" % p], ["xf%d" % p])
+
+    def second(p):
+        a, b = span(p)
+        op("s", "act", (T.xl[:, a:b], T.xf[:, a:b], F.Copy), ["xf%d" % p], ["xl%d" % p])
+
+    unpack(0, range(6))
+    for t in range(3):
+        if t == 0:
+            prepare(0)
+            for c in range(NC):
+                if c:
+                    vts(T.vt[:, 1024 * c:1024 * c + 1024], T.vt[:, 0:1024], 128.0 * c, None, (A.add,), ["vt0"], ["vt%d" % c])
+                look(0, c, 0, "s")
+                look(0, c, 1, "v")
+                if c:
+                    mask(c - 1)
+            mask(NC - 1)
+            ook = ["oo%d" % c for c in range(NC)]
+            dma("s", [(T.l0d[:], T.oo[:])], "dlb", ook, ["l0d"])
+            send(to_all(T.l0d, T.l0r, "l0a"), ["l0d"])
+            constants()
+            send(to_all(T.lrd, T.lrr, "lra"), ["lrd"])
+            for p in npc:
+                a, b = span(p)
+                op("v", "copy", (T.xf[:, a:b], T.xi[:, a:b]), xik, ["xf%d" % p])
+                second(p)
+            arrives("l0a", 14, "l0r")
+            land("y", T.om, T.l0r, T.oo, "dl0", ["l0r"] + ook, "om")
+            arrives("lra", 14, "lrr")
+            land("y", T.llr, T.lrr, T.lsr, "dlq", ["lrr", "lsr", "lsr.r"], "llr")
+            for c in range(NC):
+                see0(c, 0)
+                see1(c, 0)
+            thresholds()
+            op("v", "copy", (T.wf[:], T.llr[:, 0:176]), ["llr"], wfk)
+            op("v", "copy", (T.wu[:], T.llr[:, 0:176]), ["llr"], ["wu%d" % p for p in npc])
+            reduce(0, 3)
+            reduce(3, 4)
+        else:
+            for s in SCHED.split():
+                c = int(s[1])
+                if s[0] == "L":
+                    look(t, c, int(s[2]), s[3])
+                elif s[0] == "R":
+                    reduce(c, int(s[2]))
+                else:
+                    {"M": mask, "Z": see0, "V": see1, "X": second}[s[0]](c)
+        carve()
+        places(t)
+        if t == 0:
+            later_lists()
+        elif t == 1:
+            prepare(2)
+        for step in range(2):
+            end = step == 1
+            last = end and t == 2
+            gather(0, "s" if step else "vs")
+            sign(0)
+            gather(1, "s" if step else "v")
+            sign(1)
+            pack(0)
+            spread(0)
+            pack(1)
+            small(0, t, step, last)
+            move(0, 0)
+            small(1, t, step, last)
+            if end and t < 2:
+                for k in range(3):
+                    spread(1, slice(k, k + 1))
+                    unpack(t + 1, ((0, 1, 2, 3), (4, 5, 6, 7), ())[k])
+            else:
+                spread(1)
+            if last:
+                vts(T.cfin[:], T.cur[:], 1.0 / U, 3.0, (A.mult, A.min), curk, ["cfin"])
+            for p, part in ((0, 1), (0, 2), (1, 0), (1, 1), (1, 2)):
+                move(p, part)
+            if end and t == 0:
+                prepare(1)
+    w0 = span(0)[1]
+    dma("s", [(T.cd[:], T.cfin[:])], "dcd", ["cfin"], ["cd"])
+    dma("y", [(T.od0[:], T.xf[:, 0:w0])], "dod0", ["xf0"], ["od0"])
+    dma("y", [(T.od1[:], T.xf[:, w0:R])], "dod1", ["xf1"], ["od1"])
+    halves(T.od0, T.or0, "oa", T.ro0, "ro0i", ["od0"], ["od0"])
+    halves(T.od1, T.or1, "ob", T.ro1, "ro1i", ["od1"], ["od1"])
+    send(to_all(T.cd, T.cr, "ca"), ["cd"])
+    dma("s", [(T.yx[lo:hi, 0:w0], T.xf[lo:hi, 0:w0]), (T.yx[lo:hi, w0:R], T.xf[lo:hi, w0:R]),
+              (T.yc[lo:hi, :], T.cfin[lo:hi, :])], "dz", ["xf0", "xf1", "cfin"], [])
+    for s, src, dst, q0, d in (("oa", T.or0, slice(0, w0), "y", "dy"), ("ob", T.or1, slice(w0, R), "s", "dz")):
+        for q in near + far:
+            arrives(s + str(q), 4, s + ".%d" % q)
+            dma(q0, [(T.yx[16 * q:16 * q + 16, dst], src[2 * q:2 * q + 2])], d, [s + ".%d" % q], [])
+    arrives("ca", 14, "cr")
+    dma("s", [(T.yc[16 * a:16 * b, :], T.cr[a:b]) for a, b in others], "dz", ["cr"], [])
+    waits("g", [(s, cnt[s]) for s in cnt])

@@ -4,41 +4,47 @@ from concourse.mybir import dt, AluOpType, AxisListType, ActivationFunctionType
 A = AluOpType
 F = ActivationFunctionType
 R, V, TOP, BIG = 2816, 4096, 2 ** 20 - 1, 2 ** 22
+RH = R // 2
 U = 4096.0
+MAGIC = 1.5 * 2 ** 23
 NC = 4
 PIECES = ((0, 96), (96, 176))
-KB = 3
-SCHED = "L00s L01v X0 L10s X1 L11v M0 Z0 M1 L20s V0 L21v Z1 L30s L31v M2 V1 Z2 M3 V2 Z3 V3 R03 R34"
-f32, i32, u16, f16, b16 = "float32", "int32", "uint16", "float16", "bfloat16"
+LAST = ((0, 48), (48, 96), (96, 144), (144, 176))
+SPREAD = ("dram", "dram", "dma", "pe")
+LOOKS = "ss ss vs ss"
+CYCLE, GATHER, CALL, LAG, DMA, ISSUE, HOP, NEAR, FAR = 0.83e-3, 1.5, 0.04, 0.17, 1.8, 1.2, 3.0, 1 / 400e3, 1 / 40e3
+f32, i32, u16, b16 = "float32", "int32", "uint16", "bfloat16"
 SCRATCH = {n: ("sbuf", [128] + list(sh), d) for n, sh, d in (
-    ("sta", (2, 8, 4, 8), i32), ("stb", (4, 8, 4, 8), i32), ("stc", (4, 8, 4, 8), i32), ("str", (704,), i32),
-    ("sth", (1,), i32), ("sth2", (2,), i32), ("ls0", (512,), u16), ("ls1", (2048,), u16),
+    ("sta", (4, 2, 64), i32), ("stb", (8, 2, 64), i32), ("stc", (512,), i32), ("std", (512,), f32), ("str", (704,), i32),
+    ("ste", (528,), f32), ("sth", (1,), i32), ("sth2", (2,), i32), ("ls0", (512,), u16), ("ls1", (2048,), u16),
     ("lsr", (712,), u16), ("ll1", (2048,), u16), ("llr", (712,), u16), ("om", (512,), u16),
-    ("ia", (128,), i32), ("ib", (128,), i32), ("ic", (128,), i32), ("id", (128,), i32), ("ie", (128,), i32),
-    ("ig", (128,), i32), ("es", (3, 128), f32), ("io2", (64,), i32), ("io3", (64,), i32),
-    ("uk", (16, 128), f16), ("dkb", (16, 128), b16), ("ob", (128,), b16), ("ni", (128,), b16),
-    ("pmx", (128,), f32), ("ones", (512,), b16), ("six", (128,), b16), ("vt", (4096,), f32),
-    ("vp", (64,), b16), ("nth", (1,), f32), ("thf", (4,), f32),
-    ("xi", (2816,), i32), ("xf", (2824,), f32), ("xl", (2824,), f32), ("w", (2816,), f32), ("wf", (176,), f32),
-    ("wu", (176,), u16), ("w16", (176,), f16), ("cur", (176,), f32), ("dl", (528,), f32), ("q1", (352,), f32),
-    ("q2", (176,), f32), ("eq", (528,), f32), ("pr", (528,), f32), ("cfin", (176,), f32),
-    ("cf", (512,), f32), ("wg0", (1024,), b16), ("wg1", (1024,), b16), ("mk0", (1024,), b16), ("mk1", (1024,), b16),
-    ("sm", (256,), f32), ("oo", (512,), u16), ("zb0", (1024,), f32), ("zb1", (1024,), f32), ("hb0", (1024,), f32),
-    ("hb1", (1024,), f32), ("lb0", (1024,), f32), ("lb1", (1024,), f32), ("zz", (8, 4, 2, 128), f32), ("hs", (512,), f32),
-    ("fe", (512,), f32), ("far", (512,), b16), ("inc", (512,), b16), ("cum", (512,), f32), ("pc", (512,), b16),
-    ("et", (512,), f32), ("ea", (4096,), f32), ("ag", (2816,), f32), ("sg", (2816,), b16), ("tq", (176,), f32))}
+    ("ia", (144,), i32), ("ib", (128,), i32), ("ic", (128,), i32), ("id", (128,), i32), ("ig", (128,), i32),
+    ("ie", (128,), i32), ("ip", (8,), i32), ("iq", (8,), i32), ("ir", (4,), i32), ("iv", (64,), i32), ("col", (8,), f32),
+    ("es", (8, 128), f32), ("dk", (144,), b16), ("sp", (128,), b16), ("sq", (128,), b16), ("ob", (128,), b16),
+    ("ni", (128,), b16), ("ki", (128,), b16), ("tri", (128,), f32), ("trj", (128,), f32), ("sel", (128,), f32),
+    ("ones", (128,), b16), ("vp", (64,), b16), ("nth", (4,), f32), ("thf", (4,), f32), ("thc", (4,), f32), ("m4", (4,), f32),
+    ("xi", (R,), i32), ("xf", (R + 8,), f32), ("xr", (R,), f32), ("y", (R,), f32), ("w", (R,), f32), ("wf", (176,), f32),
+    ("wu0", (176,), u16), ("wu1", (176,), u16), ("cur", (176,), f32), ("dl", (528,), f32), ("q1", (352,), f32),
+    ("q2", (176,), f32), ("eq", (528,), f32), ("pr", (528,), f32), ("cfin", (176,), f32), ("tq", (176,), f32),
+    ("cf", (512,), f32), ("wg0", (1024,), b16), ("wg1", (1024,), b16), ("wg2", (1024,), b16), ("sm", (256,), f32),
+    ("oh", (512,), u16), ("ol", (512,), u16), ("za0", (1024,), f32), ("za1", (1024,), f32), ("zb0", (1024,), f32),
+    ("zb1", (1024,), f32), ("hl0", (2048,), f32), ("hl1", (2048,), f32), ("zz", (8, NC, 256), f32),
+    ("lc", (512,), i32), ("fe", (512,), f32), ("far", (512,), b16), ("sgn", (512,), b16), ("acc", (NC,), f32),
+    ("cum", (512,), b16), ("et", (512,), f32), ("ea", (V,), f32), ("sg0", (R,), b16), ("sg1", (R,), b16))}
 SCRATCH.update({n: ("dram", list(sh), d) for n, sh, d in (
     ("l0d", (8, 128, 64), u16), ("l0r", (8, 128, 64), u16), ("l1d", (8, 128, 256), u16), ("l1r", (8, 128, 256), u16),
     ("lrd", (8, 128, 89), u16), ("lrr", (8, 128, 89), u16), ("pxd", (16, 128, 176), i32), ("pxr", (16, 128, 176), i32),
-    ("rb", (4, 128, 176), i32), ("ro0", (4, 128, 96), f32), ("od0", (16, 128, 96), f32), ("or0", (16, 128, 96), f32),
-    ("ro1", (4, 128, 80), f32), ("od1", (16, 128, 80), f32), ("or1", (16, 128, 80), f32),
-    ("cd", (8, 128, 22), f32), ("cr", (8, 128, 22), f32))})
-SCRATCH.update({n: ("psum", [128, k], f32) for n, k in (("pb", 3072), ("pw", 512), ("pv", 512))})
-PSUM = ["pb%d" % k for k in range(6)] + ["pw", "pv"]
-SEMAPHORES = (["v", "s", "t", "gc", "lsem", "l0a", "l1a", "lra", "ca", "rbi", "ro0i", "ro1i", "rlo"]
-              + [n + str(q) for n in ("pxa", "oa", "ob") for q in range(8)] + [n + str(c) for n in ("rg", "rk") for c in range(NC)]
-              + ["ea0", "ea1", "dst", "dst1", "dl0", "dl1", "dpx", "dpy", "dlb", "dlc", "dxi", "dod0", "dod1", "dcd", "dy", "dz",
-                 "dlr", "dlq"])
+    ("rb", (4, 128, 176), i32), ("cd", (8, 128, 22), f32), ("cr", (8, 128, 22), f32), ("etd", (NC, 128, 128), f32))})
+for _p, (_a, _b) in enumerate(LAST):
+    SCRATCH.update({n + str(_p): ("dram", [k, 128, _b - _a], f32) for n, k in (("ro", 4), ("od", 16), ("or", 16))})
+BANKS = ("pa0", "pa1", "pa2", "pd", "pb0", "pb1", "pc0", "pc1")
+SCRATCH.update({n: ("psum", [128, 512], f32) for n in BANKS})
+SEMAPHORES = (["v", "s", "t", "gc", "lsem", "l0a", "l1a", "lra", "ca", "rbi", "rlo", "pxn"]
+              + ["px%d%d" % (h, q) for h in range(2) for q in range(8)]
+              + [n + str(p) for n in ("ri", "on", "of", "dod") for p in range(len(LAST))]
+              + [n + str(c) for n in ("rg", "rk", "ed", "ea") for c in range(NC)]
+              + ["dst", "dsr", "dst1", "dl0", "dl1", "dpx", "dpy", "dlb", "dlc", "dxn", "dxa", "dxb", "dcd", "dy", "dz", "dlr",
+                 "dlq", "dw"])
 
 
 def layout(T, topo):
@@ -63,11 +69,51 @@ def transfer(topo, dst, mask, src, out, sem):
 def relay_program(g, core, T, topo, r, far):
     masks = two(topo.engines(core, T.cores[far[0]]), len(far))
     n = 2 * len(far)
-    for s, src, dst, to in (("rbi", T.rb, T.pxr, "pxa"), ("ro0i", T.ro0, T.or0, "oa"), ("ro1i", T.ro1, T.or1, "ob")):
+    jobs = [("rbi", T.rb, T.pxr[8 + r], "px1%d" % r)]
+    jobs += [("ri%d" % p, T["ro%d" % p], T["or%d" % p][2 * r + 1], "of%d" % p) for p in range(len(LAST))]
+    for s, src, dst, to in jobs:
         g.wait_ge(T.sem[s], n)
-        g.remote_dma_fused([transfer(topo, T.cores[q], masks[k], src[k], dst[2 * r + 1], T.sem[to + str(r)])
-                            for k, q in enumerate(far)], local_sem=T.sem.rlo)
-    g.wait_ge(T.sem.rlo, 3 * n)
+        g.remote_dma_fused([transfer(topo, T.cores[q], masks[k], src[k], dst, T.sem[to]) for k, q in enumerate(far)],
+                           local_sem=T.sem.rlo)
+    g.wait_ge(T.sem.rlo, len(jobs) * n)
+
+
+def order_of_issue(prog):
+    n = len(prog)
+    succ, left, wr, rd = [[] for _ in prog], [0] * n, {}, {}
+    for i, (q, reads, writes, busy, total) in enumerate(prog):
+        before = {wr[k] for k in reads + writes if k in wr} | {j for k in writes for j in rd.get(k, ())}
+        for j in before:
+            succ[j].append(i)
+        left[i] = len(before)
+        for k in reads:
+            rd.setdefault(k, []).append(i)
+        for k in writes:
+            wr[k], rd[k] = i, []
+    way = [0.0] * n
+    for i in reversed(range(n)):
+        way[i] = prog[i][4] + LAG + max([way[j] for j in succ[i]], default=0.0)
+    banks = [{k.split(".")[0] for k in p[1] + p[2]} & set(BANKS) for p in prog]
+    ready, free, held, pool, out = [0.0] * n, {}, {}, [i for i in range(n) if not left[i]], []
+    while pool:
+        start = {i: max([ready[i], free.get(prog[i][0], 0.0)]
+                        + [t for b in banks[i] for q, t in held.get(b, {}).items() if q != prog[i][0]]) for i in pool}
+        first = min(pool, key=lambda i: start[i] + prog[i][3])
+        q = prog[first][0]
+        i = max((j for j in pool if prog[j][0] == q and start[j] <= start[first] + prog[first][3]), key=lambda j: way[j])
+        pool.remove(i)
+        out.append(i)
+        if q:
+            free[q] = start[i] + prog[i][3]
+        end = start[i] + prog[i][4] + LAG
+        for b in banks[i]:
+            held.setdefault(b, {})[q] = end
+        for j in succ[i]:
+            ready[j] = max(ready[j], end)
+            left[j] -= 1
+            if not left[j]:
+                pool.append(j)
+    return out
 
 
 def rank_program(g, core, T, topo):
@@ -82,7 +128,7 @@ def rank_program(g, core, T, topo):
     sem = T.sem
     queue = {"v": g.vector, "s": g.scalar, "t": g.tensor, "y": g.sync, "g": g}
     own = {"v": "v", "s": "s", "t": "t", "g": "gc"}
-    cnt, seen, wr, rd = {}, {}, {}, {}
+    cnt, seen, wr, rd, bank, prog, issue = {}, {}, {}, {}, {}, [], []
 
     def waits(q, deps):
         need = {}
@@ -97,11 +143,9 @@ def rank_program(g, core, T, topo):
         d = []
         for k in reads + writes:
             d += wr.get(k, [])
+            d += [(s, n) for s, n in bank.get(k.split(".")[0], {}).items() if s != own.get(q)]
         for k in writes:
             d += rd.get(k, {}).items()
-        for k in reads:
-            if k in PSUM:
-                d += [(s, n) for s, n in rd.get(k, {}).items() if s != own.get(q)]
         return d
 
     def done(tag, reads, writes):
@@ -110,42 +154,57 @@ def rank_program(g, core, T, topo):
         for k in writes:
             wr[k] = [tag]
             rd[k] = {}
+        for k in reads + writes:
+            if k.split(".")[0] in BANKS:
+                bank.setdefault(k.split(".")[0], {})[tag[0]] = tag[1]
 
     calls = {"mm": g.tensor.matmul, "acts": g.scalar.activation, "act": g.scalar.activation, "iota": g.iota,
              "copy": g.vector.tensor_copy, "tt": g.vector.tensor_tensor, "ts": g.vector.tensor_scalar, "set": g.vector.memset,
-             "scan": g.vector.tensor_tensor_scan}
+             "tss": g.vector.tensor_scalar, "scan": g.vector.tensor_tensor_scan}
 
-    def op(q, name, args, reads, writes, **kw):
-        waits(q, deps_of(q, reads, writes))
-        s = own[q]
-        for a in args if name in ("mm", "acts") else [args]:
-            ins = calls[name](*a, **kw)
-        cnt[s] = cnt.get(s, 0) + 1
-        ins.then_inc(sem[s], 1)
-        done((s, cnt[s]), reads, writes)
+    def note(q, reads, writes, busy, total, f):
+        prog.append((q, list(reads), list(writes), busy, total))
+        issue.append(f)
 
-    def vts(out, in0, s1, s2, ops, reads, writes):
-        op("v", "ts", (out, in0, s1, s2) + ops, reads, writes)
+    def op(q, name, args, reads, writes, n=64, **kw):
+        def f():
+            waits(q, deps_of(q, reads, writes))
+            s = own[q]
+            for a in args if name in ("mm", "acts", "tss") else [args]:
+                ins = calls[name](*a, **kw)
+            cnt[s] = cnt.get(s, 0) + 1
+            ins.then_inc(sem[s], 1)
+            done((s, cnt[s]), reads, writes)
+        note(q, reads, writes, CALL + n * CYCLE, CALL + n * CYCLE, f)
 
-    def dma(q, pairs, s, reads, writes):
-        waits(q, deps_of(q, reads, writes))
-        for o, i in pairs:
-            queue[q].dma_start(o, i).then_inc(sem[s], 16)
-        cnt[s] = cnt.get(s, 0) + 16 * len(pairs)
-        done((s, cnt[s]), reads, writes)
+    def vts(out, in0, s1, s2, ops, reads, writes, n=64):
+        op("v", "ts", (out, in0, s1, s2) + ops, reads, writes, n)
 
-    def arrives(s, n, key):
-        cnt[s] = cnt.get(s, 0) + n
-        wr[key] = [(s, cnt[s])]
+    def dma(q, pairs, s, reads, writes, nbytes):
+        def f():
+            waits(q, deps_of(q, reads, writes))
+            for o, i in pairs:
+                queue[q].dma_start(o, i).then_inc(sem[s], 16)
+            cnt[s] = cnt.get(s, 0) + 16 * len(pairs)
+            done((s, cnt[s]), reads, writes)
+        note(q, reads, writes, 0.06 * len(pairs), DMA + 0.06 * len(pairs) + nbytes * NEAR, f)
+
+    def arrives(s, n, key, like, time):
+        def f():
+            cnt[s] = cnt.get(s, 0) + n
+            wr[key] = [(s, cnt[s])]
+        note(None, [like], [key], 0.0, time, f)
 
     nf, nn = len(far), len(near)
     off = topo.engines(core, T.cores[far[0]])
     rest = [e for e in topo.engines(core, T.cores[near[0]]) if e not in off]
 
-    def send(moves, reads):
-        waits("g", deps_of("g", reads, []))
-        g.remote_dma_fused([transfer(topo, d, m, a, b, sem[s]) for d, m, a, b, s in moves], local_sem=sem.lsem)
-        cnt["lsem"] = cnt.get("lsem", 0) + 2 * len(moves)
+    def send(moves, reads, name):
+        def f():
+            waits("g", deps_of("g", reads, []))
+            g.remote_dma_fused([transfer(topo, d, m, a, b, sem[s]) for d, m, a, b, s in moves], local_sem=sem.lsem)
+            cnt["lsem"] = cnt.get("lsem", 0) + 2 * len(moves)
+        note("g", reads, [name, "sent"], ISSUE, ISSUE, f)
 
     def to_far(src, dst, s):
         return [(T.cores[q], m, src(q), dst, s) for q, m in zip(far, two(off, nf))]
@@ -159,361 +218,338 @@ def rank_program(g, core, T, topo):
     def to_all(src, dst, s):
         return to_far(lambda q: src[q], dst[rank], s) + to_near(lambda q: src[q], dst[rank], s, rest)
 
-    def halves(src, dst, s, via, vsem, kf, kn):
-        s = s + str(rank)
-        send(to_relay(lambda q: src[2 * q + 1], via, vsem) + to_far(lambda q: src[2 * q], dst[2 * rank], s), kf)
-        send(to_near(lambda q: src[2 * q], dst[2 * rank], s, rest) + to_near(lambda q: src[2 * q + 1], dst[2 * rank + 1], s, off), kn)
+    def halves(s0, s1, d0, d1, sf, sn, via, vsem, kf, kn):
+        send(to_relay(s1, via, vsem) + to_far(s0, d0, sf), kf, vsem + ".f")
+        send(to_near(s0, d0, sn, rest) + to_near(s1, d1, sn, off), kn, vsem + ".n")
 
     lo, hi = 16 * rank, 16 * rank + 16
-    npc = range(len(PIECES))
     others = [(a, b) for a, b in ((0, rank), (rank + 1, 8)) if b > a]
-
-    def land(q, dst, src, mine, s, reads, key):
-        dma(q, [(dst[16 * a:16 * b, :], src[a:b]) for a, b in others] + [(dst[lo:hi, :], mine[lo:hi, :])], s, reads, [key])
-
-    dma("y", [(T.sta[:], T.cand[:, 0:512]), (T["str"][:], T.ray[:]), (T.sth[:], T.th[:])], "dst", [], ["sta", "str", "sth"])
     fa, fb = far[0], far[-1] + 1
     na, nb = min(near + [rank]), max(near + [rank]) + 1
-    dma("y", [(T.pxd[2 * fa:2 * fb], T.px[16 * fa:16 * fb, :])], "dpx", [], ["pxdf"])
-    dma("y", [(T.pxd[2 * na:2 * nb], T.px[16 * na:16 * nb, :])], "dpy", [], ["pxdn"])
-    dma("y", [(T.stb[:], T.cand[:, 512:1536]), (T.xi[lo:hi, :], T.px[lo:hi, :])], "dst1", [], ["stb", "xi.own"])
-    op("g", "iota", (T.ia[:], [[-16, 8], [0, 16]], 0, 1), [], ["ia"])
-    op("g", "iota", (T.ib[:], [[-16000, 8], [-999, 16]], 0, 1000), [], ["ib"])
-    op("g", "iota", (T.vt[:, 0:1024], [[512, 8], [1, 128]], -2048, 0), [], ["vt0"], allow_small_or_imprecise_dtypes=True)
-    op("g", "iota", (T.ie[:], [[-1, 128]], 0, 1), [], ["ie"])
-    op("g", "iota", (T.io2[:], [[0, 8], [16, 8]], -64, 0), [], ["io2"])
-    op("g", "iota", (T.io3[:], [[0, 64]], 0, 1), [], ["io3"])
-    op("g", "iota", (T["id"][:], [[-1, 16], [-16, 8]], 0, 1), [], ["id"])
-    op("g", "iota", (T.ic[:], [[0, 16], [1, 8]], 1024, -1), [], ["ic"])
-    op("g", "iota", (T.ig[:], [[0, 8], [-8, 16]], 0, 1), [], ["ig"])
-    halves(T.pxd, T.pxr, "pxa", T.rb, "rbi", ["pxdf"], ["pxdn"])
-    for k in range(16):
-        vts(T.uk[:, k, :], T.ia[:], float(k), None, (A.is_equal,), ["ia"], ["uk" if k == 15 else "uk.%d" % k])
-    w16k, wfk, curk = ["w16.%d" % p for p in npc], ["wf%d" % p for p in npc], ["cur%d" % p for p in npc]
-    vts(T.w16[:], T["str"][:, 0:176], -2048.0, None, (A.add,), ["str"], w16k)
-    for m in range(2):
-        for c in range(NC):
-            k = c * 128 + m * 64
-            op("v", "copy", (T.ls0[:, k:k + 64], T.sta[:, m, :, c, :]), ["sta"], ["ls0.%d" % k])
-    ls0k = ["ls0.%d" % k for k in range(0, 512, 64)]
-    for k in range(16):
-        vts(T.dkb[:, k, :], T.ib[:], float(k), -U, (A.is_equal, A.mult), ["ib"], ["dkb" if k == 15 else "dkb.%d" % k])
-    vts(T.io3[:], T.io3[:], 15, None, (A.bitwise_and,), ["io3"], ["io3"])
-    vts(T.ni[:], T.ie[:], 0.0, -0.25, (A.is_equal, A.mult), ["ie"], ["ni"])
-    op("v", "tt", (T.io2[:], T.io2[:], T.io3[:], A.add), ["io2", "io3"], ["io2"])
-    op("v", "set", (T.six[:], 64.0), [], ["six"])
-    vts(T.vp[:], T.io2[:], -4 * U, None, (A.mult,), ["io2"], ["vp"])
+    nears = [(a, b) for a, b in ((na, rank), (rank + 1, nb)) if b > a]
 
-    def constants():
-        op("v", "set", (T.lsr[:, 704:712], 0), [], ["lsr"])
-        vts(T.sth2[:, 0:1], T.sth[:], 10, None, (A.arith_shift_right,), ["sth"], ["sth2a"])
-        vts(T.sth2[:, 1:2], T.sth[:], 1023, None, (A.bitwise_and,), ["sth"], ["sth2b"])
-        op("v", "copy", (T.lsr[:, 0:704], T["str"][:]), ["str"], ["lsr.r"])
-        op("v", "copy", (T.lsr[:, 704:706], T.sth2[:]), ["sth2a", "sth2b"], ["lsr"])
-        dma("s", [(T.lrd[:], T.lsr[:])], "dlr", ["lsr", "lsr.r"], ["lrd"])
-        vts(T.ic[:], T.ic[:], 7, None, (A.bitwise_and,), ["ic"], ["ic"])
-        vts(T.pmx[:], T["id"][:], 0.0, None, (A.is_equal,), ["id"], ["pmx"])
-        op("v", "set", (T.ones[:], 1.0), [], ["ones"])
-        vts(T.ob[:], T.ic[:], 0.0, None, (A.is_equal,), ["ic"], ["ob"])
-        op("v", "set", (T.xl[:, 2816:2824], float(BIG)), [], ["xls"])
-        op("v", "set", (T.xf[:, 2816:2824], float(-BIG)), [], ["xfs"])
-        op("v", "set", (T.cur[:], 0.0), [], curk)
-        for b in range(KB):
-            vts(T.es[:, b, :], T.ig[:], float(b), None, (A.is_equal,), ["ig"], ["es" if b == KB - 1 else "es.%d" % b])
+    def land(q, dst, src, mine, s, reads, key, nbytes):
+        dma(q, [(dst[16 * a:16 * b, :], src[a:b]) for a, b in others] + [(dst[lo:hi, :], mine[lo:hi, :])], s, reads, [key], nbytes)
 
-    def later_lists():
-        vts(T.stc[:], T.stb[:], 4, None, (A.arith_shift_right,), ["stb"], ["stc"])
-        for half in range(2):
-            for m in range(4):
-                for c in range(NC):
-                    k = half * 1024 + (m // 2) * 512 + c * 128 + (m % 2) * 64
-                    op("v", "copy", (T.ls1[:, k:k + 64], T.stb[:, m, :, c, :]), ["stb"], ["ls1.%d" % k])
-            if half == 0:
-                vts(T.stb[:], T.stb[:], 15, None, (A.bitwise_and,), ["stb"], ["stb"])
-                vts(T.stb[:], T.stb[:], 176.0, None, (A.mult,), ["stb"], ["stb"])
-                op("v", "tt", (T.stb[:], T.stb[:], T.stc[:], A.add), ["stb", "stc"], ["stb"])
-        ls1k = ["ls1.%d" % k for k in range(0, 2048, 64)]
-        dma("y", [(T.l1d[:], T.ls1[:])], "dlc", ls1k, ["l1d"])
-        send(to_all(T.l1d, T.l1r, "l1a"), ["l1d"])
-        arrives("l1a", 14, "l1r")
-        land("y", T.ll1, T.l1r, T.ls1, "dl1", ["l1r"] + ls1k, "ll1")
+    def keys(name, a, b):
+        return ["%s%d" % (name, k) for k in range(a // 16, b // 16)]
+
+    wfk, curk, xfk = keys("wf", 0, 176), keys("cur", 0, 176), keys("xf", 0, 176) + ["xfs"]
+    pdk = ["pd.%d" % j for j in range(4)]
+    lsrk, ls1k = ["lsr", "lsr.r", "lsr.d"], ["ls1.n", "ls1.0", "ls1.1"]
+    col, dl = T.col, T.dl
+
+    dma("y", [(T["str"][:], T.ray[:])], "dsr", [], ["str", "y0"], 0)
+    dma("s", [(T.sta[:, :, m, :], T.cand[:, 256 * m:256 * m + 256]) for m in range(2)], "dst", [], ["sta"], 0)
+    dma("y", [(T.pxd[8 * h + fa:8 * h + fb], T.px[16 * fa:16 * fb, RH * h:RH * h + RH]) for h in (1, 0)], "dpx", [], ["pxdf"], 720e3)
+    dma("y", [(T.pxd[8 * h + a:8 * h + b], T.px[16 * a:16 * b, RH * h:RH * h + RH]) for h in (0, 1) for a, b in nears],
+        "dpy", [], ["pxdn"], 540e3)
+    dma("y", [(T.stb[:, 4 * (k // 2):4 * (k // 2) + 4, k % 2, :], T.cand[:, 512 + 256 * k:768 + 256 * k]) for k in range(4)]
+        + [(T.xi[lo:hi, :], T.px[lo:hi, :]), (T.sth[:], T.th[:])], "dst1", [], ["stb", "xi.own", "sth"], 2e6)
+    op("v", "set", (T.w[:], 0.0), [], ["w"], R)
+    op("g", "iota", (T.ip[:], [[0, 8]], 0, 1), [], ["ip"], 200)
+    op("g", "iota", (T.ia[:], [[-1, 144]], 16, 1), [], ["ia"], 400)
+    op("g", "iota", (T.iv[:], [[0, 2], [16, 32]], -255, 0), [], ["iv"], 300)
+    op("g", "iota", (T.ib[:], [[-16, 8], [0, 16]], 0, 1), [], ["ib"], 400)
+    op("g", "iota", (T["id"][:], [[-1, 16], [-16, 2], [0, 4]], 1024, 1), [], ["id"], 400)
+    op("g", "iota", (T.ic[:], [[-4, 32], [0, 4]], 0, 1), [], ["ic"], 400)
+    op("g", "iota", (T.ig[:], [[0, 8], [-8, 16]], 0, 1), [], ["ig"], 400)
+    op("g", "iota", (T.ir[:], [[-32, 4]], 0, 1), [], ["ir"], 200)
+    halves(lambda q: T.pxd[q], lambda q: T.pxd[8 + q], T.pxr[rank], T.pxr[8 + rank], "px0%d" % rank, "pxn", T.rb, "rbi",
+           ["pxdf"], ["pxdn"])
+
+    def row_of_w():
+        dma("y", [(T.w[0:128:16, :], T.wf[:])], "dw", wfk, ["w"], 0)
+
+    def numbers_to_places(src, n, out, key, okey):
+        vts(T.stc[:, 0:n], src, 15, None, (A.bitwise_and,), [key], ["stc"], n)
+        vts(T.pd[:, 0:n], T.stc[:, 0:n], 2815.0, None, (A.mult,), ["stc"], pdk, n)
+        op("v", "tt", (T.std[:, 0:n], T.pd[:, 0:n], src, A.add), pdk + [key], ["std"], n)
+        vts(out, T.std[:, 0:n], 1.0 / 16, None, (A.mult,), ["std"], [okey], n)
+
+    vts(T.iq[:, 0:1], T.ip[:, 0:1], 15, None, (A.bitwise_and,), ["ip"], ["iq0"])
+    op("v", "copy", (T.wf[:], T["str"][:, 0:176]), ["str"], wfk, 176)
+    row_of_w()
+    vts(col[:, 0:1], T.iq[:, 0:1], 0.0, -U, (A.is_equal, A.mult), ["iq0"], ["col0"])
+    op("v", "copy", (col[:, 1:2], T.iq[:, 0:1]), ["iq0"], ["col1"])
+    for h in range(2):
+        numbers_to_places(T.sta[:, 2 * h:2 * h + 2], 256, T.ls0[:, 256 * h:256 * h + 256], "sta", "ls0.%d" % h)
+    vts(T.dk[:], T.ia[:], 0.0, col[:, 0:1], (A.is_equal, A.mult), ["ia", "col0"], ["dk"], 144)
+    vts(T.ni[:], T.ia[:, 16:144], 0.0, -0.25, (A.is_equal, A.mult), ["ia"], ["ni"], 128)
+    vts(T.vp[:], T.iv[:], col[:, 1:2], -4 * U, (A.add, A.mult), ["iv", "col1"], ["vp"])
+    op("v", "set", (T.lsr[:, 704:712], 0), [], ["lsr"])
+    vts(T.sth2[:, 0:1], T.sth[:], 10, None, (A.arith_shift_right,), ["sth"], ["sth2a"])
+    vts(T.sth2[:, 1:2], T.sth[:], 1023, None, (A.bitwise_and,), ["sth"], ["sth2b"])
+    op("v", "tt", (T.ste[:], T["str"][:, 176:704], T["str"][:, 0:528], A.subtract), ["str"], ["ste"], 1056)
+    op("v", "copy", (T.lsr[:, 0:176], T["str"][:, 0:176]), ["str"], ["lsr.r"], 176)
+    op("v", "copy", (T.lsr[:, 704:706], T.sth2[:]), ["sth2a", "sth2b"], ["lsr"])
+    vts(T.lsr[:, 176:704], T.ste[:], U, None, (A.add,), ["ste"], ["lsr.d"], 528)
+    dma("s", [(T.lrd[:], T.lsr[:])], "dlr", lsrk, ["lrd"], 180e3)
+    op("v", "set", (T.xf[:, R:R + 8], float(BIG)), [], ["xfs"])
+    op("v", "set", (T.xf[:, R:R + 1], float(-BIG)), [], ["xfs"])
+    op("v", "set", (T.cur[:], 0.0), [], curk, 176)
+    op("v", "set", (T.ones[:], 1.0), [], ["ones"])
+    op("v", "set", (col[:, 5:6], -8.5), [], ["col5"])
+    vts(T.sp[:], T.ib[:], 0.0, -0.25, (A.is_equal, A.mult), ["ib"], ["sp"], 128)
+    vts(T.sq[:], T.ib[:], 1.0, None, (A.is_equal,), ["ib"], ["sq"], 128)
+    op("v", "tt", (T.sp[:], T.sp[:], T.sq[:], A.add), ["sp", "sq"], ["sp"], 256)
+    vts(col[:, 2:3], T.iq[:, 0:1], 1.0, None, (A.is_equal,), ["iq0"], ["col2"])
+    vts(col[:, 3:4], T.iq[:, 0:1], 1.0, None, (A.not_equal,), ["iq0"], ["col3"])
+    vts(T.ki[:], T.ia[:, 16:144], 0.0, 128.0, (A.is_equal, A.mult), ["ia"], ["ki"], 128)
+    vts(T.iq[:, 1:2], T.ip[:, 0:1], 3, None, (A.bitwise_and,), ["ip"], ["iq1"])
+    vts(col[:, 4:5], T.iq[:, 1:2], 32.0, 64.0, (A.mult, A.add), ["iq1"], ["col4"])
+    vts(T.ie[:], T.ia[:, 16:144], 7, None, (A.bitwise_and,), ["ia"], ["ie"], 128)
+    vts(T.ob[:], T.ie[:], 0.0, None, (A.is_equal,), ["ie"], ["ob"], 128)
+    vts(T["id"][:], T["id"][:], 31, None, (A.bitwise_and,), ["id"], ["id"], 128)
+    vts(T.sel[:], T["id"][:], 0.0, None, (A.is_equal,), ["id"], ["sel"], 128)
+    vts(T.ir[:], T.ir[:], 5, None, (A.arith_shift_right,), ["ir"], ["ir"])
+    vts(T.m4[:], T.ir[:], 0.0, None, (A.is_equal,), ["ir"], ["m4"])
+    vts(T.tri[:], T.ic[:], 0.0, None, (A.is_ge,), ["ic"], ["tri"], 128)
+    vts(T.trj[:], T.ia[:, 16:144], 0.0, None, (A.is_lt,), ["ia"], ["trj"], 128)
+    op("v", "tt", (T.tri[:], T.tri[:], T.trj[:], A.mult), ["tri", "trj"], ["tri"], 256)
+    for b in range(8):
+        vts(T.es[:, b, :], T.ig[:], float(b), None, (A.is_equal,), ["ig"], ["es%d" % b], 128)
+    op("v", "copy", (T.ls1[:, 0:1024], T.stb[:]), ["stb"], ["ls1.n"], 1024)
+    for h in range(2):
+        numbers_to_places(T.stb[:, 4 * h:4 * h + 4], 512, T.ls1[:, 1024 + 512 * h:1536 + 512 * h], "stb", "ls1.%d" % h)
+    dma("y", [(T.l1d[:], T.ls1[:])], "dlc", ls1k, ["l1d"], 520e3)
 
     def thresholds():
         op("v", "copy", (T.thf[:, 0:2], T.llr[:, 704:706]), ["llr"], ["thf"])
-        vts(T.thf[:, 2:3], T.thf[:, 0:1], 1024.0, None, (A.mult,), ["thf"], ["thf2"])
-        op("v", "tt", (T.thf[:, 3:4], T.thf[:, 2:3], T.thf[:, 1:2], A.add), ["thf", "thf2"], ["thf3"])
-        op("t", "mm", [(T.pb[:, 2048:2049], T.pmx[:], T.thf[:, 3:4], True, True)], ["pmx", "thf3"], ["pb4"])
-        vts(T.nth[:], T.pb[:, 2048:2049], -1.0, None, (A.mult,), ["pb4"], ["nth"])
-
-    for q in near + far:
-        arrives("pxa%d" % q, 4, "pxr%d" % q)
-        dma("y", [(T.xi[16 * q:16 * q + 16, :], T.pxr[2 * q:2 * q + 2])], "dxi", ["pxr%d" % q], ["xi.%d" % q])
-    xik = ["xi.own", "xi.%d" % far[-1]]
-    wk = ["w%d" % b for b in range(8)]
-
-    def unpack(t, ns):
-        for n in ns:
-            a, b = (512 * n, min(512 * n + 512, R)) if t == 0 else (352 * n, 352 * n + 352)
-            ps, key = ((T.pw, "pw"), (T.pv, "pv"))[n % 2]
-            if t == 0:
-                mm = [(ps[:, k:b - a:16], T.uk[:, k, :], T.w16[:, a // 16:b // 16], True, True) for k in range(16)]
-            else:
-                mm = [(ps[:, 176 * k:176 * k + 176], T.uk[:, 2 * n + k, :], T.w16[:], True, True) for k in range(2)]
-            op("t", "mm", mm, ["uk"] + w16k, [key])
-            op("s", "act", (T.w[:, a:b], ps[:, 0:b - a], F.Copy), [key], [wk[n]])
-
-    def lists(t, where=0):
-        return (T.ls0, 0, ls0k) if t == 0 else (T.ll1, 512 * (t - 1) + 1024 * where, ["ll1"])
+        op("v", "copy", (T.wf[:], T.llr[:, 0:176]), ["llr"], wfk, 176)
+        vts(T.thf[:, 2:3], T.thf[:, 0:1], 1024.0, T.thf[:, 1:2], (A.mult, A.add), ["thf"], ["thf2"])
+        vts(dl[:], T.llr[:, 176:704], -U, 1.0 / U, (A.add, A.mult), ["llr"], ["dl"], 528)
+        vts(T.thc[:], T.m4[:], T.thf[:, 2:3], None, (A.mult,), ["m4", "thf2"], ["thc"])
+        op("t", "mm", [(T.pd[:, 0:4], T.sel[:], T.thc[:], True, True)], ["sel", "thc"], pdk, 128)
+        vts(T.nth[:], T.pd[:, 0:4], -1.0, -0.5, (A.mult, A.add), pdk, ["nth"])
 
     def prepare(t):
-        buf, base, key = lists(t)
-        op("v", "copy", (T.cf[:], buf[:, base:base + 512]), key, ["cf"])
+        src, key = (T.sta[:], "sta") if t == 0 else (T.ll1[:, 512 * t - 512:512 * t], "ll1")
+        op("v", "copy", (T.cf[:], src), [key], ["cf"], 512)
 
-    turn = {"s": 0, "v": 0}
+    turn = {"s": 0}
 
     def look(t, c, m, q):
-        buf, base, key = lists(t, 1)
-        k = base + c * 128 + m * 64
-        out, ok = T.pb[:, 512 * c + 64 * m:512 * c + 64 * m + 64], "pb%d" % c
-        turn[q] ^= 1
+        buf, base, key = (T.ls0, 0, "ls0.%d" % (c // 2)) if t == 0 else (T.ll1, 512 + 512 * t, "ll1")
+        k = base + 128 * c + 64 * m
+        out, ok = T["pc%d" % (c % 2)][:, 64 * m:64 * m + 64], "pc%d.%d" % (c % 2, m)
+        turn["s"] ^= q == "s"
+        e = turn["s"] if q == "s" else 2
+        wg, wgk = T["wg%d" % e], "wg%d" % e
+        parts = [(wg[:, 512 * b:512 * b + 512], T.w[:, 0:R].indirect(buf[:, k + 32 * b:k + 32 * b + 32]),
+                  float(-255 - 512 * b - 1024 * c)) for b in range(2)]
         if q == "s":
-            wg, wgk = (T.wg0, T.wg1)[turn[q]], "wg%d" % turn[q]
-            op("s", "acts", [(wg[:, 128 * b:128 * b + 128], T.w[:, 0:R].indirect(buf[:, k + 8 * b:k + 8 * b + 8]), F.Copy,
-                              float(2048 - 64 - 512 * b - 128 * c)) for b in range(8)], key + wk, [wgk])
-            op("t", "mm", [(out, T.ni[:], T.vp[:], True, False)]
-               + [(out, T.dkb[:, i, :], wg[:, i:1024:16], False, i == 15) for i in range(16)], ["dkb", "ni", "vp", wgk], [ok])
+            op("s", "acts", [(o, i, F.Copy, z) for o, i, z in parts], [key, "w"], [wgk], 1024 * GATHER + 100)
         else:
-            mk, mkk = (T.mk0, T.mk1)[turn[q]], "mk%d" % turn[q]
-            op("v", "tt", (mk[:], T.w[:, 0:R].indirect(buf[:, k:k + 64]), T.vt[:, c * 1024:c * 1024 + 1024], A.is_ge),
-               key + ["vt%d" % c] + wk, [mkk])
-            op("t", "mm", [(out, T.six[0:1, :], T.six[0:1, 0:64], True, False)]
-               + [(out, T.dkb[:, i, :], mk[:, i:1024:16], False, i == 15) for i in range(16)], ["dkb", "six", mkk], [ok])
+            op("v", "tss", [(o, i, z, None, A.add) for o, i, z in parts], [key, "w"], [wgk], 1024 * GATHER + 100)
+        op("t", "mm", [(out, T.ni[:], T.vp[:], True, False)]
+           + [(out, T.dk[:, 16 - i:144 - i], wg[:, i:1024:16], False, i == 15) for i in range(16)], ["dk", "ni", "vp", wgk], [ok], 700)
 
-    def mask(c):
-        d, e, k = slice(c * 128, c * 128 + 128), slice(c % 2 * 128, c % 2 * 128 + 128), "sm%d" % (c % 2)
-        op("v", "tt", (T.sm[:, e], T.pb[:, 512 * c:512 * c + 128], T.cf[:, d], A.max), ["pb%d" % c, "cf"], [k])
-        vts(T.oo[:, d], T.sm[:, e], float(R), None, (A.min,), [k], ["oo%d" % c])
+    def mask(c, both=True):
+        e = c % 2
+        d, s = slice(128 * c, 128 * c + 128), slice(128 * e, 128 * e + 128)
+        op("v", "tt", (T.sm[:, s], T["pc%d" % e][:, 0:128], T.cf[:, d], A.max), ["pc%d.0" % e, "pc%d.1" % e, "cf"], ["sm%d" % e], 128)
+        for o, ok, n in ((T.oh, "oh", R), (T.ol, "ol", R + 1))[0 if both else 1:]:
+            vts(o[:, d], T.sm[:, s], float(n), None, (A.min,), ["sm%d" % e], ["%s%d" % (ok, c)], 128)
 
-    xfk = ["xf%d" % p for p in npc] + ["xfs"]
-    xlk = ["xl%d" % p for p in npc] + ["xls"]
+    def side(c, j, n):
+        return slice(n * j, n * j + n) if c == NC - 1 else slice(j, 2 * n, 2)
 
-    def masked(t, c):
-        return (T.om, "om") if t == 0 else (T.oo, "oo%d" % c)
+    def see(t, c):
+        e = c % 2
+        hl = T["hl%d" % e]
+        for j, (o, ok), z, f in zip((0, 1), ((T.oh, "oh%d" % c), (T.om, "om") if t == 0 else (T.ol, "ol%d" % c)),
+                                    ("za%d" % e, "zb%d" % e), (A.max, A.min)):
+            d, k = side(c, j, 1024), 128 * c
+            op("s", "act", (T[z][:], T.xf[:, 0:R + 8].indirect(o[:, k:k + 64]), F.Copy), [ok] + xfk, [z], 1024 * GATHER)
+            op("v", "tt", (hl[:, d], T.xf[:, 0:R + 8].indirect(o[:, k + 64:k + 128]), T[z][:], f), [ok, z] + xfk,
+               ["hl%d%d" % (e, j)], 1024 * GATHER)
+            if c == NC - 1:
+                dma("y", [(T.zz[:, a, c, side(c, j, 128)], hl[16 * a:16 * a + 16, d]) for a in range(8)], ("rg", "rk")[j] + str(c),
+                    ["hl%d%d" % (e, j)], ["z%d%d" % (c, j)], 520e3)
+        if c < NC - 1:
+            dma("y", [(T.zz[:, a, c, :], hl[16 * a:16 * a + 16, :]) for a in range(8)], "rg%d" % c,
+                ["hl%d0" % e, "hl%d1" % e], ["z%d0" % c, "z%d1" % c], 1040e3)
 
-    def see0(c, t=1):
-        e, d = c % 2, slice(c * 128, c * 128 + 64)
-        o, ok = masked(t, c)
-        za = T.ag[:, 1024 * e:1024 * e + 1024]
-        op("s", "act", (za, T.xf[:, 0:2824].indirect(o[:, d]), F.Copy), [ok] + xfk, ["za%d" % e, "ag0", "agh", "ag1"])
-        op("s", "act", ((T.zb0, T.zb1)[e][:], za, F.Abs), ["za%d" % e], ["zb%d" % e])
-
-    def see1(c, t=1):
-        e, d = c % 2, slice(c * 128 + 64, c * 128 + 128)
-        o, ok = masked(t, c)
-        za, zb, hb, lb = T.ag[:, 1024 * e:1024 * e + 1024], (T.zb0, T.zb1)[e], (T.hb0, T.hb1)[e], (T.lb0, T.lb1)[e]
-        op("v", "tt", (hb[:], T.xf[:, 0:2824].indirect(o[:, d]), za, A.max), [ok, "za%d" % e] + xfk, ["hb%d" % e])
-        dma("y", [(T.zz[:, a, c, 0, :], hb[16 * a:16 * a + 16, :]) for a in range(8)], "rg%d" % c, ["hb%d" % e], ["zh%d" % c])
-        op("v", "tt", (lb[:], T.xl[:, 0:2824].indirect(o[:, d]), zb[:], A.min), [ok, "zb%d" % e] + xlk, ["lb%d" % e])
-        dma("y", [(T.zz[:, a, c, 1, :], lb[16 * a:16 * a + 16, :]) for a in range(8)], "rk%d" % c, ["lb%d" % e], ["zl%d" % c])
-
-    def reduce(c0, c1):
+    def carve(c):
+        ps, d, n = T[BANKS[c]], slice(128 * c, 128 * c + 128), BANKS[c] + "."
         for a in range(1, 8):
-            for j, o, z in ((0, A.max, "zh"), (1, A.min, "zl")):
-                b = 2048 + 512 * j
-                acc, key = T.pb[:, b + 128 * c0:b + 128 * c1], "pb%d" % (4 + j)
-                src = [z + str(c) for c in range(c0, c1)]
+            for j, o in ((0, A.max), (1, A.min)):
+                acc, key, z = ps[:, 128 * j:128 * j + 128], n + str(j), "z%d%d" % (c, j)
                 if a == 1:
-                    op("s", "act", (acc, T.zz[:, 0, c0:c1, j, :], F.Copy), src, [key])
-                op("v", "tt", (acc, acc, T.zz[:, a, c0:c1, j, :], o), src + [key], [key])
+                    op("v", "tt", (acc, T.zz[:, 0, c, side(c, j, 128)], T.zz[:, 1, c, side(c, j, 128)], o), [z], [key], 256)
+                else:
+                    op("v", "tt", (acc, acc, T.zz[:, a, c, side(c, j, 128)], o), [z, key], [key], 128)
+        k = str(c)
+        vts(T.lc[:, d], ps[:, 128:256], 0.0, float(TOP), (A.max, A.min), [n + "1"], ["lc" + k], 128)
+        vts(ps[:, 0:128], ps[:, 0:128], float(TOP), T.nth[:, c:c + 1], (A.min, A.add), [n + "0", "nth"], [n + "0"], 128)
+        op("v", "tt", (T.far[:, d], ps[:, 0:128], T.lc[:, d], A.is_gt), [n + "0", "lc" + k], ["far" + k], 128)
+        op("t", "mm", [(ps[:, 256:384], T.ob[:], T.far[:, d], True, True)], ["ob", "far" + k], [n + "2"], 100)
+        vts(T.fe[:, d], T.lc[:, d], -0.25, -0.375, (A.mult, A.add), ["lc" + k], ["fe" + k], 128)
+        op("s", "act", (T.sgn[:, d], ps[:, 256:384], F.Sign, col[:, 5:6]), [n + "2", "col5"], ["sgn" + k, "acc" + k], 250,
+           accum_out=T.acc[:, c:c + 1])
+        op("t", "mm", [(ps[:, 256:257], T.tri[:], T.acc[:, c:c + 1], True, True)], ["tri", "acc" + k], [n + "2"], 150)
+        op("v", "scan", (T.cum[:, d], T.sgn[:, d], T.ones[:], ps[:, 256:257], A.add, A.add), ["sgn" + k, "ones", n + "2"],
+           ["cum" + k], 128)
+        op("t", "mm", [(ps[:, 384:512], T.ni[:], T.cum[:, d], True, False), (ps[:, 384:512], T.ki[:], T.sgn[:, d], False, True)],
+           ["ni", "ki", "cum" + k, "sgn" + k], [n + "3"], 200)
+        et, ek, x = T.et[:, d], "et" + k, 1024 * c
+        vts(ps[:, 384:512], ps[:, 384:512], col[:, 4:5], None, (A.is_ge,), [n + "3", "col4"], [n + "3"], 128)
+        op("v", "tt", (et, ps[:, 384:512], T.fe[:, d], A.mult), [n + "3", "fe" + k], [ek], 128)
+        if SPREAD[c] == "pe":
+            for h in range(2):
+                pc, pk = T["pc%d" % h], ["pc%d.0" % h, "pc%d.1" % h]
+                op("t", "mm", [(pc[:, 128 * s:128 * s + 128], T.es[:, 4 * h + s, :], et, True, True) for s in range(4)],
+                   ["es%d" % b for b in range(8)] + [ek], pk, 1100)
+                op("s", "act", (T.ea[:, x + 512 * h:x + 512 * h + 512], pc[:], F.Copy), pk, ["ea%d%d" % (c, h)], 600)
+            return
+        if SPREAD[c] == "dram":
+            dma("y", [(T.etd[c], et)], "ed" + k, [ek], ["etd" + k], 65e3)
+            et, ek = T.etd[c], "etd" + k
+        dma("y", [(T.ea[16 * a:16 * a + 16, x:x + 1024], et) for a in range(8)], "ea" + k, [ek], ["ea%d0" % c, "ea%d1" % c], 520e3)
 
-    def carve():
-        op("s", "act", (T.hs[:], T.pb[:, 2048:2560], F.Identity, T.nth[:]), ["pb4", "nth"], ["hs"])
-        op("v", "tt", (T.far[:], T.hs[:], T.pb[:, 2560:3072], A.is_gt), ["hs", "pb5"], ["far"])
-        op("s", "act", (T.fe[:], T.pb[:, 2560:3072], F.Copy, -0.375, -0.25), ["pb5"], ["fe"])
-        op("t", "mm", [(T.pw[:], T.ob[:], T.far[:], True, True)], ["ob", "far"], ["pw"])
-        vts(T.inc[:], T.pw[:], 9.0, None, (A.is_ge,), ["pw"], ["inc"])
-        op("v", "scan", (T.cum[:], T.inc[:], T.inc[:], 0.0, A.add, A.max), ["inc"], ["cum"])
-        op("v", "tt", (T.pv[:], T.inc[:], T.fe[:], A.mult), ["inc", "fe"], ["pv"])
-        vts(T.pc[:], T.cum[:], 128.0, None, (A.is_le,), ["cum"], ["pc"])
-        op("v", "tt", (T.et[:], T.pc[:], T.pv[:], A.mult), ["pc", "pv"], ["et"])
-        pairs = [(T.ea[16 * a:16 * a + 16, 512 * b:512 * b + 512], T.et[b:128:8, :]) for b in range(KB, 8) for a in range(8)]
-        n = len(pairs) * 5 // 8
-        dma("y", pairs[:n], "ea0", ["et"], ["eaa"])
-        dma("s", pairs[n:], "ea1", ["et"], ["eab"])
-        for b in range(KB):
-            d = slice(512 * b, 512 * b + 512)
-            op("t", "mm", [(T.pb[:, d], T.es[:, b, :], T.et[:], True, True)], ["es", "et"], ["pb%d" % b])
-            op("s", "act", (T.ea[:, d], T.pb[:, d], F.Copy), ["pb%d" % b], ["eac"])
-
-    dl = T.dl
+    eak = ["ea%d%d" % (c, h) for c in range(NC) for h in range(2)]
 
     def places(t):
+        op("v", "copy", (T.wu0[:], T.wf[:]), wfk, ["wu0"], 176)
         if t == 0:
-            op("v", "copy", (T.eq[:], T.llr[:, 176:704]), ["llr"], ["eq0", "eq1", "eq2"])
-            op("v", "tt", (T.pr[:, 0:176], T.eq[:, 0:176], T.wf[:], A.subtract), ["eq0"] + wfk, ["pr.0"])
-            op("v", "tt", (T.pr[:, 176:528], T.eq[:, 176:528], T.eq[:, 0:352], A.subtract), ["eq0"], ["pr"])
-            vts(dl[:], T.pr[:], 1.0 / U, None, (A.mult,), ["pr.0", "pr"], ["dl"])
             return
-        for k in range(3):
-            vts(T.eq[:, k * 176:k * 176 + 176], T.cur[:], U * k, None, (A.is_equal,), curk, ["eq%d" % k])
-        op("v", "tt", (T.pr[:], T.eq[:], dl[:], A.mult), ["eq0", "eq1", "eq2", "dl"], ["pr"])
-        op("v", "tt", (T.q1[:, 176:352], T.pr[:, 0:176], T.pr[:, 176:352], A.add), ["pr"], ["q1t"])
-        op("v", "tt", (T.q1[:, 0:176], T.q1[:, 176:352], T.pr[:, 352:528], A.add), ["pr", "q1t"], ["q1"])
-        op("v", "tt", (T.pr[:, 0:352], T.eq[:, 0:352], dl[:, 176:528], A.mult), ["eq0", "eq1", "dl"], ["pr"])
-        op("v", "tt", (T.q2[:], T.pr[:, 0:176], T.pr[:, 176:352], A.add), ["pr"], ["q2"])
+        op("v", "tss", [(T.eq[:, k * 176:k * 176 + 176], T.cur[:], U * k, None, A.is_equal) for k in range(3)], curk, ["eq"], 600)
+        op("v", "tt", (T.pr[:], T.eq[:], dl[:], A.mult), ["eq", "dl"], ["pr"], 1056)
+        op("v", "tt", (T.q1[:, 176:352], T.pr[:, 0:176], T.pr[:, 176:352], A.add), ["pr"], ["q1t"], 352)
+        op("v", "tt", (T.q1[:, 0:176], T.q1[:, 176:352], T.pr[:, 352:528], A.add), ["pr", "q1t"], ["q1"], 352)
+        if t == 1:
+            op("v", "tt", (T.pr[:, 0:352], T.eq[:, 0:352], dl[:, 176:528], A.mult), ["eq", "dl"], ["pr"], 704)
+            op("v", "tt", (T.q2[:], T.pr[:, 0:176], T.pr[:, 176:352], A.add), ["pr"], ["q2"], 352)
 
-    pgs = ((T.pw, "pw"), (T.pv, "pv"))
+    def units(a, b, most=32):
+        n = (b - a + most - 1) // most
+        cut = [a + 16 * ((b - a) // 16 * k // n) for k in range(n + 1)]
+        return list(zip(cut, cut[1:]))
 
-    def span(p):
-        return 16 * PIECES[p][0], 16 * PIECES[p][1]
+    rot = [0]
 
-    def banks(p):
-        a, b = span(p)
-        return [(k, 512 * k, min(512 * k + 512, R)) for k in range(a // 512, (b + 511) // 512)]
-
-    def agk(p):
-        return ["ag0", "agh"] if p == 0 else ["ag1"]
-
-    def gather(p, q):
-        a, b = span(p)
-        h = (a + b) // 2
-        parts = (("v", a, h, ["agh"]), ("s", h, b, ["ag0"])) if q == "vs" else ((q, a, b, agk(p)),)
-        for q, x, y, keys in parts:
-            args = (T.ag[:, x:y], T.ea[:, 0:V].indirect(T.wu[:, x // 16:y // 16]))
-            op(q, "act" if q == "s" else "copy", args + ((F.Copy,) if q == "s" else ()), ["eaa", "eab", "eac", "wu%d" % p], keys)
-
-    def sign(p):
-        a, b = span(p)
-        op("s", "act", (T.sg[:, a:b], T.ag[:, a:b], F.Sign), agk(p), ["sg%d" % p])
-
-    def pack(p):
-        a, b = PIECES[p]
-        ps, key = pgs[p]
-        op("t", "mm", [(ps[:, a:b], T.dkb[:, k, :], T.sg[:, 16 * a + k:16 * b:16], k == 0, k == 15) for k in range(16)],
-           ["dkb", "sg%d" % p], [key])
-
-    def spread(p, ks=slice(0, 6)):
-        for k, x, y in banks(p)[ks]:
-            op("t", "mm", [(T.pb[:, x:y], T.ones[0:1, 0:128], T.ones[0:1, 0:y - x], True, False),
-                           (T.pb[:, x:y], T.ni[:], T.sg[:, x:y], False, True)], ["ni", "ones", "sg%d" % p], ["pb%d" % k])
-
-    def small(p, t, step, last):
-        a, b = PIECES[p]
-        ps, key = pgs[p]
+    def flags(t, step, p, a, b):
+        sg, sk = T["sg%d" % step], "sg%d" % step
+        o = T["wu%d" % step]
+        for x, y in units(a, b):
+            op("s", "act", (sg[:, 16 * x:16 * y], T.ea[:, 0:V].indirect(o[:, x:y]), F.Sign, col[:, 2:3], col[:, 3:4]),
+               eak + (keys("wu1", x, y) if step else ["wu0"]) + ["col2", "col3"], keys(sk, x, y), 16 * (y - x) * GATHER + 30)
+        ps, key = T["pb%d" % (p % 2)][:, 176 * step + a:176 * step + b], "pb%d.%d.%d" % (p % 2, step, 0)
+        op("t", "mm", [(ps, T.dk[:, 16 - k:144 - k], sg[:, 16 * a + k:16 * b:16], k == 0, k == 15) for k in range(16)],
+           ["dk"] + keys(sk, a, b), [key], 8 * max(64, b - a) + 100)
         if t == 0:
             q, qk = dl[:, 176 * step + a:176 * step + b], "dl"
         else:
             q, qk = (T.q1[:, a:b], "q1") if step == 0 else (T.q2[:, a:b], "q2")
-        wfp, tqp = ["wf%d" % p], ["tq%d" % p]
-        if not last:
-            op("v", "tt", (T.tq[:, a:b], ps[:, a:b], q, A.mult), [key, qk], tqp)
-            op("v", "tt", (T.wf[:, a:b], T.wf[:, a:b], T.tq[:, a:b], A.add), wfp + tqp, wfp)
-            if step == 1:
-                vts(T.w16[:, a:b], T.wf[:, a:b], -2048.0, None, (A.add,), wfp, ["w16.%d" % p])
-            op("v", "copy", (T.wu[:, a:b], T.wf[:, a:b]), wfp, ["wu%d" % p])
-        op("v", "tt", (T.cur[:, a:b], ps[:, a:b], T.cur[:, a:b], A.add), [key, "cur%d" % p], ["cur%d" % p])
+        wfp, tqp, cp = keys("wf", a, b), keys("tq", a, b), keys("cur", a, b)
+        if step == 0 or t < 2:
+            op("v", "tt", (T.tq[:, a:b], ps, q, A.mult), [key, qk], tqp, b - a)
+            op("v", "tt", (T.wf[:, a:b], T.wf[:, a:b], T.tq[:, a:b], A.add), wfp + tqp, wfp, 2 * (b - a))
+        if step == 0:
+            op("v", "copy", (T.wu1[:, a:b], T.wf[:, a:b]), wfp, keys("wu1", a, b), b - a)
+        op("v", "tt", (T.cur[:, a:b], ps, T.cur[:, a:b], A.add), [key] + cp, cp, b - a)
 
-    def move(p, part):
-        a, b = span(p)
-        pk = ["pb%d" % k for k, _, _ in banks(p)]
-        if part == 0:
-            for k, x, y in banks(p):
-                op("v", "tt", (T.pb[:, x:y], T.xf[:, x:y], T.pb[:, x:y], A.mult), ["pb%d" % k, "xf%d" % p], ["pb%d" % k])
-        elif part == 1:
-            op("v", "tt", (T.xi[:, a:b], T.pb[:, a:b], T.ag[:, a:b], A.add), pk + agk(p), ["xi%d" % p])
-        else:
-            vts(T.xf[:, a:b], T.xi[:, a:b], 0.0, float(TOP), (A.max, A.min), ["xi%d" % p], ["xf%d" % p])
+    def move(t, step, a, b):
+        src, name = (T.xi, "xi") if step else (T.xr, "xr") if t else (T.xf, "xf")
+        sg, sk = T["sg%d" % step], "sg%d" % step
+        for x, y in units(a, b):
+            k = BANKS[rot[0]]
+            rot[0] = (rot[0] + 1) % 4
+            pk, n = [k + ".%d" % j for j in range(4)], 16 * (y - x)
+            op("t", "mm", [(T[k][:, 0:n], T.sp[:], sg[:, 16 * x:16 * y], True, True)], ["sp"] + keys(sk, x, y), pk, n // 2 + 50)
+            op("v", "tt", (T.y[:, 16 * x:16 * y], src[:, 16 * x:16 * y], T[k][:, 0:n], A.mult), pk + keys(name, x, y),
+               keys("y", x, y), n)
+        dst, name = (T.xf, "xf") if step and t < 2 else (T.xi, "xi")
+        for x, y in units(a, b, 48):
+            op("v", "tt", (dst[:, 16 * x:16 * y], T.ea[:, 0:V].indirect(T["wu%d" % step][:, x:y]), T.y[:, 16 * x:16 * y], A.add),
+               eak + (keys("wu1", x, y) if step else ["wu0"]) + keys("y", x, y), keys(name, x, y), 16 * (y - x) * GATHER)
 
-    def second(p):
-        a, b = span(p)
-        op("s", "act", (T.xl[:, a:b], T.xf[:, a:b], F.Copy), ["xf%d" % p], ["xl%d" % p])
+    def rounded():
+        for a, b in units(0, 176):
+            d = slice(16 * a, 16 * b)
+            op("s", "act", (T.xr[:, d], T.xf[:, d], F.Copy, MAGIC), keys("xf", a, b), keys("xr", a, b), 16 * (b - a) + 100)
+            op("s", "act", (T.xr[:, d], T.xr[:, d], F.Copy, -MAGIC), keys("xr", a, b), keys("xr", a, b), 16 * (b - a) + 100)
 
-    unpack(0, range(6))
+    def home(p, a, b):
+        d, k = slice(16 * a, 16 * b), keys("xf", a, b)
+        od, to, key = T["od%d" % p], T["or%d" % p], ["od%d" % p]
+        vts(T.xf[:, d], T.xi[:, d], 0.0, float(TOP), (A.max, A.min), keys("xi", a, b), k, 16 * (b - a))
+        dma("y", [(od[:], T.xf[:, d])], "dod%d" % p, k, key, 8192 * (b - a))
+        dma("y", [(T.yx[lo:hi, d], T.xf[lo:hi, d])], "dy", k + key, [], 0)
+        halves(lambda q: od[2 * q], lambda q: od[2 * q + 1], to[2 * rank], to[2 * rank + 1], "of%d" % p, "on%d" % p,
+               T["ro%d" % p], "ri%d" % p, key, key)
+
+    def cursors():
+        vts(T.cfin[:], T.cur[:], 1.0 / U, 3.0, (A.mult, A.min), curk, ["cfin"], 176)
+        dma("y", [(T.cd[:], T.cfin[:])], "dcd", ["cfin"], ["cd"], 0)
+        dma("y", [(T.yc[lo:hi, :], T.cfin[lo:hi, :])], "dy", ["cfin", "cd"], [], 0)
+        send(to_all(T.cd, T.cr, "ca"), ["cd"], "ca")
+
+    prepare(0)
+    for c in range(NC):
+        look(0, c, 0, "s")
+        look(0, c, 1, "v")
+        mask(c, False)
+    olk = ["ol%d" % c for c in range(NC)]
+    dma("s", [(T.l0d[:], T.ol[:])], "dlb", olk, ["l0d"], 130e3)
+    send(to_all(T.l0d, T.l0r, "l0a"), ["l0d"], "l0a")
+    send(to_all(T.lrd, T.lrr, "lra"), ["lrd"], "lra")
+    arrives("pxn", 4 * nn, "pxrn", "rbi.n", 2 * HOP)
+    dma("y", [(T.xi[16 * a:16 * b, RH * h:RH * h + RH], T.pxr[8 * h + a:8 * h + b]) for h in (0, 1) for a, b in nears],
+        "dxn", ["pxrn", "l1d"], ["xi.n"], 540e3)
+    for h in range(2):
+        for k, q in enumerate(far):
+            arrives("px%d%d" % (h, q), 2, "pxr%d%d" % (h, q), "rbi.f", 3 + (1 + h) * HOP + (k + 1) * 90e3 * FAR)
+            dma("y", [(T.xi[16 * q:16 * q + 16, RH * h:RH * h + RH], T.pxr[8 * h + q])], ("dxa", "dxb")[h],
+                ["pxr%d%d" % (h, q), "l1d"], ["xi.f%d%d" % (h, q)], 90e3)
+    arrives("l0a", 14, "l0r", "l0a", 2 * HOP)
+    land("s", T.om, T.l0r, T.ol, "dl0", ["l0r", "lrd"] + olk, "om", 130e3)
+    arrives("lra", 14, "lrr", "lra", 2 * HOP)
+    land("s", T.llr, T.lrr, T.lsr, "dlq", ["lrr"] + lsrk, "llr", 180e3)
+    for h in range(2):
+        op("v", "copy", (T.xf[:, RH * h:RH * h + RH], T.xi[:, RH * h:RH * h + RH]),
+           ["xi.own", "xi.n"] + ["xi.f%d%d" % (h, q) for q in far], keys("xf", 80 * h, 80 * h + 96), RH)
+    vts(T.oh[:], T.om[:], float(R), None, (A.min,), ["om"], ["oh%d" % c for c in range(NC)], 256)
+    send(to_all(T.l1d, T.l1r, "l1a"), ["l1d", "xf10"], "l1a")
+    arrives("l1a", 14, "l1r", "l1a", 5 * HOP)
+    thresholds()
     for t in range(3):
+        for c in range(NC):
+            if t:
+                for m in range(2):
+                    look(t, c, m, LOOKS.split()[c][m])
+                mask(c)
+            see(t, c)
+        for c in range(NC):
+            carve(c)
         if t == 0:
-            prepare(0)
-            for c in range(NC):
-                if c:
-                    vts(T.vt[:, 1024 * c:1024 * c + 1024], T.vt[:, 0:1024], 128.0 * c, None, (A.add,), ["vt0"], ["vt%d" % c])
-                look(0, c, 0, "s")
-                look(0, c, 1, "v")
-                if c:
-                    mask(c - 1)
-            mask(NC - 1)
-            ook = ["oo%d" % c for c in range(NC)]
-            dma("s", [(T.l0d[:], T.oo[:])], "dlb", ook, ["l0d"])
-            send(to_all(T.l0d, T.l0r, "l0a"), ["l0d"])
-            constants()
-            send(to_all(T.lrd, T.lrr, "lra"), ["lrd"])
-            for p in npc:
-                a, b = span(p)
-                op("v", "copy", (T.xf[:, a:b], T.xi[:, a:b]), xik, ["xf%d" % p])
-                second(p)
-            arrives("l0a", 14, "l0r")
-            land("y", T.om, T.l0r, T.oo, "dl0", ["l0r"] + ook, "om")
-            arrives("lra", 14, "lrr")
-            land("y", T.llr, T.lrr, T.lsr, "dlq", ["lrr", "lsr", "lsr.r"], "llr")
-            for c in range(NC):
-                see0(c, 0)
-                see1(c, 0)
-            thresholds()
-            op("v", "copy", (T.wf[:], T.llr[:, 0:176]), ["llr"], wfk)
-            op("v", "copy", (T.wu[:], T.llr[:, 0:176]), ["llr"], ["wu%d" % p for p in npc])
-            reduce(0, 3)
-            reduce(3, 4)
+            land("y", T.ll1, T.l1r, T.ls1, "dl1", ["l1r", "z31"] + ls1k, "ll1", 520e3)
         else:
-            for s in SCHED.split():
-                c = int(s[1])
-                if s[0] == "L":
-                    look(t, c, int(s[2]), s[3])
-                elif s[0] == "R":
-                    reduce(c, int(s[2]))
-                else:
-                    {"M": mask, "Z": see0, "V": see1, "X": second}[s[0]](c)
-        carve()
+            rounded()
         places(t)
-        if t == 0:
-            later_lists()
-        elif t == 1:
-            prepare(2)
+        if t < 2:
+            prepare(t + 1)
+            for step in range(2):
+                for p, (a, b) in enumerate(PIECES):
+                    flags(t, step, p, a, b)
+                    move(t, step, a, b)
+            row_of_w()
+    for p, (a, b) in enumerate(LAST):
         for step in range(2):
-            end = step == 1
-            last = end and t == 2
-            gather(0, "s" if step else "vs")
-            sign(0)
-            gather(1, "s" if step else "v")
-            sign(1)
-            pack(0)
-            spread(0)
-            pack(1)
-            small(0, t, step, last)
-            move(0, 0)
-            small(1, t, step, last)
-            if end and t < 2:
-                for k in range(3):
-                    spread(1, slice(k, k + 1))
-                    unpack(t + 1, ((0, 1, 2, 3), (4, 5, 6, 7), ())[k])
-            else:
-                spread(1)
-            if last:
-                vts(T.cfin[:], T.cur[:], 1.0 / U, 3.0, (A.mult, A.min), curk, ["cfin"])
-            for p, part in ((0, 1), (0, 2), (1, 0), (1, 1), (1, 2)):
-                move(p, part)
-            if end and t == 0:
-                prepare(1)
-    w0 = span(0)[1]
-    dma("s", [(T.cd[:], T.cfin[:])], "dcd", ["cfin"], ["cd"])
-    dma("y", [(T.od0[:], T.xf[:, 0:w0])], "dod0", ["xf0"], ["od0"])
-    dma("y", [(T.od1[:], T.xf[:, w0:R])], "dod1", ["xf1"], ["od1"])
-    halves(T.od0, T.or0, "oa", T.ro0, "ro0i", ["od0"], ["od0"])
-    halves(T.od1, T.or1, "ob", T.ro1, "ro1i", ["od1"], ["od1"])
-    send(to_all(T.cd, T.cr, "ca"), ["cd"])
-    dma("s", [(T.yx[lo:hi, 0:w0], T.xf[lo:hi, 0:w0]), (T.yx[lo:hi, w0:R], T.xf[lo:hi, w0:R]),
-              (T.yc[lo:hi, :], T.cfin[lo:hi, :])], "dz", ["xf0", "xf1", "cfin"], [])
-    for s, src, dst, q0, d in (("oa", T.or0, slice(0, w0), "y", "dy"), ("ob", T.or1, slice(w0, R), "s", "dz")):
-        for q in near + far:
-            arrives(s + str(q), 4, s + ".%d" % q)
-            dma(q0, [(T.yx[16 * q:16 * q + 16, dst], src[2 * q:2 * q + 2])], d, [s + ".%d" % q], [])
-    arrives("ca", 14, "cr")
-    dma("s", [(T.yc[16 * a:16 * b, :], T.cr[a:b]) for a, b in others], "dz", ["cr"], [])
+            flags(2, step, p, a, b)
+            move(2, step, a, b)
+        if p == len(LAST) - 1:
+            cursors()
+        home(p, a, b)
+    for p, (a, b) in enumerate(LAST):
+        src, d = T["or%d" % p], slice(16 * a, 16 * b)
+        arrives("on%d" % p, 4 * nn, "orn%d" % p, "ri%d.n" % p, HOP)
+        dma("s", [(T.yx[16 * x:16 * y, d], src[2 * x:2 * y]) for x, y in nears], "dz", ["orn%d" % p, "sg110"], [], 0)
+        arrives("of%d" % p, 4 * nf, "orf%d" % p, "ri%d.f" % p, 2 * HOP + ISSUE + 2048 * (b - a) * FAR)
+        dma("s", [(T.yx[16 * fa:16 * fb, d], src[2 * fa:2 * fb])], "dz", ["orf%d" % p, "sg110"], [], 0)
+    arrives("ca", 14, "cr", "ca", HOP + 1)
+    dma("s", [(T.yc[16 * x:16 * y, :], T.cr[x:y]) for x, y in others], "dz", ["cr", "sg110"], [], 0)
+    for i in order_of_issue(prog):
+        issue[i]()
     waits("g", [(s, cnt[s]) for s in cnt])

@@ -4,47 +4,59 @@ from concourse.mybir import dt, AluOpType, AxisListType, ActivationFunctionType
 A = AluOpType
 F = ActivationFunctionType
 R, V, TOP, BIG = 2816, 4096, 2 ** 20 - 1, 2 ** 22
-RH = R // 2
+RH, RQ, CORES = R // 2, R // 4, 64
 U = 4096.0
 MAGIC = 1.5 * 2 ** 23
-NC = 4
-PIECES = ((0, 96), (96, 176))
+CHUNKS = ((0, 2), (2, 2), (4, 2), (6, 1), (7, 1))
+SPREAD = ("dram", "dram", "dma", "pe", "pe")
+PIECES = ((0, 64), (64, 128), (128, 176))
 LAST = ((0, 48), (48, 96), (96, 144), (144, 176))
-SPREAD = ("dram", "dram", "dma", "pe")
-LOOKS = "ss ss vs ss"
-CYCLE, GATHER, CALL, LAG, DMA, ISSUE, HOP, NEAR, FAR = 0.83e-3, 1.5, 0.04, 0.17, 1.8, 1.2, 3.0, 1 / 400e3, 1 / 40e3
+LOOK0 = "sv ss sv sv sv"
+LOOKS = "ss ss vs ss ss"
+FIRST = ("ssssv", "vsssv")
+ROUND = ("vvvvv", "vvvvv")
+GATHERS = ((1, 1), (1, 2))
+FLAGS = ((0, 0),)
+LASTG = (0, 1, 2)
+CYCLE, GATHER, CALL, LAG, DMA, ISSUE, HOP, NEAR, FAR = 0.83e-3, 1.6, 0.02, 0.22, 1.8, 1.2, 3.0, 1 / 400e3, 1 / 40e3
+PASSES = 1
+NC = len(CHUNKS)
 f32, i32, u16, b16 = "float32", "int32", "uint16", "bfloat16"
 SCRATCH = {n: ("sbuf", [128] + list(sh), d) for n, sh, d in (
     ("sta", (4, 2, 64), i32), ("stb", (8, 2, 64), i32), ("stc", (512,), i32), ("std", (512,), f32), ("str", (704,), i32),
-    ("ste", (528,), f32), ("sth", (1,), i32), ("sth2", (2,), i32), ("ls0", (512,), u16), ("ls1", (2048,), u16),
-    ("lsr", (712,), u16), ("ll1", (2048,), u16), ("llr", (712,), u16), ("om", (512,), u16),
-    ("ia", (144,), i32), ("ib", (128,), i32), ("ic", (128,), i32), ("id", (128,), i32), ("ig", (128,), i32),
-    ("ie", (128,), i32), ("ip", (8,), i32), ("iq", (8,), i32), ("ir", (4,), i32), ("iv", (64,), i32), ("col", (8,), f32),
+    ("ste", (528,), f32), ("sth", (1,), i32), ("sth2", (2,), i32), ("ls0", (512,), u16), ("ls1", (704,), u16),
+    ("ls2", (1024,), u16), ("ls3", (1024,), u16), ("ll1", (704,), u16), ("ll2", (1024,), u16), ("ll3", (1024,), u16),
+    ("om", (520,), u16), ("st0", (176,), i32),
+    ("ia", (144,), i32), ("ib", (128,), i32), ("ic", (2, 128), i32), ("id", (2, 128), i32), ("ig", (128,), i32),
+    ("ie", (128,), i32), ("ip", (8,), i32), ("iq", (8,), i32), ("iv", (64,), i32), ("col", (12,), f32),
     ("es", (8, 128), f32), ("dk", (144,), b16), ("sp", (128,), b16), ("sq", (128,), b16), ("ob", (128,), b16),
-    ("ni", (128,), b16), ("ki", (128,), b16), ("tri", (128,), f32), ("trj", (128,), f32), ("sel", (128,), f32),
-    ("ones", (128,), b16), ("vp", (64,), b16), ("nth", (4,), f32), ("thf", (4,), f32), ("thc", (4,), f32), ("m4", (4,), f32),
+    ("ni", (128,), b16), ("ki", (128,), b16), ("tri", (2, 128), f32), ("trj", (128,), f32), ("sel", (2, 128), f32),
+    ("ones", (128,), b16), ("vp", (64,), b16), ("nth", (8,), f32), ("thf", (4,), f32), ("thc", (8,), f32), ("mk", (8,), f32),
     ("xi", (R,), i32), ("xf", (R + 8,), f32), ("xr", (R,), f32), ("y", (R,), f32), ("w", (R,), f32), ("wf", (176,), f32),
-    ("wu0", (176,), u16), ("wu1", (176,), u16), ("cur", (176,), f32), ("dl", (528,), f32), ("q1", (352,), f32),
-    ("q2", (176,), f32), ("eq", (528,), f32), ("pr", (528,), f32), ("cfin", (176,), f32), ("tq", (176,), f32),
+    ("wu0", (176,), u16), ("wu1", (176,), u16), ("cur", (176,), f32), ("dl", (528,), f32), ("q1", (176,), f32),
+    ("q2", (176,), f32), ("pr", (352,), f32), ("cfin", (176,), f32),
     ("cf", (512,), f32), ("wg0", (1024,), b16), ("wg1", (1024,), b16), ("wg2", (1024,), b16), ("sm", (256,), f32),
-    ("oh", (512,), u16), ("ol", (512,), u16), ("za0", (1024,), f32), ("za1", (1024,), f32), ("zb0", (1024,), f32),
-    ("zb1", (1024,), f32), ("hl0", (2048,), f32), ("hl1", (2048,), f32), ("zz", (8, NC, 256), f32),
-    ("lc", (512,), i32), ("fe", (512,), f32), ("far", (512,), b16), ("sgn", (512,), b16), ("acc", (NC,), f32),
+    ("oh", (512,), u16), ("ol", (520,), u16), ("za0", (1024,), f32), ("za1", (1024,), f32), ("zb0", (1024,), f32),
+    ("zb1", (1024,), f32), ("hl0", (2048,), f32), ("hl1", (2048,), f32), ("zz", (8, 1024), f32), ("lc", (512,), i32),
+    ("lf", (512,), f32), ("fe", (512,), f32), ("far", (512,), b16), ("sgn", (512,), b16), ("acc", (8,), f32),
     ("cum", (512,), b16), ("et", (512,), f32), ("ea", (V,), f32), ("sg0", (R,), b16), ("sg1", (R,), b16))}
 SCRATCH.update({n: ("dram", list(sh), d) for n, sh, d in (
-    ("l0d", (8, 128, 64), u16), ("l0r", (8, 128, 64), u16), ("l1d", (8, 128, 256), u16), ("l1r", (8, 128, 256), u16),
-    ("lrd", (8, 128, 89), u16), ("lrr", (8, 128, 89), u16), ("pxd", (16, 128, 176), i32), ("pxr", (16, 128, 176), i32),
-    ("rb", (4, 128, 176), i32), ("cd", (8, 128, 22), f32), ("cr", (8, 128, 22), f32), ("etd", (NC, 128, 128), f32))})
+    ("l0d", (8, 128, 65), u16), ("l0r", (8, 128, 65), u16), ("l1d", (8, 128, 88), u16), ("l1r", (8, 128, 88), u16),
+    ("l1v", (4, 128, 88), u16), ("l2v", (4, 128, 128), u16), ("l2d", (8, 128, 128), u16), ("l2r", (8, 128, 128), u16),
+    ("l3v", (4, 128, 128), u16), ("l3d", (8, 128, 128), u16), ("l3r", (8, 128, 128), u16),
+    ("pxd", (32, 128, 88), i32), ("pxr", (32, 128, 88), i32), ("rb0", (4, 128, 88), i32), ("rb1", (4, 128, 88), i32),
+    ("pnd", (16, 128, 176), i32), ("pnr", (16, 128, 176), i32), ("cd", (8, 128, 22), f32),
+    ("cr", (8, 128, 22), f32), ("etd", (NC, 128, 128), f32))})
 for _p, (_a, _b) in enumerate(LAST):
     SCRATCH.update({n + str(_p): ("dram", [k, 128, _b - _a], f32) for n, k in (("ro", 4), ("od", 16), ("or", 16))})
 BANKS = ("pa0", "pa1", "pa2", "pd", "pb0", "pb1", "pc0", "pc1")
 SCRATCH.update({n: ("psum", [128, 512], f32) for n in BANKS})
-SEMAPHORES = (["v", "s", "t", "gc", "lsem", "l0a", "l1a", "lra", "ca", "rbi", "rlo", "pxn"]
-              + ["px%d%d" % (h, q) for h in range(2) for q in range(8)]
+SEMAPHORES = (["v", "s", "t", "gc", "lsem", "l0a", "l1a", "l2a", "l3a", "l1i", "l2i", "l3i", "ca", "rb0", "rb1", "rlo", "pxn"]
+              + ["px%d%d" % (k, q) for k in range(4) for q in range(8)] + ["dx%d" % k for k in range(4)]
               + [n + str(p) for n in ("ri", "on", "of", "dod") for p in range(len(LAST))]
-              + [n + str(c) for n in ("rg", "rk", "ed", "ea") for c in range(NC)]
-              + ["dst", "dsr", "dst1", "dl0", "dl1", "dpx", "dpy", "dlb", "dlc", "dxn", "dxa", "dxb", "dcd", "dy", "dz", "dlr",
-                 "dlq", "dw"])
+              + [n + str(c) for n in ("rg", "ed", "ea") for c in range(NC)]
+              + ["rk", "dst", "dsr", "dst1", "dl0", "dl1", "dl2", "dl3", "dpx0", "dpx1", "dpy", "dlb", "dlc1", "dlc2", "dlc3",
+                 "dxn", "dcd", "dy", "dz", "dw"])
 
 
 def layout(T, topo):
@@ -52,8 +64,13 @@ def layout(T, topo):
     for r, c in enumerate(T.cores):
         mine = [q for q, d in enumerate(T.cores) if topo.chip(d) == topo.chip(c)]
         far = [q for q in range(len(T.cores)) if q not in mine]
-        other = [d for d in topo.cores_of(c) if topo.die(d) != topo.die(c)]
-        lay.append(([q for q in mine if q != r], far, other[mine.index(r)]))
+        goal = T.cores[far[0]]
+        gates = [d for d in range(CORES) if topo.mates(topo.chip(d), topo.chip(goal)) and topo.may_write(d, goal)]
+        out = topo.may_write(c, gates[0])
+        k = [q for q in mine if topo.may_write(T.cores[q], gates[0]) == out].index(r)
+        other = [d for d in topo.cores_of(c) if topo.die(d) != topo.die(c) and topo.may_write(d, gates[0]) != out][k]
+        gate = [d for d in gates if topo.die(d) == topo.die(c if out else other)][k]
+        lay.append(([q for q in mine if q != r], far, ([gate], [other]) if out else ([], [other, gate])))
     return lay
 
 
@@ -66,65 +83,81 @@ def transfer(topo, dst, mask, src, out, sem):
     return RemoteDMATransfer(dst_ids=[DstId(rid=rid, pnc=pid)], dma_engine_mask=mask, remote_sem=sem, src=src, dst=out)
 
 
-def relay_program(g, core, T, topo, r, far):
-    masks = two(topo.engines(core, T.cores[far[0]]), len(far))
-    n = 2 * len(far)
-    jobs = [("rbi", T.rb, T.pxr[8 + r], "px1%d" % r)]
-    jobs += [("ri%d" % p, T["ro%d" % p], T["or%d" % p][2 * r + 1], "of%d" % p) for p in range(len(LAST))]
-    for s, src, dst, to in jobs:
-        g.wait_ge(T.sem[s], n)
-        g.remote_dma_fused([transfer(topo, T.cores[q], masks[k], src[k], dst, T.sem[to]) for k, q in enumerate(far)],
+def relay_program(g, core, T, topo, r, far, h, way):
+    ahead = way[way.index(core) + 1:]
+    engines = topo.engines(core, (ahead or [T.cores[far[0]]])[0])
+    n = len(far)
+    short = len(way) < 2
+    jobs = [("rb%d" % s, n, T["rb%d" % s], T.pxr[8 * (2 * h + s) + r], "px%d%d" % (2 * h + s, r)) for s in range(1 + short)]
+    jobs += [("l%di" % t, 2 * n if core == way[0] else n, T["l%dv" % t], T["l%dr" % t][r], "l%da" % t) for t in (1, 2, 3) if h]
+    jobs += [("ri%d" % p, n, T["ro%d" % p], T["or%d" % p][2 * r + h], "of%d" % p) for p in range(len(LAST) - 1 + short)]
+    for i, (s, count, src, dst, to) in enumerate(jobs):
+        masks = [1 << e for e in engines[i % 2::2]]
+        g.wait_ge(T.sem[s], count)
+        g.remote_dma_fused([transfer(topo, ahead[0], masks[k], src[k], src[k], T.sem[s]) if ahead else
+                            transfer(topo, T.cores[q], masks[k], src[k], dst, T.sem[to]) for k, q in enumerate(far)],
                            local_sem=T.sem.rlo)
     g.wait_ge(T.sem.rlo, len(jobs) * n)
 
 
 def order_of_issue(prog):
     n = len(prog)
-    succ, left, wr, rd = [[] for _ in prog], [0] * n, {}, {}
+    succ, pred, wr, rd = [[] for _ in prog], [], {}, {}
     for i, (q, reads, writes, busy, total) in enumerate(prog):
-        before = {wr[k] for k in reads + writes if k in wr} | {j for k in writes for j in rd.get(k, ())}
-        for j in before:
+        pred.append(sorted({wr[k] for k in reads + writes if k in wr} | {j for k in writes for j in rd.get(k, ())}))
+        for j in pred[i]:
             succ[j].append(i)
-        left[i] = len(before)
         for k in reads:
             rd.setdefault(k, []).append(i)
         for k in writes:
             wr[k], rd[k] = i, []
+    banks = [{k.split(".")[0] for k in p[1] + p[2]} & set(BANKS) for p in prog]
+
+    def lay_out(before, after, way, back):
+        left = [len(x) for x in before]
+        ready, ends, free, held, pool, out = [0.0] * n, [0.0] * n, {}, {}, [i for i in range(n) if not left[i]], []
+        lead = [p[4] - p[3] if back else 0.0 for p in prog]
+        while pool:
+            start = {i: max([ready[i] + lead[i], free.get(prog[i][0], 0.0)]
+                            + [t for b in banks[i] for q, t in held.get(b, {}).items() if q != prog[i][0]]) for i in pool}
+            first = min(pool, key=lambda i: start[i] + prog[i][3])
+            q = prog[first][0]
+            i = max((j for j in pool if prog[j][0] == q and start[j] <= start[first] + prog[first][3]), key=lambda j: way[j])
+            pool.remove(i)
+            out.append(i)
+            if q:
+                free[q] = start[i] + prog[i][3]
+            ends[i] = start[i] + prog[i][4] - lead[i] + LAG
+            for b in banks[i]:
+                held.setdefault(b, {})[q] = ends[i]
+            for j in after[i]:
+                ready[j] = max(ready[j], ends[i])
+                left[j] -= 1
+                if not left[j]:
+                    pool.append(j)
+        return out, ends
+
     way = [0.0] * n
     for i in reversed(range(n)):
         way[i] = prog[i][4] + LAG + max([way[j] for j in succ[i]], default=0.0)
-    banks = [{k.split(".")[0] for k in p[1] + p[2]} & set(BANKS) for p in prog]
-    ready, free, held, pool, out = [0.0] * n, {}, {}, [i for i in range(n) if not left[i]], []
-    while pool:
-        start = {i: max([ready[i], free.get(prog[i][0], 0.0)]
-                        + [t for b in banks[i] for q, t in held.get(b, {}).items() if q != prog[i][0]]) for i in pool}
-        first = min(pool, key=lambda i: start[i] + prog[i][3])
-        q = prog[first][0]
-        i = max((j for j in pool if prog[j][0] == q and start[j] <= start[first] + prog[first][3]), key=lambda j: way[j])
-        pool.remove(i)
-        out.append(i)
-        if q:
-            free[q] = start[i] + prog[i][3]
-        end = start[i] + prog[i][4] + LAG
-        for b in banks[i]:
-            held.setdefault(b, {})[q] = end
-        for j in succ[i]:
-            ready[j] = max(ready[j], end)
-            left[j] -= 1
-            if not left[j]:
-                pool.append(j)
-    return out
+    best = lay_out(pred, succ, way, False)
+    last = best
+    for _ in range(PASSES):
+        last = lay_out(pred, succ, lay_out(succ, pred, last[1], True)[1], False)
+        best = min(best, last, key=lambda x: max(x[1]))
+    return best[0]
 
 
 def rank_program(g, core, T, topo):
     lay = layout(T, topo)
     rank = T.rank_of(core)
     if rank is None:
-        for r, (near, far, rel) in enumerate(lay):
-            if rel == core:
-                relay_program(g, core, T, topo, r, far)
+        for r, (near, far, ways) in enumerate(lay):
+            for h, way in enumerate(ways):
+                if core in way:
+                    relay_program(g, core, T, topo, r, far, h, way)
         return
-    near, far, rel = lay[rank]
+    near, far, ways = lay[rank]
     sem = T.sem
     queue = {"v": g.vector, "s": g.scalar, "t": g.tensor, "y": g.sync, "g": g}
     own = {"v": "v", "s": "s", "t": "t", "g": "gc"}
@@ -152,7 +185,7 @@ def rank_program(g, core, T, topo):
         for k in reads:
             rd.setdefault(k, {})[tag[0]] = tag[1]
         for k in writes:
-            wr[k] = [tag]
+            wr[k] = [tag] * (k != "sent")
             rd[k] = {}
         for k in reads + writes:
             if k.split(".")[0] in BANKS:
@@ -199,28 +232,24 @@ def rank_program(g, core, T, topo):
     off = topo.engines(core, T.cores[far[0]])
     rest = [e for e in topo.engines(core, T.cores[near[0]]) if e not in off]
 
-    def send(moves, reads, name):
+    def send(moves, reads, name, engines=2):
         def f():
             waits("g", deps_of("g", reads, []))
             g.remote_dma_fused([transfer(topo, d, m, a, b, sem[s]) for d, m, a, b, s in moves], local_sem=sem.lsem)
-            cnt["lsem"] = cnt.get("lsem", 0) + 2 * len(moves)
+            cnt["lsem"] = cnt.get("lsem", 0) + engines * len(moves)
         note("g", reads, [name, "sent"], ISSUE, ISSUE, f)
 
     def to_far(src, dst, s):
         return [(T.cores[q], m, src(q), dst, s) for q, m in zip(far, two(off, nf))]
 
     def to_relay(src, via, vsem):
-        return [(rel, m, src(q), via[k], vsem) for k, (q, m) in enumerate(zip(far, two(rest, nf)))]
+        return [(ways[1][0], m, src(q), via[k], vsem) for k, (q, m) in enumerate(zip(far, two(rest, nf)))]
 
     def to_near(src, dst, s, engines):
         return [(T.cores[q], m, src(q), dst, s) for q, m in zip(near, two(engines, nn))]
 
     def to_all(src, dst, s):
         return to_far(lambda q: src[q], dst[rank], s) + to_near(lambda q: src[q], dst[rank], s, rest)
-
-    def halves(s0, s1, d0, d1, sf, sn, via, vsem, kf, kn):
-        send(to_relay(s1, via, vsem) + to_far(s0, d0, sf), kf, vsem + ".f")
-        send(to_near(s0, d0, sn, rest) + to_near(s1, d1, sn, off), kn, vsem + ".n")
 
     lo, hi = 16 * rank, 16 * rank + 16
     others = [(a, b) for a, b in ((0, rank), (rank + 1, 8)) if b > a]
@@ -234,29 +263,45 @@ def rank_program(g, core, T, topo):
     def keys(name, a, b):
         return ["%s%d" % (name, k) for k in range(a // 16, b // 16)]
 
+    def candidates(st, k, t):
+        wide = sum(n == 2 for o, n in CHUNKS)
+        pairs = []
+        for m in range(2):
+            x = 512 * t + 256 * m
+            pairs.append((st[:, k:k + wide, m, :], T.cand[:, x:x + 64 * wide]))
+            pairs += [(st[:, k + o // 2, o % 2, 32 * m:32 * m + 32], T.cand[:, x + 32 * o:x + 32 * o + 32]) for o, n in CHUNKS[wide:]]
+        return pairs
+
     wfk, curk, xfk = keys("wf", 0, 176), keys("cur", 0, 176), keys("xf", 0, 176) + ["xfs"]
     pdk = ["pd.%d" % j for j in range(4)]
-    lsrk, ls1k = ["lsr", "lsr.r", "lsr.d"], ["ls1.n", "ls1.0", "ls1.1"]
+    lsk = {1: ["lsr.r", "lsr.d"], 2: ["ls2.n", "ls2.p"], 3: ["ls3.n", "ls3.p"]}
     col, dl = T.col, T.dl
 
-    dma("y", [(T["str"][:], T.ray[:])], "dsr", [], ["str", "y0"], 0)
-    dma("s", [(T.sta[:, :, m, :], T.cand[:, 256 * m:256 * m + 256]) for m in range(2)], "dst", [], ["sta"], 0)
-    dma("y", [(T.pxd[8 * h + fa:8 * h + fb], T.px[16 * fa:16 * fb, RH * h:RH * h + RH]) for h in (1, 0)], "dpx", [], ["pxdf"], 720e3)
-    dma("y", [(T.pxd[8 * h + a:8 * h + b], T.px[16 * a:16 * b, RH * h:RH * h + RH]) for h in (0, 1) for a, b in nears],
+    dma("s", [(T.st0[:], T.ray[:, 0:176])], "dsr", [], ["st0"], 0)
+    dma("s", candidates(T.sta, 0, 0) + [(T.sth[:], T.th[:])], "dst", [], ["sta", "sth"], 0)
+    for s in range(2):
+        dma("y", [(T.pxd[8 * k + fa:8 * k + fb], T.px[16 * fa:16 * fb, RQ * k:RQ * k + RQ]) for k in (2 + s, s)], "dpx%d" % s, [],
+            ["pxd%d" % s], 360e3 * (1 + s))
+    dma("y", [(T.pnd[8 * h + a:8 * h + b], T.px[16 * a:16 * b, RH * h:RH * h + RH]) for h in (0, 1) for a, b in nears],
         "dpy", [], ["pxdn"], 540e3)
-    dma("y", [(T.stb[:, 4 * (k // 2):4 * (k // 2) + 4, k % 2, :], T.cand[:, 512 + 256 * k:768 + 256 * k]) for k in range(4)]
-        + [(T.xi[lo:hi, :], T.px[lo:hi, :]), (T.sth[:], T.th[:])], "dst1", [], ["stb", "xi.own", "sth"], 2e6)
     op("v", "set", (T.w[:], 0.0), [], ["w"], R)
-    op("g", "iota", (T.ip[:], [[0, 8]], 0, 1), [], ["ip"], 200)
-    op("g", "iota", (T.ia[:], [[-1, 144]], 16, 1), [], ["ia"], 400)
-    op("g", "iota", (T.iv[:], [[0, 2], [16, 32]], -255, 0), [], ["iv"], 300)
-    op("g", "iota", (T.ib[:], [[-16, 8], [0, 16]], 0, 1), [], ["ib"], 400)
-    op("g", "iota", (T["id"][:], [[-1, 16], [-16, 2], [0, 4]], 1024, 1), [], ["id"], 400)
-    op("g", "iota", (T.ic[:], [[-4, 32], [0, 4]], 0, 1), [], ["ic"], 400)
-    op("g", "iota", (T.ig[:], [[0, 8], [-8, 16]], 0, 1), [], ["ig"], 400)
-    op("g", "iota", (T.ir[:], [[-32, 4]], 0, 1), [], ["ir"], 200)
-    halves(lambda q: T.pxd[q], lambda q: T.pxd[8 + q], T.pxr[rank], T.pxr[8 + rank], "px0%d" % rank, "pxn", T.rb, "rbi",
-           ["pxdf"], ["pxdn"])
+    op("g", "iota", (T.ip[:], [[0, 8]], 0, 1), [], ["ip", "sent"], 200)
+    op("g", "iota", (T.ia[:], [[-1, 144]], 16, 1), [], ["ia", "sent"], 400)
+    op("g", "iota", (T.iv[:], [[0, 2], [16, 32]], -255, 0), [], ["iv", "sent"], 300)
+    op("g", "iota", (T.ib[:], [[-16, 8], [0, 16]], 0, 1), [], ["ib", "sent"], 400)
+    op("g", "iota", (T.ig[:], [[0, 8], [-8, 16]], 0, 1), [], ["ig", "sent"], 400)
+    for n in (1, 2):
+        op("g", "iota", (T["id"][:, n - 1, :], [[-1, 16], [-16, n], [0, 8 // n]], 1024, 1), [], ["id%d" % n, "sent"], 400)
+        op("g", "iota", (T.ic[:, n - 1, :], [[-8 // n, 16 * n], [0, 8 // n]], 0, 1), [], ["ic%d" % n, "sent"], 400)
+    for s in range(2):
+        via = [way if not s or len(way) < 2 else [] for way in ways]
+        moves = [(via[h][0], T.pxd[8 * (2 * h + s) + q], T["rb%d" % s][k], "rb%d" % s) if via[h] else
+                 (T.cores[q], T.pxd[8 * (2 * h + s) + q], T.pxr[8 * (2 * h + s) + rank], "px%d%d" % (2 * h + s, rank))
+                 for h in range(2) for k, q in enumerate(far)]
+        engines = off[s::2] + (rest[s::2] if via[1] else off[1 - s::2])
+        send([(c, 1 << e, x, y, z) for e, (c, x, y, z) in zip(engines, moves)], ["pxd%d" % s], "pxf%d" % s, 1)
+    send(to_near(lambda q: T.pnd[q], T.pnr[rank], "pxn", rest) + to_near(lambda q: T.pnd[8 + q], T.pnr[8 + rank], "pxn", off),
+         ["pxdn"], "pxn")
 
     def row_of_w():
         dma("y", [(T.w[0:128:16, :], T.wf[:])], "dw", wfk, ["w"], 0)
@@ -268,8 +313,10 @@ def rank_program(g, core, T, topo):
         vts(out, T.std[:, 0:n], 1.0 / 16, None, (A.mult,), ["std"], [okey], n)
 
     vts(T.iq[:, 0:1], T.ip[:, 0:1], 15, None, (A.bitwise_and,), ["ip"], ["iq0"])
-    op("v", "copy", (T.wf[:], T["str"][:, 0:176]), ["str"], wfk, 176)
+    op("v", "copy", (T.wf[:], T.st0[:]), ["st0"], wfk, 176)
     row_of_w()
+    dma("y", [(T["str"][:], T.ray[:])] + candidates(T.stb, 0, 1) + candidates(T.stb, 4, 2) + [(T.xi[lo:hi, :], T.px[lo:hi, :])],
+        "dst1", wfk, ["stb", "xi.own", "str"], 4e6)
     vts(col[:, 0:1], T.iq[:, 0:1], 0.0, -U, (A.is_equal, A.mult), ["iq0"], ["col0"])
     op("v", "copy", (col[:, 1:2], T.iq[:, 0:1]), ["iq0"], ["col1"])
     for h in range(2):
@@ -277,150 +324,194 @@ def rank_program(g, core, T, topo):
     vts(T.dk[:], T.ia[:], 0.0, col[:, 0:1], (A.is_equal, A.mult), ["ia", "col0"], ["dk"], 144)
     vts(T.ni[:], T.ia[:, 16:144], 0.0, -0.25, (A.is_equal, A.mult), ["ia"], ["ni"], 128)
     vts(T.vp[:], T.iv[:], col[:, 1:2], -4 * U, (A.add, A.mult), ["iv", "col1"], ["vp"])
-    op("v", "set", (T.lsr[:, 704:712], 0), [], ["lsr"])
+    op("v", "set", (T.ol[:, 512:520], 0), [], ["olt"])
     vts(T.sth2[:, 0:1], T.sth[:], 10, None, (A.arith_shift_right,), ["sth"], ["sth2a"])
     vts(T.sth2[:, 1:2], T.sth[:], 1023, None, (A.bitwise_and,), ["sth"], ["sth2b"])
     op("v", "tt", (T.ste[:], T["str"][:, 176:704], T["str"][:, 0:528], A.subtract), ["str"], ["ste"], 1056)
-    op("v", "copy", (T.lsr[:, 0:176], T["str"][:, 0:176]), ["str"], ["lsr.r"], 176)
-    op("v", "copy", (T.lsr[:, 704:706], T.sth2[:]), ["sth2a", "sth2b"], ["lsr"])
-    vts(T.lsr[:, 176:704], T.ste[:], U, None, (A.add,), ["ste"], ["lsr.d"], 528)
-    dma("s", [(T.lrd[:], T.lsr[:])], "dlr", lsrk, ["lrd"], 180e3)
+    op("v", "copy", (T.ls1[:, 0:176], T["str"][:, 0:176]), ["str"], ["lsr.r"], 176)
+    op("v", "copy", (T.ol[:, 512:514], T.sth2[:]), ["sth2a", "sth2b"], ["olt"])
+    vts(T.ls1[:, 176:704], T.ste[:], U, None, (A.add,), ["ste"], ["lsr.d"], 528)
     op("v", "set", (T.xf[:, R:R + 8], float(BIG)), [], ["xfs"])
     op("v", "set", (T.xf[:, R:R + 1], float(-BIG)), [], ["xfs"])
     op("v", "set", (T.cur[:], 0.0), [], curk, 176)
     op("v", "set", (T.ones[:], 1.0), [], ["ones"])
-    op("v", "set", (col[:, 5:6], -8.5), [], ["col5"])
+    op("v", "set", (col[:, 4:5], -8.5), [], ["col4"])
     vts(T.sp[:], T.ib[:], 0.0, -0.25, (A.is_equal, A.mult), ["ib"], ["sp"], 128)
     vts(T.sq[:], T.ib[:], 1.0, None, (A.is_equal,), ["ib"], ["sq"], 128)
     op("v", "tt", (T.sp[:], T.sp[:], T.sq[:], A.add), ["sp", "sq"], ["sp"], 256)
     vts(col[:, 2:3], T.iq[:, 0:1], 1.0, None, (A.is_equal,), ["iq0"], ["col2"])
     vts(col[:, 3:4], T.iq[:, 0:1], 1.0, None, (A.not_equal,), ["iq0"], ["col3"])
+    vts(col[:, 5:6], col[:, 2:3], 2.0, -1.0, (A.mult, A.add), ["col2"], ["col5"])
     vts(T.ki[:], T.ia[:, 16:144], 0.0, 128.0, (A.is_equal, A.mult), ["ia"], ["ki"], 128)
-    vts(T.iq[:, 1:2], T.ip[:, 0:1], 3, None, (A.bitwise_and,), ["ip"], ["iq1"])
-    vts(col[:, 4:5], T.iq[:, 1:2], 32.0, 64.0, (A.mult, A.add), ["iq1"], ["col4"])
     vts(T.ie[:], T.ia[:, 16:144], 7, None, (A.bitwise_and,), ["ia"], ["ie"], 128)
     vts(T.ob[:], T.ie[:], 0.0, None, (A.is_equal,), ["ie"], ["ob"], 128)
-    vts(T["id"][:], T["id"][:], 31, None, (A.bitwise_and,), ["id"], ["id"], 128)
-    vts(T.sel[:], T["id"][:], 0.0, None, (A.is_equal,), ["id"], ["sel"], 128)
-    vts(T.ir[:], T.ir[:], 5, None, (A.arith_shift_right,), ["ir"], ["ir"])
-    vts(T.m4[:], T.ir[:], 0.0, None, (A.is_equal,), ["ir"], ["m4"])
-    vts(T.tri[:], T.ic[:], 0.0, None, (A.is_ge,), ["ic"], ["tri"], 128)
     vts(T.trj[:], T.ia[:, 16:144], 0.0, None, (A.is_lt,), ["ia"], ["trj"], 128)
-    op("v", "tt", (T.tri[:], T.tri[:], T.trj[:], A.mult), ["tri", "trj"], ["tri"], 256)
+    for n in (1, 2):
+        k, ids, tri = str(n), T["id"][:, n - 1, :], T.tri[:, n - 1, :]
+        vts(T.iq[:, n:n + 1], T.ip[:, 0:1], 8 // n - 1, None, (A.bitwise_and,), ["ip"], ["iq" + k])
+        vts(col[:, 5 + n:6 + n], T.iq[:, n:n + 1], 16.0 * n, 64.0, (A.mult, A.add), ["iq" + k], ["lim" + k])
+        vts(ids, ids, 16 * n - 1, None, (A.bitwise_and,), ["id" + k], ["id" + k], 128)
+        vts(T.sel[:, n - 1, :], ids, 0.0, None, (A.is_equal,), ["id" + k], ["sel" + k], 128)
+        vts(tri, T.ic[:, n - 1, :], 0.0, None, (A.is_ge,), ["ic" + k], ["tri" + k], 128)
+        op("v", "tt", (tri, tri, T.trj[:], A.mult), ["tri" + k, "trj"], ["tri" + k], 256)
+        vts(T.iq[:, 2 + n:3 + n], T.ip[:, 0:1], 3 + n, None, (A.arith_shift_right,), ["ip"], ["is" + k])
+    for c, (o, n) in enumerate(CHUNKS):
+        vts(T.mk[:, c:c + 1], T.iq[:, 2 + n:3 + n], float(o // n), None, (A.is_equal,), ["is%d" % n], ["mk%d" % c])
     for b in range(8):
         vts(T.es[:, b, :], T.ig[:], float(b), None, (A.is_equal,), ["ig"], ["es%d" % b], 128)
-    op("v", "copy", (T.ls1[:, 0:1024], T.stb[:]), ["stb"], ["ls1.n"], 1024)
-    for h in range(2):
-        numbers_to_places(T.stb[:, 4 * h:4 * h + 4], 512, T.ls1[:, 1024 + 512 * h:1536 + 512 * h], "stb", "ls1.%d" % h)
-    dma("y", [(T.l1d[:], T.ls1[:])], "dlc", ls1k, ["l1d"], 520e3)
+    for t in (2, 3):
+        ls, src = T["ls%d" % t], T.stb[:, 4 * t - 8:4 * t - 4]
+        op("v", "copy", (ls[:, 0:512], src), ["stb"], ["ls%d.n" % t], 512)
+        numbers_to_places(src, 512, ls[:, 512:1024], "stb", "ls%d.p" % t)
+    for t in (1, 2, 3):
+        dma("s", [(T["l%dd" % t][:], T["ls%d" % t][:])], "dlc%d" % t, lsk[t], ["l%dd" % t], 260e3)
+
+    def later_lists(t, after):
+        n = "l%d" % t
+        src = T[n + "d"]
+        send(to_relay(lambda q: src[q], T[n + "v"], n + "i") + to_near(lambda q: src[q], T[n + "r"][rank], n + "a", off),
+             [n + "d"] + after, n + "a")
+        arrives(n + "a", 2 * nn + nf, n + "r", n + "a", 5 * HOP)
+
+    def lists_land(t, after):
+        n = "l%d" % t
+        land("y", T["l" + n], T[n + "r"], T["ls%d" % t], "d" + n, [n + "r", after] + lsk[t], "l" + n, 260e3)
+
+    def rays():
+        lists_land(1, "z%d1" % (NC - 1))
+        op("v", "copy", (T.wf[:], T.ll1[:, 0:176]), ["ll1"], wfk, 176)
+        vts(dl[:], T.ll1[:, 176:704], -U, 1.0 / U, (A.add, A.mult), ["ll1"], ["dl"], 528)
 
     def thresholds():
-        op("v", "copy", (T.thf[:, 0:2], T.llr[:, 704:706]), ["llr"], ["thf"])
-        op("v", "copy", (T.wf[:], T.llr[:, 0:176]), ["llr"], wfk, 176)
+        op("v", "copy", (T.thf[:, 0:2], T.om[:, 512:514]), ["om"], ["thf"])
         vts(T.thf[:, 2:3], T.thf[:, 0:1], 1024.0, T.thf[:, 1:2], (A.mult, A.add), ["thf"], ["thf2"])
-        vts(dl[:], T.llr[:, 176:704], -U, 1.0 / U, (A.add, A.mult), ["llr"], ["dl"], 528)
-        vts(T.thc[:], T.m4[:], T.thf[:, 2:3], None, (A.mult,), ["m4", "thf2"], ["thc"])
-        op("t", "mm", [(T.pd[:, 0:4], T.sel[:], T.thc[:], True, True)], ["sel", "thc"], pdk, 128)
-        vts(T.nth[:], T.pd[:, 0:4], -1.0, -0.5, (A.mult, A.add), pdk, ["nth"])
+        vts(T.thc[:, 0:NC], T.mk[:, 0:NC], T.thf[:, 2:3], None, (A.mult,), ["mk%d" % c for c in range(NC)] + ["thf2"], ["thc"])
+        op("t", "mm", [(T.pd[:, c:c + 1], T.sel[:, n - 1, :], T.thc[:, c:c + 1], True, True) for c, (o, n) in enumerate(CHUNKS)],
+           ["sel1", "sel2", "thc"], pdk, 700)
+        vts(T.nth[:, 0:NC], T.pd[:, 0:NC], -1.0, -0.5, (A.mult, A.add), pdk, ["nth"])
 
     def prepare(t):
-        src, key = (T.sta[:], "sta") if t == 0 else (T.ll1[:, 512 * t - 512:512 * t], "ll1")
+        src, key = (T.sta[:], "sta") if t == 0 else (T["ll%d" % (t + 1)][:, 0:512], "ll%d" % (t + 1))
         op("v", "copy", (T.cf[:], src), [key], ["cf"], 512)
 
     turn = {"s": 0}
 
     def look(t, c, m, q):
-        buf, base, key = (T.ls0, 0, "ls0.%d" % (c // 2)) if t == 0 else (T.ll1, 512 + 512 * t, "ll1")
-        k = base + 128 * c + 64 * m
-        out, ok = T["pc%d" % (c % 2)][:, 64 * m:64 * m + 64], "pc%d.%d" % (c % 2, m)
+        o, n = CHUNKS[c]
+        buf, base, key = (T.ls0, 0, "ls0.%d" % (o // 4)) if t == 0 else (T["ll%d" % (t + 1)], 512, "ll%d" % (t + 1))
+        k = base + 64 * o + 32 * n * m
+        out, ok = T["pc%d" % (c % 2)][:, 32 * n * m:32 * n * (m + 1)], "pc%d.%d" % (c % 2, m)
         turn["s"] ^= q == "s"
         e = turn["s"] if q == "s" else 2
         wg, wgk = T["wg%d" % e], "wg%d" % e
         parts = [(wg[:, 512 * b:512 * b + 512], T.w[:, 0:R].indirect(buf[:, k + 32 * b:k + 32 * b + 32]),
-                  float(-255 - 512 * b - 1024 * c)) for b in range(2)]
+                  float(-255 - 512 * (o + b))) for b in range(n)]
         if q == "s":
-            op("s", "acts", [(o, i, F.Copy, z) for o, i, z in parts], [key, "w"], [wgk], 1024 * GATHER + 100)
+            op("s", "acts", [(x, i, F.Copy, z) for x, i, z in parts], [key, "w"], [wgk], n * (512 * GATHER + 50))
         else:
-            op("v", "tss", [(o, i, z, None, A.add) for o, i, z in parts], [key, "w"], [wgk], 1024 * GATHER + 100)
-        op("t", "mm", [(out, T.ni[:], T.vp[:], True, False)]
-           + [(out, T.dk[:, 16 - i:144 - i], wg[:, i:1024:16], False, i == 15) for i in range(16)], ["dk", "ni", "vp", wgk], [ok], 700)
+            op("v", "tss", [(x, i, z, None, A.add) for x, i, z in parts], [key, "w"], [wgk], n * (512 * GATHER + 50))
+        op("t", "mm", [(out, T.ni[:], T.vp[:, 0:32 * n], True, False)]
+           + [(out, T.dk[:, 16 - i:144 - i], wg[:, i:512 * n:16], False, i == 15) for i in range(16)],
+           ["dk", "ni", "vp", wgk], [ok], 700)
 
     def mask(c, both=True):
-        e = c % 2
-        d, s = slice(128 * c, 128 * c + 128), slice(128 * e, 128 * e + 128)
-        op("v", "tt", (T.sm[:, s], T["pc%d" % e][:, 0:128], T.cf[:, d], A.max), ["pc%d.0" % e, "pc%d.1" % e, "cf"], ["sm%d" % e], 128)
-        for o, ok, n in ((T.oh, "oh", R), (T.ol, "ol", R + 1))[0 if both else 1:]:
-            vts(o[:, d], T.sm[:, s], float(n), None, (A.min,), ["sm%d" % e], ["%s%d" % (ok, c)], 128)
+        (o, n), e = CHUNKS[c], c % 2
+        d, s = slice(64 * o, 64 * (o + n)), slice(128 * e, 128 * e + 64 * n)
+        op("v", "tt", (T.sm[:, s], T["pc%d" % e][:, 0:64 * n], T.cf[:, d], A.max), ["pc%d.0" % e, "pc%d.1" % e, "cf"],
+           ["sm%d" % e], 64 * n)
+        for x, ok, r in ((T.oh, "oh", R), (T.ol, "ol", R + 1))[0 if both else 1:]:
+            vts(x[:, d], T.sm[:, s], float(r), None, (A.min,), ["sm%d" % e], ["%s%d" % (ok, c)], 64 * n)
 
-    def side(c, j, n):
-        return slice(n * j, n * j + n) if c == NC - 1 else slice(j, 2 * n, 2)
+    def side(c, j, n, x=0):
+        return slice(x + n * j, x + n * j + n) if c == NC - 1 else slice(x + j, x + 2 * n, 2)
 
     def see(t, c):
-        e = c % 2
-        hl = T["hl%d" % e]
-        for j, (o, ok), z, f in zip((0, 1), ((T.oh, "oh%d" % c), (T.om, "om") if t == 0 else (T.ol, "ol%d" % c)),
+        (o, n), e = CHUNKS[c], c % 2
+        hl, nv, k = T["hl%d" % e], 512 * n, 64 * o
+        for j, (x, ok), z, f in zip((0, 1), ((T.oh, "oh%d" % c), (T.om, "om") if t == 0 else (T.ol, "ol%d" % c)),
                                     ("za%d" % e, "zb%d" % e), (A.max, A.min)):
-            d, k = side(c, j, 1024), 128 * c
-            op("s", "act", (T[z][:], T.xf[:, 0:R + 8].indirect(o[:, k:k + 64]), F.Copy), [ok] + xfk, [z], 1024 * GATHER)
-            op("v", "tt", (hl[:, d], T.xf[:, 0:R + 8].indirect(o[:, k + 64:k + 128]), T[z][:], f), [ok, z] + xfk,
-               ["hl%d%d" % (e, j)], 1024 * GATHER)
+            d = side(c, j, nv)
+            op("s", "act", (T[z][:, 0:nv], T.xf[:, 0:R + 8].indirect(x[:, k:k + 32 * n]), F.Copy), [ok] + xfk, [z], nv * GATHER)
+            op("v", "tt", (hl[:, d], T.xf[:, 0:R + 8].indirect(x[:, k + 32 * n:k + 64 * n]), T[z][:, 0:nv], f), [ok, z] + xfk,
+               ["hl%d%d" % (e, j)], nv * GATHER)
             if c == NC - 1:
-                dma("y", [(T.zz[:, a, c, side(c, j, 128)], hl[16 * a:16 * a + 16, d]) for a in range(8)], ("rg", "rk")[j] + str(c),
-                    ["hl%d%d" % (e, j)], ["z%d%d" % (c, j)], 520e3)
+                dma("y", [(T.zz[:, a, side(c, j, 64 * n, 2 * k)], hl[16 * a:16 * a + 16, d]) for a in range(8)],
+                    ("rg%d" % c, "rk")[j], ["hl%d%d" % (e, j)], ["z%d%d" % (c, j)], 512 * nv)
         if c < NC - 1:
-            dma("y", [(T.zz[:, a, c, :], hl[16 * a:16 * a + 16, :]) for a in range(8)], "rg%d" % c,
-                ["hl%d0" % e, "hl%d1" % e], ["z%d0" % c, "z%d1" % c], 1040e3)
+            dma("y", [(T.zz[:, a, 2 * k:2 * k + 128 * n], hl[16 * a:16 * a + 16, 0:2 * nv]) for a in range(8)], "rg%d" % c,
+                ["hl%d0" % e, "hl%d1" % e], ["z%d0" % c, "z%d1" % c], 1024 * nv)
 
-    def carve(c):
-        ps, d, n = T[BANKS[c]], slice(128 * c, 128 * c + 128), BANKS[c] + "."
+    def carve(t, c):
+        o, n = CHUNKS[c]
+        wd, k, b = 64 * n, str(c), BANKS[c] + ".c"[:1 + c // 4]
+        d, ps = slice(64 * o, 64 * o + wd), [T[BANKS[c]][:, 128 * j:128 * j + wd] for j in range(4)]
+        shared = [BANKS[c] + ".%d" % j for j in range(3 * (c // 4))]
         for a in range(1, 8):
-            for j, o in ((0, A.max), (1, A.min)):
-                acc, key, z = ps[:, 128 * j:128 * j + 128], n + str(j), "z%d%d" % (c, j)
-                if a == 1:
-                    op("v", "tt", (acc, T.zz[:, 0, c, side(c, j, 128)], T.zz[:, 1, c, side(c, j, 128)], o), [z], [key], 256)
+            for j, f in ((0, A.max), (1, A.min)):
+                key, z, x = b + str(j), "z%d%d" % (c, j), side(c, j, wd, 128 * o)
+                if a == 1 and FIRST[t > 0][c] == "v":
+                    op("v", "tt", (ps[j], T.zz[:, 0, x], T.zz[:, 1, x], f), [z] + shared * j, [key] + shared * (1 - j), 2 * wd)
                 else:
-                    op("v", "tt", (acc, acc, T.zz[:, a, c, side(c, j, 128)], o), [z, key], [key], 128)
-        k = str(c)
-        vts(T.lc[:, d], ps[:, 128:256], 0.0, float(TOP), (A.max, A.min), [n + "1"], ["lc" + k], 128)
-        vts(ps[:, 0:128], ps[:, 0:128], float(TOP), T.nth[:, c:c + 1], (A.min, A.add), [n + "0", "nth"], [n + "0"], 128)
-        op("v", "tt", (T.far[:, d], ps[:, 0:128], T.lc[:, d], A.is_gt), [n + "0", "lc" + k], ["far" + k], 128)
-        op("t", "mm", [(ps[:, 256:384], T.ob[:], T.far[:, d], True, True)], ["ob", "far" + k], [n + "2"], 100)
-        vts(T.fe[:, d], T.lc[:, d], -0.25, -0.375, (A.mult, A.add), ["lc" + k], ["fe" + k], 128)
-        op("s", "act", (T.sgn[:, d], ps[:, 256:384], F.Sign, col[:, 5:6]), [n + "2", "col5"], ["sgn" + k, "acc" + k], 250,
+                    if a == 1:
+                        op("s", "act", (ps[j], T.zz[:, 0, x], F.Copy), [z], [key], wd + 80)
+                    op("v", "tt", (ps[j], ps[j], T.zz[:, a, x], f), [z, key], [key], wd)
+        fe, lk, fk = T.fe[:, d], ["lc" + k], ["fe" + k]
+        if ROUND[t > 0][c] == "v":
+            low = T.lc[:, d]
+            vts(low, ps[1], 0.0, float(TOP), (A.max, A.min), [b + "1"], lk, wd)
+            vts(fe, low, -0.25, -0.375, (A.mult, A.add), lk, fk, wd)
+        else:
+            low = T.lf[:, d]
+            op("s", "act", (low, ps[1], F.Copy, MAGIC), [b + "1"], lk, wd + 80)
+            op("s", "act", (low, low, F.Relu, -MAGIC), lk, lk, wd + 80)
+            op("s", "act", (fe, low, F.Relu, float(TOP), -1.0), lk, fk, wd + 80)
+            op("s", "act", (fe, fe, F.Copy, -TOP / 4 - 0.375, 0.25), fk, fk, wd + 80)
+        vts(ps[0], ps[0], float(TOP), T.nth[:, c:c + 1], (A.min, A.add), [b + "0", "nth"], [b + "0"], wd)
+        op("v", "tt", (T.far[:, d], ps[0], low, A.is_gt), [b + "0"] + lk, ["far" + k], wd)
+        op("t", "mm", [(ps[2], T.ob[:], T.far[:, d], True, True)], ["ob", "far" + k], [b + "2"], 100)
+        op("s", "act", (T.sgn[:, d], ps[2], F.Sign, col[:, 4:5]), [b + "2", "col4"], ["sgn" + k, "acc" + k], wd + 120,
            accum_out=T.acc[:, c:c + 1])
-        op("t", "mm", [(ps[:, 256:257], T.tri[:], T.acc[:, c:c + 1], True, True)], ["tri", "acc" + k], [n + "2"], 150)
-        op("v", "scan", (T.cum[:, d], T.sgn[:, d], T.ones[:], ps[:, 256:257], A.add, A.add), ["sgn" + k, "ones", n + "2"],
-           ["cum" + k], 128)
-        op("t", "mm", [(ps[:, 384:512], T.ni[:], T.cum[:, d], True, False), (ps[:, 384:512], T.ki[:], T.sgn[:, d], False, True)],
-           ["ni", "ki", "cum" + k, "sgn" + k], [n + "3"], 200)
-        et, ek, x = T.et[:, d], "et" + k, 1024 * c
-        vts(ps[:, 384:512], ps[:, 384:512], col[:, 4:5], None, (A.is_ge,), [n + "3", "col4"], [n + "3"], 128)
-        op("v", "tt", (et, ps[:, 384:512], T.fe[:, d], A.mult), [n + "3", "fe" + k], [ek], 128)
+        start = T[BANKS[c]][:, 256:257]
+        op("t", "mm", [(start, T.tri[:, n - 1, :], T.acc[:, c:c + 1], True, True)], ["tri%d" % n, "acc" + k], [b + "2"], 150)
+        op("v", "scan", (T.cum[:, d], T.sgn[:, d], T.ones[:, 0:wd], start, A.add, A.add), ["sgn" + k, "ones", b + "2"],
+           ["cum" + k], wd)
+        op("t", "mm", [(ps[3], T.ni[:], T.cum[:, d], True, False), (ps[3], T.ki[:], T.sgn[:, d], False, True)],
+           ["ni", "ki", "cum" + k, "sgn" + k], [b + "3"], 200)
+        et, ek, x = T.et[:, d], "et" + k, 512 * o
+        vts(ps[3], ps[3], col[:, 5 + n:6 + n], None, (A.is_ge,), [b + "3", "lim%d" % n], [b + "3"], wd)
+        op("v", "tt", (et, ps[3], fe, A.mult), [b + "3"] + fk + shared, [ek], wd)
         if SPREAD[c] == "pe":
             for h in range(2):
-                pc, pk = T["pc%d" % h], ["pc%d.0" % h, "pc%d.1" % h]
-                op("t", "mm", [(pc[:, 128 * s:128 * s + 128], T.es[:, 4 * h + s, :], et, True, True) for s in range(4)],
-                   ["es%d" % b for b in range(8)] + [ek], pk, 1100)
-                op("s", "act", (T.ea[:, x + 512 * h:x + 512 * h + 512], pc[:], F.Copy), pk, ["ea%d%d" % (c, h)], 600)
+                pc, pk = T["pc%d" % h], ["pc%d.%d" % (h, j) for j in range(3)]
+                op("t", "mm", [(pc[:, wd * s:wd * s + wd], T.es[:, 4 * h + s, :], et, True, True) for s in range(4)],
+                   ["es%d" % j for j in range(8)] + [ek], pk, 550 * n)
+                op("s", "act", (T.ea[:, x + 4 * wd * h:x + 4 * wd * (h + 1)], pc[:, 0:4 * wd], F.Copy), pk, ["ea" + k + "h" * h],
+                   4 * wd + 80)
             return
         if SPREAD[c] == "dram":
             dma("y", [(T.etd[c], et)], "ed" + k, [ek], ["etd" + k], 65e3)
             et, ek = T.etd[c], "etd" + k
-        dma("y", [(T.ea[16 * a:16 * a + 16, x:x + 1024], et) for a in range(8)], "ea" + k, [ek], ["ea%d0" % c, "ea%d1" % c], 520e3)
+        dma("y", [(T.ea[16 * a:16 * a + 16, x:x + 512 * n], et) for a in range(8)], "ea" + k, [ek], ["ea" + k, "ea" + k + "h"],
+            260e3 * n)
 
-    eak = ["ea%d%d" % (c, h) for c in range(NC) for h in range(2)]
+    eak = ["ea%d" % c + "h" * h for c in range(NC) for h in range(2)]
 
     def places(t):
         op("v", "copy", (T.wu0[:], T.wf[:]), wfk, ["wu0"], 176)
         if t == 0:
             return
-        op("v", "tss", [(T.eq[:, k * 176:k * 176 + 176], T.cur[:], U * k, None, A.is_equal) for k in range(3)], curk, ["eq"], 600)
-        op("v", "tt", (T.pr[:], T.eq[:], dl[:], A.mult), ["eq", "dl"], ["pr"], 1056)
-        op("v", "tt", (T.q1[:, 176:352], T.pr[:, 0:176], T.pr[:, 176:352], A.add), ["pr"], ["q1t"], 352)
-        op("v", "tt", (T.q1[:, 0:176], T.q1[:, 176:352], T.pr[:, 352:528], A.add), ["pr", "q1t"], ["q1"], 352)
+        eq = (T.pc0[:, 128:304], T.pc0[:, 304:480], T.pc1[:, 128:304], T.pc1[:, 304:480])
+        ek, d, pr = ("pc0.2", "pc0.2", "pc1.2"), [dl[:, 176 * k:176 * k + 176] for k in range(3)], (T.pr[:, 0:176], T.pr[:, 176:352])
+        op("v", "tss", [(eq[k], T.cur[:], U * k, None, A.is_equal) for k in range(3)], curk, ["pc0.2", "pc1.2"], 600)
         if t == 1:
-            op("v", "tt", (T.pr[:, 0:352], T.eq[:, 0:352], dl[:, 176:528], A.mult), ["eq", "dl"], ["pr"], 704)
-            op("v", "tt", (T.q2[:], T.pr[:, 0:176], T.pr[:, 176:352], A.add), ["pr"], ["q2"], 352)
+            op("v", "tt", (pr[0], eq[0], d[1], A.mult), [ek[0], "dl"], ["pr0"], 176)
+            op("v", "tt", (eq[3], eq[1], d[2], A.mult), [ek[1], "dl"], [ek[2]], 176)
+            op("v", "tt", (T.q2[:], eq[3], pr[0], A.add), [ek[2], "pr0"], ["q2"], 176)
+        op("v", "tt", (pr[0], eq[0], d[0], A.mult), [ek[0], "dl"], ["pr0"], 176)
+        op("v", "tt", (eq[1], eq[1], d[1], A.mult), [ek[1], "dl"], [ek[1]], 176)
+        op("v", "tt", (eq[2], eq[2], d[2], A.mult), [ek[2], "dl"], [ek[2]], 176)
+        op("v", "tt", (pr[1], eq[1], pr[0], A.add), [ek[1], "pr0"], ["pr1"], 176)
+        op("v", "tt", (T.q1[:], eq[2], pr[1], A.add), [ek[2], "pr1"], ["q1"], 176)
 
     def units(a, b, most=32):
         n = (b - a + most - 1) // most
@@ -431,39 +522,48 @@ def rank_program(g, core, T, topo):
 
     def flags(t, step, p, a, b):
         sg, sk = T["sg%d" % step], "sg%d" % step
-        o = T["wu%d" % step]
         for x, y in units(a, b):
-            op("s", "act", (sg[:, 16 * x:16 * y], T.ea[:, 0:V].indirect(o[:, x:y]), F.Sign, col[:, 2:3], col[:, 3:4]),
-               eak + (keys("wu1", x, y) if step else ["wu0"]) + ["col2", "col3"], keys(sk, x, y), 16 * (y - x) * GATHER + 30)
-        ps, key = T["pb%d" % (p % 2)][:, 176 * step + a:176 * step + b], "pb%d.%d.%d" % (p % 2, step, 0)
+            out, src = sg[:, 16 * x:16 * y], T.ea[:, 0:V].indirect(T["wu%d" % step][:, x:y])
+            reads, n = eak + (keys("wu1", x, y) if step else ["wu0"]) + ["col2", "col3", "col5"], 16 * (y - x) * GATHER + 30
+            if (step, p) in FLAGS and x == a:
+                vts(out, src, col[:, 2:3], col[:, 5:6], (A.is_lt, A.mult), reads, keys(sk, x, y), n)
+            else:
+                op("s", "act", (out, src, F.Sign, col[:, 2:3], col[:, 3:4]), reads, keys(sk, x, y), n)
+        pb, key, tk = T["pb%d" % (p % 2)], "pb%d.%d" % (p % 2, step), "pb%d.2" % (p % 2)
+        ps, tq = pb[:, 176 * step + a:176 * step + b], pb[:, 352:352 + b - a]
         op("t", "mm", [(ps, T.dk[:, 16 - k:144 - k], sg[:, 16 * a + k:16 * b:16], k == 0, k == 15) for k in range(16)],
            ["dk"] + keys(sk, a, b), [key], 8 * max(64, b - a) + 100)
         if t == 0:
             q, qk = dl[:, 176 * step + a:176 * step + b], "dl"
         else:
             q, qk = (T.q1[:, a:b], "q1") if step == 0 else (T.q2[:, a:b], "q2")
-        wfp, tqp, cp = keys("wf", a, b), keys("tq", a, b), keys("cur", a, b)
+        wfp, cp = keys("wf", a, b), keys("cur", a, b)
         if step == 0 or t < 2:
-            op("v", "tt", (T.tq[:, a:b], ps, q, A.mult), [key, qk], tqp, b - a)
-            op("v", "tt", (T.wf[:, a:b], T.wf[:, a:b], T.tq[:, a:b], A.add), wfp + tqp, wfp, 2 * (b - a))
+            op("v", "tt", (tq, ps, q, A.mult), [key, qk], [tk], b - a)
+            op("v", "tt", (T.wf[:, a:b], tq, T.wf[:, a:b], A.add), wfp + [tk], wfp, b - a)
         if step == 0:
             op("v", "copy", (T.wu1[:, a:b], T.wf[:, a:b]), wfp, keys("wu1", a, b), b - a)
         op("v", "tt", (T.cur[:, a:b], ps, T.cur[:, a:b], A.add), [key] + cp, cp, b - a)
 
-    def move(t, step, a, b):
+    def move(t, step, a, b, scalar):
         src, name = (T.xi, "xi") if step else (T.xr, "xr") if t else (T.xf, "xf")
+        dst, dname = (T.xf, "xf") if step and t < 2 else (T.xi, "xi")
         sg, sk = T["sg%d" % step], "sg%d" % step
         for x, y in units(a, b):
             k = BANKS[rot[0]]
             rot[0] = (rot[0] + 1) % 4
-            pk, n = [k + ".%d" % j for j in range(4)], 16 * (y - x)
-            op("t", "mm", [(T[k][:, 0:n], T.sp[:], sg[:, 16 * x:16 * y], True, True)], ["sp"] + keys(sk, x, y), pk, n // 2 + 50)
-            op("v", "tt", (T.y[:, 16 * x:16 * y], src[:, 16 * x:16 * y], T[k][:, 0:n], A.mult), pk + keys(name, x, y),
-               keys("y", x, y), n)
-        dst, name = (T.xf, "xf") if step and t < 2 else (T.xi, "xi")
-        for x, y in units(a, b, 48):
+            pk, n, d = [k + ".%d" % j for j in range(4)], 16 * (y - x), slice(16 * x, 16 * y)
+            op("t", "mm", [(T[k][:, 0:n], T.sp[:], sg[:, d], True, True)], ["sp"] + keys(sk, x, y), pk, n // 2 + 50)
+            if scalar:
+                op("s", "act", (T.xr[:, d], T.ea[:, 0:V].indirect(T.wu1[:, x:y]), F.Copy), eak + keys("wu1", x, y),
+                   keys("xr", x, y), n * GATHER + 30)
+                op("v", "tt", (T[k][:, 0:n], src[:, d], T[k][:, 0:n], A.mult), pk + keys(name, x, y), pk, n)
+                op("v", "tt", (dst[:, d], T[k][:, 0:n], T.xr[:, d], A.add), pk + keys("xr", x, y), keys(dname, x, y), n)
+            else:
+                op("v", "tt", (T.y[:, d], src[:, d], T[k][:, 0:n], A.mult), pk + keys(name, x, y), keys("y", x, y), n)
+        for x, y in [] if scalar else units(a, b, 48):
             op("v", "tt", (dst[:, 16 * x:16 * y], T.ea[:, 0:V].indirect(T["wu%d" % step][:, x:y]), T.y[:, 16 * x:16 * y], A.add),
-               eak + (keys("wu1", x, y) if step else ["wu0"]) + keys("y", x, y), keys(name, x, y), 16 * (y - x) * GATHER)
+               eak + (keys("wu1", x, y) if step else ["wu0"]) + keys("y", x, y), keys(dname, x, y), 16 * (y - x) * GATHER)
 
     def rounded():
         for a, b in units(0, 176):
@@ -471,14 +571,21 @@ def rank_program(g, core, T, topo):
             op("s", "act", (T.xr[:, d], T.xf[:, d], F.Copy, MAGIC), keys("xf", a, b), keys("xr", a, b), 16 * (b - a) + 100)
             op("s", "act", (T.xr[:, d], T.xr[:, d], F.Copy, -MAGIC), keys("xr", a, b), keys("xr", a, b), 16 * (b - a) + 100)
 
+    def ways_home(q, p):
+        return [way if p < len(LAST) - 1 or len(way) < 2 else [] for way in lay[q][2]]
+
     def home(p, a, b):
         d, k = slice(16 * a, 16 * b), keys("xf", a, b)
         od, to, key = T["od%d" % p], T["or%d" % p], ["od%d" % p]
         vts(T.xf[:, d], T.xi[:, d], 0.0, float(TOP), (A.max, A.min), keys("xi", a, b), k, 16 * (b - a))
         dma("y", [(od[:], T.xf[:, d])], "dod%d" % p, k, key, 8192 * (b - a))
         dma("y", [(T.yx[lo:hi, d], T.xf[lo:hi, d])], "dy", k + key, [], 0)
-        halves(lambda q: od[2 * q], lambda q: od[2 * q + 1], to[2 * rank], to[2 * rank + 1], "of%d" % p, "on%d" % p,
-               T["ro%d" % p], "ri%d" % p, key, key)
+        via = ways_home(rank, p)
+        one = [1 << e for e in (off[0::2] + rest[0::2] + off[1::2] + rest[1::2] if via[1] else off + rest)]
+        moves = [(via[h][0], od[2 * q + h], T["ro%d" % p][k], "ri%d" % p) if via[h] else
+                 (T.cores[q], od[2 * q + h], to[2 * rank + h], "of%d" % p) for h in range(2) for k, q in enumerate(far)]
+        moves += [(T.cores[q], od[2 * q + h], to[2 * rank + h], "on%d" % p) for q in near for h in range(2)]
+        send([(c, m, x, y, s) for m, (c, x, y, s) in zip(one, moves)], key, "ri%d" % p, 1)
 
     def cursors():
         vts(T.cfin[:], T.cur[:], 1.0 / U, 3.0, (A.mult, A.min), curk, ["cfin"], 176)
@@ -488,31 +595,30 @@ def rank_program(g, core, T, topo):
 
     prepare(0)
     for c in range(NC):
-        look(0, c, 0, "s")
-        look(0, c, 1, "v")
+        for m in range(2):
+            look(0, c, m, LOOK0.split()[c][m])
         mask(c, False)
-    olk = ["ol%d" % c for c in range(NC)]
+    olk = ["ol%d" % c for c in range(NC)] + ["olt"]
     dma("s", [(T.l0d[:], T.ol[:])], "dlb", olk, ["l0d"], 130e3)
     send(to_all(T.l0d, T.l0r, "l0a"), ["l0d"], "l0a")
-    send(to_all(T.lrd, T.lrr, "lra"), ["lrd"], "lra")
-    arrives("pxn", 4 * nn, "pxrn", "rbi.n", 2 * HOP)
-    dma("y", [(T.xi[16 * a:16 * b, RH * h:RH * h + RH], T.pxr[8 * h + a:8 * h + b]) for h in (0, 1) for a, b in nears],
-        "dxn", ["pxrn", "l1d"], ["xi.n"], 540e3)
-    for h in range(2):
-        for k, q in enumerate(far):
-            arrives("px%d%d" % (h, q), 2, "pxr%d%d" % (h, q), "rbi.f", 3 + (1 + h) * HOP + (k + 1) * 90e3 * FAR)
-            dma("y", [(T.xi[16 * q:16 * q + 16, RH * h:RH * h + RH], T.pxr[8 * h + q])], ("dxa", "dxb")[h],
-                ["pxr%d%d" % (h, q), "l1d"], ["xi.f%d%d" % (h, q)], 90e3)
-    arrives("l0a", 14, "l0r", "l0a", 2 * HOP)
-    land("s", T.om, T.l0r, T.ol, "dl0", ["l0r", "lrd"] + olk, "om", 130e3)
-    arrives("lra", 14, "lrr", "lra", 2 * HOP)
-    land("s", T.llr, T.lrr, T.lsr, "dlq", ["lrr"] + lsrk, "llr", 180e3)
-    for h in range(2):
-        op("v", "copy", (T.xf[:, RH * h:RH * h + RH], T.xi[:, RH * h:RH * h + RH]),
-           ["xi.own", "xi.n"] + ["xi.f%d%d" % (h, q) for q in far], keys("xf", 80 * h, 80 * h + 96), RH)
-    vts(T.oh[:], T.om[:], float(R), None, (A.min,), ["om"], ["oh%d" % c for c in range(NC)], 256)
-    send(to_all(T.l1d, T.l1r, "l1a"), ["l1d", "xf10"], "l1a")
-    arrives("l1a", 14, "l1r", "l1a", 5 * HOP)
+    arrives("pxn", 4 * nn, "pxrn", "pxn", 2 * HOP)
+    dma("y", [(T.xi[16 * a:16 * b, RH * h:RH * h + RH], T.pnr[8 * h + a:8 * h + b]) for h in (0, 1) for a, b in nears],
+        "dxn", ["pxrn", "w"], ["xi.n"], 540e3)
+    for k in (0, 2, 1, 3):
+        for q in far:
+            straight = k % 2 and not lay[q][2][0]
+            arrives("px%d%d" % (k, q), 1, "pxr%d%d" % (k, q), "pxf%d" % (k % 2),
+                    (5 if straight else 2 + k % 2 + 2 * len(lay[q][2][k // 2])) * HOP)
+            dma("y", [(T.xi[16 * q:16 * q + 16, RQ * k:RQ * k + RQ], T.pxr[8 * k + q])], "dx%d" % k,
+                ["pxr%d%d" % (k, q), "w"], ["xi.f%d%d" % (k, q)], 45e3)
+    arrives("l0a", 14, "l0r", "l0a", HOP + 1)
+    land("s", T.om, T.l0r, T.ol, "dl0", ["l0r"] + olk, "om", 130e3)
+    later_lists(1, ["pxr3%d" % q for q in far])
+    later_lists(2, ["om"] + ["xi.f3%d" % q for q in far])
+    for k in (0, 2, 1, 3):
+        op("v", "copy", (T.xf[:, RQ * k:RQ * k + RQ], T.xi[:, RQ * k:RQ * k + RQ]),
+           ["xi.own", "xi.n"] + ["xi.f%d%d" % (k, q) for q in far], keys("xf", 44 * k, 44 * k + 59), RQ)
+    vts(T.oh[:], T.om[:, 0:512], float(R), None, (A.min,), ["om"], ["oh%d" % c for c in range(NC)], 256)
     thresholds()
     for t in range(3):
         for c in range(NC):
@@ -521,32 +627,36 @@ def rank_program(g, core, T, topo):
                     look(t, c, m, LOOKS.split()[c][m])
                 mask(c)
             see(t, c)
-        for c in range(NC):
-            carve(c)
-        if t == 0:
-            land("y", T.ll1, T.l1r, T.ls1, "dl1", ["l1r", "z31"] + ls1k, "ll1", 520e3)
-        else:
+        if t:
+            places(t)
             rounded()
-        places(t)
+        for c in range(NC):
+            carve(t, c)
+        if not t:
+            rays()
+            places(t)
         if t < 2:
+            lists_land(t + 2, "ea%d" % (NC - 2))
             prepare(t + 1)
             for step in range(2):
                 for p, (a, b) in enumerate(PIECES):
                     flags(t, step, p, a, b)
-                    move(t, step, a, b)
+                    move(t, step, a, b, (step, p) in GATHERS)
             row_of_w()
+        if t == 0:
+            later_lists(3, ["w"])
     for p, (a, b) in enumerate(LAST):
         for step in range(2):
             flags(2, step, p, a, b)
-            move(2, step, a, b)
+            move(2, step, a, b, step == 1 and p in LASTG)
         if p == len(LAST) - 1:
             cursors()
         home(p, a, b)
     for p, (a, b) in enumerate(LAST):
         src, d = T["or%d" % p], slice(16 * a, 16 * b)
-        arrives("on%d" % p, 4 * nn, "orn%d" % p, "ri%d.n" % p, HOP)
+        arrives("on%d" % p, 2 * nn, "orn%d" % p, "ri%d" % p, HOP)
         dma("s", [(T.yx[16 * x:16 * y, d], src[2 * x:2 * y]) for x, y in nears], "dz", ["orn%d" % p, "sg110"], [], 0)
-        arrives("of%d" % p, 4 * nf, "orf%d" % p, "ri%d.f" % p, 2 * HOP + ISSUE + 2048 * (b - a) * FAR)
+        arrives("of%d" % p, 2 * nf, "orf%d" % p, "ri%d" % p, 3 * HOP)
         dma("s", [(T.yx[16 * fa:16 * fb, d], src[2 * fa:2 * fb])], "dz", ["orf%d" % p, "sg110"], [], 0)
     arrives("ca", 14, "cr", "ca", HOP + 1)
     dma("s", [(T.yc[16 * x:16 * y, :], T.cr[x:y]) for x, y in others], "dz", ["cr", "sg110"], [], 0)

from concourse.bass import DstId, RemoteDMATransfer
from concourse.mybir import dt, AluOpType, AxisListType, ActivationFunctionType

A = AluOpType
F = ActivationFunctionType
R, V, TOP, BIG = 2816, 4096, 2 ** 20 - 1, 2 ** 22
RH, RQ, CORES = R // 2, R // 4, 64
U = 4096.0
MAGIC = 1.5 * 2 ** 23
CHUNKS = ((0, 2), (2, 2), (4, 2), (6, 1), (7, 1))
SPREAD = ("dram", "dram", "dma", "pe", "pe")
PIECES = ((0, 64), (64, 128), (128, 176))
LAST = ((0, 48), (48, 96), (96, 144), (144, 176))
LOOK0 = "sv ss sv sv sv"
LOOKS = "ss ss vs ss ss"
FIRST = ("ssssv", "vsssv")
ROUND = ("vvvvv", "vvvvv")
GATHERS = ((1, 1), (1, 2))
FLAGS = ((0, 0),)
LASTG = (0, 1, 2)
CYCLE, GATHER, CALL, LAG, DMA, ISSUE, HOP, NEAR, FAR = 0.83e-3, 1.6, 0.02, 0.22, 1.8, 1.2, 3.0, 1 / 400e3, 1 / 40e3
PASSES = 1
NC = len(CHUNKS)
f32, i32, u16, b16 = "float32", "int32", "uint16", "bfloat16"
SCRATCH = {n: ("sbuf", [128] + list(sh), d) for n, sh, d in (
    ("sta", (4, 2, 64), i32), ("stb", (8, 2, 64), i32), ("stc", (512,), i32), ("std", (512,), f32), ("str", (704,), i32),
    ("ste", (528,), f32), ("sth", (1,), i32), ("sth2", (2,), i32), ("ls0", (512,), u16), ("ls1", (704,), u16),
    ("ls2", (1024,), u16), ("ls3", (1024,), u16), ("ll1", (704,), u16), ("ll2", (1024,), u16), ("ll3", (1024,), u16),
    ("om", (520,), u16), ("st0", (176,), i32),
    ("ia", (144,), i32), ("ib", (128,), i32), ("ic", (2, 128), i32), ("id", (2, 128), i32), ("ig", (128,), i32),
    ("ie", (128,), i32), ("ip", (8,), i32), ("iq", (8,), i32), ("iv", (64,), i32), ("col", (12,), f32),
    ("es", (8, 128), f32), ("dk", (144,), b16), ("sp", (128,), b16), ("sq", (128,), b16), ("ob", (128,), b16),
    ("ni", (128,), b16), ("ki", (128,), b16), ("tri", (2, 128), f32), ("trj", (128,), f32), ("sel", (2, 128), f32),
    ("ones", (128,), b16), ("vp", (64,), b16), ("nth", (8,), f32), ("thf", (4,), f32), ("thc", (8,), f32), ("mk", (8,), f32),
    ("xi", (R,), i32), ("xf", (R + 8,), f32), ("xr", (R,), f32), ("y", (R,), f32), ("w", (R,), f32), ("wf", (176,), f32),
    ("wu0", (176,), u16), ("wu1", (176,), u16), ("cur", (176,), f32), ("dl", (528,), f32), ("q1", (176,), f32),
    ("q2", (176,), f32), ("pr", (352,), f32), ("cfin", (176,), f32),
    ("cf", (512,), f32), ("wg0", (1024,), b16), ("wg1", (1024,), b16), ("wg2", (1024,), b16), ("sm", (256,), f32),
    ("oh", (512,), u16), ("ol", (520,), u16), ("za0", (1024,), f32), ("za1", (1024,), f32), ("zb0", (1024,), f32),
    ("zb1", (1024,), f32), ("hl0", (2048,), f32), ("hl1", (2048,), f32), ("zz", (8, 1024), f32), ("lc", (512,), i32),
    ("lf", (512,), f32), ("fe", (512,), f32), ("far", (512,), b16), ("sgn", (512,), b16), ("acc", (8,), f32),
    ("cum", (512,), b16), ("et", (512,), f32), ("ea", (V,), f32), ("sg0", (R,), b16), ("sg1", (R,), b16))}
SCRATCH.update({n: ("dram", list(sh), d) for n, sh, d in (
    ("l0d", (8, 128, 65), u16), ("l0r", (8, 128, 65), u16), ("l1d", (8, 128, 88), u16), ("l1r", (8, 128, 88), u16),
    ("l1v", (4, 128, 88), u16), ("l2v", (4, 128, 128), u16), ("l2d", (8, 128, 128), u16), ("l2r", (8, 128, 128), u16),
    ("l3v", (4, 128, 128), u16), ("l3d", (8, 128, 128), u16), ("l3r", (8, 128, 128), u16),
    ("pxd", (32, 128, 88), i32), ("pxr", (32, 128, 88), i32), ("rb0", (4, 128, 88), i32), ("rb1", (4, 128, 88), i32),
    ("pnd", (16, 128, 176), i32), ("pnr", (16, 128, 176), i32), ("cd", (8, 128, 22), f32),
    ("cr", (8, 128, 22), f32), ("etd", (NC, 128, 128), f32))})
for _p, (_a, _b) in enumerate(LAST):
    SCRATCH.update({n + str(_p): ("dram", [k, 128, _b - _a], f32) for n, k in (("ro", 4), ("od", 16), ("or", 16))})
BANKS = ("pa0", "pa1", "pa2", "pd", "pb0", "pb1", "pc0", "pc1")
SCRATCH.update({n: ("psum", [128, 512], f32) for n in BANKS})
SEMAPHORES = (["v", "s", "t", "gc", "lsem", "l0a", "l1a", "l2a", "l3a", "l1i", "l2i", "l3i", "ca", "rb0", "rb1", "rlo", "pxn"]
              + ["px%d%d" % (k, q) for k in range(4) for q in range(8)] + ["dx%d" % k for k in range(4)]
              + [n + str(p) for n in ("ri", "on", "of", "dod") for p in range(len(LAST))]
              + [n + str(c) for n in ("rg", "ed", "ea") for c in range(NC)]
              + ["rk", "dst", "dsr", "dst1", "dl0", "dl1", "dl2", "dl3", "dpx0", "dpx1", "dpy", "dlb", "dlc1", "dlc2", "dlc3",
                 "dxn", "dcd", "dy", "dz", "dw"])


def layout(T, topo):
    lay = []
    for r, c in enumerate(T.cores):
        mine = [q for q, d in enumerate(T.cores) if topo.chip(d) == topo.chip(c)]
        far = [q for q in range(len(T.cores)) if q not in mine]
        goal = T.cores[far[0]]
        gates = [d for d in range(CORES) if topo.mates(topo.chip(d), topo.chip(goal)) and topo.may_write(d, goal)]
        out = topo.may_write(c, gates[0])
        k = [q for q in mine if topo.may_write(T.cores[q], gates[0]) == out].index(r)
        other = [d for d in topo.cores_of(c) if topo.die(d) != topo.die(c) and topo.may_write(d, gates[0]) != out][k]
        gate = [d for d in gates if topo.die(d) == topo.die(c if out else other)][k]
        lay.append(([q for q in mine if q != r], far, ([gate], [other]) if out else ([], [other, gate])))
    return lay


def two(engines, n):
    return [(1 << engines[2 * k]) | (1 << engines[2 * k + 1]) for k in range(n)]


def transfer(topo, dst, mask, src, out, sem):
    rid, pid, _ = topo.addr(dst)
    return RemoteDMATransfer(dst_ids=[DstId(rid=rid, pnc=pid)], dma_engine_mask=mask, remote_sem=sem, src=src, dst=out)


def relay_program(g, core, T, topo, r, far, h, way):
    ahead = way[way.index(core) + 1:]
    engines = topo.engines(core, (ahead or [T.cores[far[0]]])[0])
    n = len(far)
    short = len(way) < 2
    jobs = [("rb%d" % s, n, T["rb%d" % s], T.pxr[8 * (2 * h + s) + r], "px%d%d" % (2 * h + s, r)) for s in range(1 + short)]
    jobs += [("l%di" % t, 2 * n if core == way[0] else n, T["l%dv" % t], T["l%dr" % t][r], "l%da" % t) for t in (1, 2, 3) if h]
    jobs += [("ri%d" % p, n, T["ro%d" % p], T["or%d" % p][2 * r + h], "of%d" % p) for p in range(len(LAST) - 1 + short)]
    for i, (s, count, src, dst, to) in enumerate(jobs):
        masks = [1 << e for e in engines[i % 2::2]]
        g.wait_ge(T.sem[s], count)
        g.remote_dma_fused([transfer(topo, ahead[0], masks[k], src[k], src[k], T.sem[s]) if ahead else
                            transfer(topo, T.cores[q], masks[k], src[k], dst, T.sem[to]) for k, q in enumerate(far)],
                           local_sem=T.sem.rlo)
    g.wait_ge(T.sem.rlo, len(jobs) * n)


def order_of_issue(prog):
    n = len(prog)
    succ, pred, wr, rd = [[] for _ in prog], [], {}, {}
    for i, (q, reads, writes, busy, total) in enumerate(prog):
        pred.append(sorted({wr[k] for k in reads + writes if k in wr} | {j for k in writes for j in rd.get(k, ())}))
        for j in pred[i]:
            succ[j].append(i)
        for k in reads:
            rd.setdefault(k, []).append(i)
        for k in writes:
            wr[k], rd[k] = i, []
    banks = [{k.split(".")[0] for k in p[1] + p[2]} & set(BANKS) for p in prog]

    def lay_out(before, after, way, back):
        left = [len(x) for x in before]
        ready, ends, free, held, pool, out = [0.0] * n, [0.0] * n, {}, {}, [i for i in range(n) if not left[i]], []
        lead = [p[4] - p[3] if back else 0.0 for p in prog]
        while pool:
            start = {i: max([ready[i] + lead[i], free.get(prog[i][0], 0.0)]
                            + [t for b in banks[i] for q, t in held.get(b, {}).items() if q != prog[i][0]]) for i in pool}
            first = min(pool, key=lambda i: start[i] + prog[i][3])
            q = prog[first][0]
            i = max((j for j in pool if prog[j][0] == q and start[j] <= start[first] + prog[first][3]), key=lambda j: way[j])
            pool.remove(i)
            out.append(i)
            if q:
                free[q] = start[i] + prog[i][3]
            ends[i] = start[i] + prog[i][4] - lead[i] + LAG
            for b in banks[i]:
                held.setdefault(b, {})[q] = ends[i]
            for j in after[i]:
                ready[j] = max(ready[j], ends[i])
                left[j] -= 1
                if not left[j]:
                    pool.append(j)
        return out, ends

    way = [0.0] * n
    for i in reversed(range(n)):
        way[i] = prog[i][4] + LAG + max([way[j] for j in succ[i]], default=0.0)
    best = lay_out(pred, succ, way, False)
    last = best
    for _ in range(PASSES):
        last = lay_out(pred, succ, lay_out(succ, pred, last[1], True)[1], False)
        best = min(best, last, key=lambda x: max(x[1]))
    return best[0]


def rank_program(g, core, T, topo):
    lay = layout(T, topo)
    rank = T.rank_of(core)
    if rank is None:
        for r, (near, far, ways) in enumerate(lay):
            for h, way in enumerate(ways):
                if core in way:
                    relay_program(g, core, T, topo, r, far, h, way)
        return
    near, far, ways = lay[rank]
    sem = T.sem
    queue = {"v": g.vector, "s": g.scalar, "t": g.tensor, "y": g.sync, "g": g}
    own = {"v": "v", "s": "s", "t": "t", "g": "gc"}
    cnt, seen, wr, rd, bank, prog, issue = {}, {}, {}, {}, {}, [], []

    def waits(q, deps):
        need = {}
        for s, n in deps:
            need[s] = max(need.get(s, 0), n)
        for s in need:
            if seen.get((q, s), 0) < need[s]:
                queue[q].wait_ge(sem[s], need[s])
                seen[(q, s)] = need[s]

    def deps_of(q, reads, writes):
        d = []
        for k in reads + writes:
            d += wr.get(k, [])
            d += [(s, n) for s, n in bank.get(k.split(".")[0], {}).items() if s != own.get(q)]
        for k in writes:
            d += rd.get(k, {}).items()
        return d

    def done(tag, reads, writes):
        for k in reads:
            rd.setdefault(k, {})[tag[0]] = tag[1]
        for k in writes:
            wr[k] = [tag] * (k != "sent")
            rd[k] = {}
        for k in reads + writes:
            if k.split(".")[0] in BANKS:
                bank.setdefault(k.split(".")[0], {})[tag[0]] = tag[1]

    calls = {"mm": g.tensor.matmul, "acts": g.scalar.activation, "act": g.scalar.activation, "iota": g.iota,
             "copy": g.vector.tensor_copy, "tt": g.vector.tensor_tensor, "ts": g.vector.tensor_scalar, "set": g.vector.memset,
             "tss": g.vector.tensor_scalar, "scan": g.vector.tensor_tensor_scan}

    def note(q, reads, writes, busy, total, f):
        prog.append((q, list(reads), list(writes), busy, total))
        issue.append(f)

    def op(q, name, args, reads, writes, n=64, **kw):
        def f():
            waits(q, deps_of(q, reads, writes))
            s = own[q]
            for a in args if name in ("mm", "acts", "tss") else [args]:
                ins = calls[name](*a, **kw)
            cnt[s] = cnt.get(s, 0) + 1
            ins.then_inc(sem[s], 1)
            done((s, cnt[s]), reads, writes)
        note(q, reads, writes, CALL + n * CYCLE, CALL + n * CYCLE, f)

    def vts(out, in0, s1, s2, ops, reads, writes, n=64):
        op("v", "ts", (out, in0, s1, s2) + ops, reads, writes, n)

    def dma(q, pairs, s, reads, writes, nbytes):
        def f():
            waits(q, deps_of(q, reads, writes))
            for o, i in pairs:
                queue[q].dma_start(o, i).then_inc(sem[s], 16)
            cnt[s] = cnt.get(s, 0) + 16 * len(pairs)
            done((s, cnt[s]), reads, writes)
        note(q, reads, writes, 0.06 * len(pairs), DMA + 0.06 * len(pairs) + nbytes * NEAR, f)

    def arrives(s, n, key, like, time):
        def f():
            cnt[s] = cnt.get(s, 0) + n
            wr[key] = [(s, cnt[s])]
        note(None, [like], [key], 0.0, time, f)

    nf, nn = len(far), len(near)
    off = topo.engines(core, T.cores[far[0]])
    rest = [e for e in topo.engines(core, T.cores[near[0]]) if e not in off]

    def send(moves, reads, name, engines=2):
        def f():
            waits("g", deps_of("g", reads, []))
            g.remote_dma_fused([transfer(topo, d, m, a, b, sem[s]) for d, m, a, b, s in moves], local_sem=sem.lsem)
            cnt["lsem"] = cnt.get("lsem", 0) + engines * len(moves)
        note("g", reads, [name, "sent"], ISSUE, ISSUE, f)

    def to_far(src, dst, s):
        return [(T.cores[q], m, src(q), dst, s) for q, m in zip(far, two(off, nf))]

    def to_relay(src, via, vsem):
        return [(ways[1][0], m, src(q), via[k], vsem) for k, (q, m) in enumerate(zip(far, two(rest, nf)))]

    def to_near(src, dst, s, engines):
        return [(T.cores[q], m, src(q), dst, s) for q, m in zip(near, two(engines, nn))]

    def to_all(src, dst, s):
        return to_far(lambda q: src[q], dst[rank], s) + to_near(lambda q: src[q], dst[rank], s, rest)

    lo, hi = 16 * rank, 16 * rank + 16
    others = [(a, b) for a, b in ((0, rank), (rank + 1, 8)) if b > a]
    fa, fb = far[0], far[-1] + 1
    na, nb = min(near + [rank]), max(near + [rank]) + 1
    nears = [(a, b) for a, b in ((na, rank), (rank + 1, nb)) if b > a]

    def land(q, dst, src, mine, s, reads, key, nbytes):
        dma(q, [(dst[16 * a:16 * b, :], src[a:b]) for a, b in others] + [(dst[lo:hi, :], mine[lo:hi, :])], s, reads, [key], nbytes)

    def keys(name, a, b):
        return ["%s%d" % (name, k) for k in range(a // 16, b // 16)]

    def candidates(st, k, t):
        wide = sum(n == 2 for o, n in CHUNKS)
        pairs = []
        for m in range(2):
            x = 512 * t + 256 * m
            pairs.append((st[:, k:k + wide, m, :], T.cand[:, x:x + 64 * wide]))
            pairs += [(st[:, k + o // 2, o % 2, 32 * m:32 * m + 32], T.cand[:, x + 32 * o:x + 32 * o + 32]) for o, n in CHUNKS[wide:]]
        return pairs

    wfk, curk, xfk = keys("wf", 0, 176), keys("cur", 0, 176), keys("xf", 0, 176) + ["xfs"]
    pdk = ["pd.%d" % j for j in range(4)]
    lsk = {1: ["lsr.r", "lsr.d"], 2: ["ls2.n", "ls2.p"], 3: ["ls3.n", "ls3.p"]}
    col, dl = T.col, T.dl

    dma("s", [(T.st0[:], T.ray[:, 0:176])], "dsr", [], ["st0"], 0)
    dma("s", candidates(T.sta, 0, 0) + [(T.sth[:], T.th[:])], "dst", [], ["sta", "sth"], 0)
    for s in range(2):
        dma("y", [(T.pxd[8 * k + fa:8 * k + fb], T.px[16 * fa:16 * fb, RQ * k:RQ * k + RQ]) for k in (2 + s, s)], "dpx%d" % s, [],
            ["pxd%d" % s], 360e3 * (1 + s))
    dma("y", [(T.pnd[8 * h + a:8 * h + b], T.px[16 * a:16 * b, RH * h:RH * h + RH]) for h in (0, 1) for a, b in nears],
        "dpy", [], ["pxdn"], 540e3)
    op("v", "set", (T.w[:], 0.0), [], ["w"], R)
    op("g", "iota", (T.ip[:], [[0, 8]], 0, 1), [], ["ip", "sent"], 200)
    op("g", "iota", (T.ia[:], [[-1, 144]], 16, 1), [], ["ia", "sent"], 400)
    op("g", "iota", (T.iv[:], [[0, 2], [16, 32]], -255, 0), [], ["iv", "sent"], 300)
    op("g", "iota", (T.ib[:], [[-16, 8], [0, 16]], 0, 1), [], ["ib", "sent"], 400)
    op("g", "iota", (T.ig[:], [[0, 8], [-8, 16]], 0, 1), [], ["ig", "sent"], 400)
    for n in (1, 2):
        op("g", "iota", (T["id"][:, n - 1, :], [[-1, 16], [-16, n], [0, 8 // n]], 1024, 1), [], ["id%d" % n, "sent"], 400)
        op("g", "iota", (T.ic[:, n - 1, :], [[-8 // n, 16 * n], [0, 8 // n]], 0, 1), [], ["ic%d" % n, "sent"], 400)
    for s in range(2):
        via = [way if not s or len(way) < 2 else [] for way in ways]
        moves = [(via[h][0], T.pxd[8 * (2 * h + s) + q], T["rb%d" % s][k], "rb%d" % s) if via[h] else
                 (T.cores[q], T.pxd[8 * (2 * h + s) + q], T.pxr[8 * (2 * h + s) + rank], "px%d%d" % (2 * h + s, rank))
                 for h in range(2) for k, q in enumerate(far)]
        engines = off[s::2] + (rest[s::2] if via[1] else off[1 - s::2])
        send([(c, 1 << e, x, y, z) for e, (c, x, y, z) in zip(engines, moves)], ["pxd%d" % s], "pxf%d" % s, 1)
    send(to_near(lambda q: T.pnd[q], T.pnr[rank], "pxn", rest) + to_near(lambda q: T.pnd[8 + q], T.pnr[8 + rank], "pxn", off),
         ["pxdn"], "pxn")

    def row_of_w():
        dma("y", [(T.w[0:128:16, :], T.wf[:])], "dw", wfk, ["w"], 0)

    def numbers_to_places(src, n, out, key, okey):
        vts(T.stc[:, 0:n], src, 15, None, (A.bitwise_and,), [key], ["stc"], n)
        vts(T.pd[:, 0:n], T.stc[:, 0:n], 2815.0, None, (A.mult,), ["stc"], pdk, n)
        op("v", "tt", (T.std[:, 0:n], T.pd[:, 0:n], src, A.add), pdk + [key], ["std"], n)
        vts(out, T.std[:, 0:n], 1.0 / 16, None, (A.mult,), ["std"], [okey], n)

    vts(T.iq[:, 0:1], T.ip[:, 0:1], 15, None, (A.bitwise_and,), ["ip"], ["iq0"])
    op("v", "copy", (T.wf[:], T.st0[:]), ["st0"], wfk, 176)
    row_of_w()
    dma("y", [(T["str"][:], T.ray[:])] + candidates(T.stb, 0, 1) + candidates(T.stb, 4, 2) + [(T.xi[lo:hi, :], T.px[lo:hi, :])],
        "dst1", wfk, ["stb", "xi.own", "str"], 4e6)
    vts(col[:, 0:1], T.iq[:, 0:1], 0.0, -U, (A.is_equal, A.mult), ["iq0"], ["col0"])
    op("v", "copy", (col[:, 1:2], T.iq[:, 0:1]), ["iq0"], ["col1"])
    for h in range(2):
        numbers_to_places(T.sta[:, 2 * h:2 * h + 2], 256, T.ls0[:, 256 * h:256 * h + 256], "sta", "ls0.%d" % h)
    vts(T.dk[:], T.ia[:], 0.0, col[:, 0:1], (A.is_equal, A.mult), ["ia", "col0"], ["dk"], 144)
    vts(T.ni[:], T.ia[:, 16:144], 0.0, -0.25, (A.is_equal, A.mult), ["ia"], ["ni"], 128)
    vts(T.vp[:], T.iv[:], col[:, 1:2], -4 * U, (A.add, A.mult), ["iv", "col1"], ["vp"])
    op("v", "set", (T.ol[:, 512:520], 0), [], ["olt"])
    vts(T.sth2[:, 0:1], T.sth[:], 10, None, (A.arith_shift_right,), ["sth"], ["sth2a"])
    vts(T.sth2[:, 1:2], T.sth[:], 1023, None, (A.bitwise_and,), ["sth"], ["sth2b"])
    op("v", "tt", (T.ste[:], T["str"][:, 176:704], T["str"][:, 0:528], A.subtract), ["str"], ["ste"], 1056)
    op("v", "copy", (T.ls1[:, 0:176], T["str"][:, 0:176]), ["str"], ["lsr.r"], 176)
    op("v", "copy", (T.ol[:, 512:514], T.sth2[:]), ["sth2a", "sth2b"], ["olt"])
    vts(T.ls1[:, 176:704], T.ste[:], U, None, (A.add,), ["ste"], ["lsr.d"], 528)
    op("v", "set", (T.xf[:, R:R + 8], float(BIG)), [], ["xfs"])
    op("v", "set", (T.xf[:, R:R + 1], float(-BIG)), [], ["xfs"])
    op("v", "set", (T.cur[:], 0.0), [], curk, 176)
    op("v", "set", (T.ones[:], 1.0), [], ["ones"])
    op("v", "set", (col[:, 4:5], -8.5), [], ["col4"])
    vts(T.sp[:], T.ib[:], 0.0, -0.25, (A.is_equal, A.mult), ["ib"], ["sp"], 128)
    vts(T.sq[:], T.ib[:], 1.0, None, (A.is_equal,), ["ib"], ["sq"], 128)
    op("v", "tt", (T.sp[:], T.sp[:], T.sq[:], A.add), ["sp", "sq"], ["sp"], 256)
    vts(col[:, 2:3], T.iq[:, 0:1], 1.0, None, (A.is_equal,), ["iq0"], ["col2"])
    vts(col[:, 3:4], T.iq[:, 0:1], 1.0, None, (A.not_equal,), ["iq0"], ["col3"])
    vts(col[:, 5:6], col[:, 2:3], 2.0, -1.0, (A.mult, A.add), ["col2"], ["col5"])
    vts(T.ki[:], T.ia[:, 16:144], 0.0, 128.0, (A.is_equal, A.mult), ["ia"], ["ki"], 128)
    vts(T.ie[:], T.ia[:, 16:144], 7, None, (A.bitwise_and,), ["ia"], ["ie"], 128)
    vts(T.ob[:], T.ie[:], 0.0, None, (A.is_equal,), ["ie"], ["ob"], 128)
    vts(T.trj[:], T.ia[:, 16:144], 0.0, None, (A.is_lt,), ["ia"], ["trj"], 128)
    for n in (1, 2):
        k, ids, tri = str(n), T["id"][:, n - 1, :], T.tri[:, n - 1, :]
        vts(T.iq[:, n:n + 1], T.ip[:, 0:1], 8 // n - 1, None, (A.bitwise_and,), ["ip"], ["iq" + k])
        vts(col[:, 5 + n:6 + n], T.iq[:, n:n + 1], 16.0 * n, 64.0, (A.mult, A.add), ["iq" + k], ["lim" + k])
        vts(ids, ids, 16 * n - 1, None, (A.bitwise_and,), ["id" + k], ["id" + k], 128)
        vts(T.sel[:, n - 1, :], ids, 0.0, None, (A.is_equal,), ["id" + k], ["sel" + k], 128)
        vts(tri, T.ic[:, n - 1, :], 0.0, None, (A.is_ge,), ["ic" + k], ["tri" + k], 128)
        op("v", "tt", (tri, tri, T.trj[:], A.mult), ["tri" + k, "trj"], ["tri" + k], 256)
        vts(T.iq[:, 2 + n:3 + n], T.ip[:, 0:1], 3 + n, None, (A.arith_shift_right,), ["ip"], ["is" + k])
    for c, (o, n) in enumerate(CHUNKS):
        vts(T.mk[:, c:c + 1], T.iq[:, 2 + n:3 + n], float(o // n), None, (A.is_equal,), ["is%d" % n], ["mk%d" % c])
    for b in range(8):
        vts(T.es[:, b, :], T.ig[:], float(b), None, (A.is_equal,), ["ig"], ["es%d" % b], 128)
    for t in (2, 3):
        ls, src = T["ls%d" % t], T.stb[:, 4 * t - 8:4 * t - 4]
        op("v", "copy", (ls[:, 0:512], src), ["stb"], ["ls%d.n" % t], 512)
        numbers_to_places(src, 512, ls[:, 512:1024], "stb", "ls%d.p" % t)
    for t in (1, 2, 3):
        dma("s", [(T["l%dd" % t][:], T["ls%d" % t][:])], "dlc%d" % t, lsk[t], ["l%dd" % t], 260e3)

    def later_lists(t, after):
        n = "l%d" % t
        src = T[n + "d"]
        send(to_relay(lambda q: src[q], T[n + "v"], n + "i") + to_near(lambda q: src[q], T[n + "r"][rank], n + "a", off),
             [n + "d"] + after, n + "a")
        arrives(n + "a", 2 * nn + nf, n + "r", n + "a", 5 * HOP)

    def lists_land(t, after):
        n = "l%d" % t
        land("y", T["l" + n], T[n + "r"], T["ls%d" % t], "d" + n, [n + "r", after] + lsk[t], "l" + n, 260e3)

    def rays():
        lists_land(1, "z%d1" % (NC - 1))
        op("v", "copy", (T.wf[:], T.ll1[:, 0:176]), ["ll1"], wfk, 176)
        vts(dl[:], T.ll1[:, 176:704], -U, 1.0 / U, (A.add, A.mult), ["ll1"], ["dl"], 528)

    def thresholds():
        op("v", "copy", (T.thf[:, 0:2], T.om[:, 512:514]), ["om"], ["thf"])
        vts(T.thf[:, 2:3], T.thf[:, 0:1], 1024.0, T.thf[:, 1:2], (A.mult, A.add), ["thf"], ["thf2"])
        vts(T.thc[:, 0:NC], T.mk[:, 0:NC], T.thf[:, 2:3], None, (A.mult,), ["mk%d" % c for c in range(NC)] + ["thf2"], ["thc"])
        op("t", "mm", [(T.pd[:, c:c + 1], T.sel[:, n - 1, :], T.thc[:, c:c + 1], True, True) for c, (o, n) in enumerate(CHUNKS)],
           ["sel1", "sel2", "thc"], pdk, 700)
        vts(T.nth[:, 0:NC], T.pd[:, 0:NC], -1.0, -0.5, (A.mult, A.add), pdk, ["nth"])

    def prepare(t):
        src, key = (T.sta[:], "sta") if t == 0 else (T["ll%d" % (t + 1)][:, 0:512], "ll%d" % (t + 1))
        op("v", "copy", (T.cf[:], src), [key], ["cf"], 512)

    turn = {"s": 0}

    def look(t, c, m, q):
        o, n = CHUNKS[c]
        buf, base, key = (T.ls0, 0, "ls0.%d" % (o // 4)) if t == 0 else (T["ll%d" % (t + 1)], 512, "ll%d" % (t + 1))
        k = base + 64 * o + 32 * n * m
        out, ok = T["pc%d" % (c % 2)][:, 32 * n * m:32 * n * (m + 1)], "pc%d.%d" % (c % 2, m)
        turn["s"] ^= q == "s"
        e = turn["s"] if q == "s" else 2
        wg, wgk = T["wg%d" % e], "wg%d" % e
        parts = [(wg[:, 512 * b:512 * b + 512], T.w[:, 0:R].indirect(buf[:, k + 32 * b:k + 32 * b + 32]),
                  float(-255 - 512 * (o + b))) for b in range(n)]
        if q == "s":
            op("s", "acts", [(x, i, F.Copy, z) for x, i, z in parts], [key, "w"], [wgk], n * (512 * GATHER + 50))
        else:
            op("v", "tss", [(x, i, z, None, A.add) for x, i, z in parts], [key, "w"], [wgk], n * (512 * GATHER + 50))
        op("t", "mm", [(out, T.ni[:], T.vp[:, 0:32 * n], True, False)]
           + [(out, T.dk[:, 16 - i:144 - i], wg[:, i:512 * n:16], False, i == 15) for i in range(16)],
           ["dk", "ni", "vp", wgk], [ok], 700)

    def mask(c, both=True):
        (o, n), e = CHUNKS[c], c % 2
        d, s = slice(64 * o, 64 * (o + n)), slice(128 * e, 128 * e + 64 * n)
        op("v", "tt", (T.sm[:, s], T["pc%d" % e][:, 0:64 * n], T.cf[:, d], A.max), ["pc%d.0" % e, "pc%d.1" % e, "cf"],
           ["sm%d" % e], 64 * n)
        for x, ok, r in ((T.oh, "oh", R), (T.ol, "ol", R + 1))[0 if both else 1:]:
            vts(x[:, d], T.sm[:, s], float(r), None, (A.min,), ["sm%d" % e], ["%s%d" % (ok, c)], 64 * n)

    def side(c, j, n, x=0):
        return slice(x + n * j, x + n * j + n) if c == NC - 1 else slice(x + j, x + 2 * n, 2)

    def see(t, c):
        (o, n), e = CHUNKS[c], c % 2
        hl, nv, k = T["hl%d" % e], 512 * n, 64 * o
        for j, (x, ok), z, f in zip((0, 1), ((T.oh, "oh%d" % c), (T.om, "om") if t == 0 else (T.ol, "ol%d" % c)),
                                    ("za%d" % e, "zb%d" % e), (A.max, A.min)):
            d = side(c, j, nv)
            op("s", "act", (T[z][:, 0:nv], T.xf[:, 0:R + 8].indirect(x[:, k:k + 32 * n]), F.Copy), [ok] + xfk, [z], nv * GATHER)
            op("v", "tt", (hl[:, d], T.xf[:, 0:R + 8].indirect(x[:, k + 32 * n:k + 64 * n]), T[z][:, 0:nv], f), [ok, z] + xfk,
               ["hl%d%d" % (e, j)], nv * GATHER)
            if c == NC - 1:
                dma("y", [(T.zz[:, a, side(c, j, 64 * n, 2 * k)], hl[16 * a:16 * a + 16, d]) for a in range(8)],
                    ("rg%d" % c, "rk")[j], ["hl%d%d" % (e, j)], ["z%d%d" % (c, j)], 512 * nv)
        if c < NC - 1:
            dma("y", [(T.zz[:, a, 2 * k:2 * k + 128 * n], hl[16 * a:16 * a + 16, 0:2 * nv]) for a in range(8)], "rg%d" % c,
                ["hl%d0" % e, "hl%d1" % e], ["z%d0" % c, "z%d1" % c], 1024 * nv)

    def carve(t, c):
        o, n = CHUNKS[c]
        wd, k, b = 64 * n, str(c), BANKS[c] + ".c"[:1 + c // 4]
        d, ps = slice(64 * o, 64 * o + wd), [T[BANKS[c]][:, 128 * j:128 * j + wd] for j in range(4)]
        shared = [BANKS[c] + ".%d" % j for j in range(3 * (c // 4))]
        for a in range(1, 8):
            for j, f in ((0, A.max), (1, A.min)):
                key, z, x = b + str(j), "z%d%d" % (c, j), side(c, j, wd, 128 * o)
                if a == 1 and FIRST[t > 0][c] == "v":
                    op("v", "tt", (ps[j], T.zz[:, 0, x], T.zz[:, 1, x], f), [z] + shared * j, [key] + shared * (1 - j), 2 * wd)
                else:
                    if a == 1:
                        op("s", "act", (ps[j], T.zz[:, 0, x], F.Copy), [z], [key], wd + 80)
                    op("v", "tt", (ps[j], ps[j], T.zz[:, a, x], f), [z, key], [key], wd)
        fe, lk, fk = T.fe[:, d], ["lc" + k], ["fe" + k]
        if ROUND[t > 0][c] == "v":
            low = T.lc[:, d]
            vts(low, ps[1], 0.0, float(TOP), (A.max, A.min), [b + "1"], lk, wd)
            vts(fe, low, -0.25, -0.375, (A.mult, A.add), lk, fk, wd)
        else:
            low = T.lf[:, d]
            op("s", "act", (low, ps[1], F.Copy, MAGIC), [b + "1"], lk, wd + 80)
            op("s", "act", (low, low, F.Relu, -MAGIC), lk, lk, wd + 80)
            op("s", "act", (fe, low, F.Relu, float(TOP), -1.0), lk, fk, wd + 80)
            op("s", "act", (fe, fe, F.Copy, -TOP / 4 - 0.375, 0.25), fk, fk, wd + 80)
        vts(ps[0], ps[0], float(TOP), T.nth[:, c:c + 1], (A.min, A.add), [b + "0", "nth"], [b + "0"], wd)
        op("v", "tt", (T.far[:, d], ps[0], low, A.is_gt), [b + "0"] + lk, ["far" + k], wd)
        op("t", "mm", [(ps[2], T.ob[:], T.far[:, d], True, True)], ["ob", "far" + k], [b + "2"], 100)
        op("s", "act", (T.sgn[:, d], ps[2], F.Sign, col[:, 4:5]), [b + "2", "col4"], ["sgn" + k, "acc" + k], wd + 120,
           accum_out=T.acc[:, c:c + 1])
        start = T[BANKS[c]][:, 256:257]
        op("t", "mm", [(start, T.tri[:, n - 1, :], T.acc[:, c:c + 1], True, True)], ["tri%d" % n, "acc" + k], [b + "2"], 150)
        op("v", "scan", (T.cum[:, d], T.sgn[:, d], T.ones[:, 0:wd], start, A.add, A.add), ["sgn" + k, "ones", b + "2"],
           ["cum" + k], wd)
        op("t", "mm", [(ps[3], T.ni[:], T.cum[:, d], True, False), (ps[3], T.ki[:], T.sgn[:, d], False, True)],
           ["ni", "ki", "cum" + k, "sgn" + k], [b + "3"], 200)
        et, ek, x = T.et[:, d], "et" + k, 512 * o
        vts(ps[3], ps[3], col[:, 5 + n:6 + n], None, (A.is_ge,), [b + "3", "lim%d" % n], [b + "3"], wd)
        op("v", "tt", (et, ps[3], fe, A.mult), [b + "3"] + fk + shared, [ek], wd)
        if SPREAD[c] == "pe":
            for h in range(2):
                pc, pk = T["pc%d" % h], ["pc%d.%d" % (h, j) for j in range(3)]
                op("t", "mm", [(pc[:, wd * s:wd * s + wd], T.es[:, 4 * h + s, :], et, True, True) for s in range(4)],
                   ["es%d" % j for j in range(8)] + [ek], pk, 550 * n)
                op("s", "act", (T.ea[:, x + 4 * wd * h:x + 4 * wd * (h + 1)], pc[:, 0:4 * wd], F.Copy), pk, ["ea" + k + "h" * h],
                   4 * wd + 80)
            return
        if SPREAD[c] == "dram":
            dma("y", [(T.etd[c], et)], "ed" + k, [ek], ["etd" + k], 65e3)
            et, ek = T.etd[c], "etd" + k
        dma("y", [(T.ea[16 * a:16 * a + 16, x:x + 512 * n], et) for a in range(8)], "ea" + k, [ek], ["ea" + k, "ea" + k + "h"],
            260e3 * n)

    eak = ["ea%d" % c + "h" * h for c in range(NC) for h in range(2)]

    def places(t):
        op("v", "copy", (T.wu0[:], T.wf[:]), wfk, ["wu0"], 176)
        if t == 0:
            return
        eq = (T.pc0[:, 128:304], T.pc0[:, 304:480], T.pc1[:, 128:304], T.pc1[:, 304:480])
        ek, d, pr = ("pc0.2", "pc0.2", "pc1.2"), [dl[:, 176 * k:176 * k + 176] for k in range(3)], (T.pr[:, 0:176], T.pr[:, 176:352])
        op("v", "tss", [(eq[k], T.cur[:], U * k, None, A.is_equal) for k in range(3)], curk, ["pc0.2", "pc1.2"], 600)
        if t == 1:
            op("v", "tt", (pr[0], eq[0], d[1], A.mult), [ek[0], "dl"], ["pr0"], 176)
            op("v", "tt", (eq[3], eq[1], d[2], A.mult), [ek[1], "dl"], [ek[2]], 176)
            op("v", "tt", (T.q2[:], eq[3], pr[0], A.add), [ek[2], "pr0"], ["q2"], 176)
        op("v", "tt", (pr[0], eq[0], d[0], A.mult), [ek[0], "dl"], ["pr0"], 176)
        op("v", "tt", (eq[1], eq[1], d[1], A.mult), [ek[1], "dl"], [ek[1]], 176)
        op("v", "tt", (eq[2], eq[2], d[2], A.mult), [ek[2], "dl"], [ek[2]], 176)
        op("v", "tt", (pr[1], eq[1], pr[0], A.add), [ek[1], "pr0"], ["pr1"], 176)
        op("v", "tt", (T.q1[:], eq[2], pr[1], A.add), [ek[2], "pr1"], ["q1"], 176)

    def units(a, b, most=32):
        n = (b - a + most - 1) // most
        cut = [a + 16 * ((b - a) // 16 * k // n) for k in range(n + 1)]
        return list(zip(cut, cut[1:]))

    rot = [0]

    def flags(t, step, p, a, b):
        sg, sk = T["sg%d" % step], "sg%d" % step
        for x, y in units(a, b):
            out, src = sg[:, 16 * x:16 * y], T.ea[:, 0:V].indirect(T["wu%d" % step][:, x:y])
            reads, n = eak + (keys("wu1", x, y) if step else ["wu0"]) + ["col2", "col3", "col5"], 16 * (y - x) * GATHER + 30
            if (step, p) in FLAGS and x == a:
                vts(out, src, col[:, 2:3], col[:, 5:6], (A.is_lt, A.mult), reads, keys(sk, x, y), n)
            else:
                op("s", "act", (out, src, F.Sign, col[:, 2:3], col[:, 3:4]), reads, keys(sk, x, y), n)
        pb, key, tk = T["pb%d" % (p % 2)], "pb%d.%d" % (p % 2, step), "pb%d.2" % (p % 2)
        ps, tq = pb[:, 176 * step + a:176 * step + b], pb[:, 352:352 + b - a]
        op("t", "mm", [(ps, T.dk[:, 16 - k:144 - k], sg[:, 16 * a + k:16 * b:16], k == 0, k == 15) for k in range(16)],
           ["dk"] + keys(sk, a, b), [key], 8 * max(64, b - a) + 100)
        if t == 0:
            q, qk = dl[:, 176 * step + a:176 * step + b], "dl"
        else:
            q, qk = (T.q1[:, a:b], "q1") if step == 0 else (T.q2[:, a:b], "q2")
        wfp, cp = keys("wf", a, b), keys("cur", a, b)
        if step == 0 or t < 2:
            op("v", "tt", (tq, ps, q, A.mult), [key, qk], [tk], b - a)
            op("v", "tt", (T.wf[:, a:b], tq, T.wf[:, a:b], A.add), wfp + [tk], wfp, b - a)
        if step == 0:
            op("v", "copy", (T.wu1[:, a:b], T.wf[:, a:b]), wfp, keys("wu1", a, b), b - a)
        op("v", "tt", (T.cur[:, a:b], ps, T.cur[:, a:b], A.add), [key] + cp, cp, b - a)

    def move(t, step, a, b, scalar):
        src, name = (T.xi, "xi") if step else (T.xr, "xr") if t else (T.xf, "xf")
        dst, dname = (T.xf, "xf") if step and t < 2 else (T.xi, "xi")
        sg, sk = T["sg%d" % step], "sg%d" % step
        for x, y in units(a, b):
            k = BANKS[rot[0]]
            rot[0] = (rot[0] + 1) % 4
            pk, n, d = [k + ".%d" % j for j in range(4)], 16 * (y - x), slice(16 * x, 16 * y)
            op("t", "mm", [(T[k][:, 0:n], T.sp[:], sg[:, d], True, True)], ["sp"] + keys(sk, x, y), pk, n // 2 + 50)
            if scalar:
                op("s", "act", (T.xr[:, d], T.ea[:, 0:V].indirect(T.wu1[:, x:y]), F.Copy), eak + keys("wu1", x, y),
                   keys("xr", x, y), n * GATHER + 30)
                op("v", "tt", (T[k][:, 0:n], src[:, d], T[k][:, 0:n], A.mult), pk + keys(name, x, y), pk, n)
                op("v", "tt", (dst[:, d], T[k][:, 0:n], T.xr[:, d], A.add), pk + keys("xr", x, y), keys(dname, x, y), n)
            else:
                op("v", "tt", (T.y[:, d], src[:, d], T[k][:, 0:n], A.mult), pk + keys(name, x, y), keys("y", x, y), n)
        for x, y in [] if scalar else units(a, b, 48):
            op("v", "tt", (dst[:, 16 * x:16 * y], T.ea[:, 0:V].indirect(T["wu%d" % step][:, x:y]), T.y[:, 16 * x:16 * y], A.add),
               eak + (keys("wu1", x, y) if step else ["wu0"]) + keys("y", x, y), keys(dname, x, y), 16 * (y - x) * GATHER)

    def rounded():
        for a, b in units(0, 176):
            d = slice(16 * a, 16 * b)
            op("s", "act", (T.xr[:, d], T.xf[:, d], F.Copy, MAGIC), keys("xf", a, b), keys("xr", a, b), 16 * (b - a) + 100)
            op("s", "act", (T.xr[:, d], T.xr[:, d], F.Copy, -MAGIC), keys("xr", a, b), keys("xr", a, b), 16 * (b - a) + 100)

    def ways_home(q, p):
        return [way if p < len(LAST) - 1 or len(way) < 2 else [] for way in lay[q][2]]

    def home(p, a, b):
        d, k = slice(16 * a, 16 * b), keys("xf", a, b)
        od, to, key = T["od%d" % p], T["or%d" % p], ["od%d" % p]
        vts(T.xf[:, d], T.xi[:, d], 0.0, float(TOP), (A.max, A.min), keys("xi", a, b), k, 16 * (b - a))
        dma("y", [(od[:], T.xf[:, d])], "dod%d" % p, k, key, 8192 * (b - a))
        dma("y", [(T.yx[lo:hi, d], T.xf[lo:hi, d])], "dy", k + key, [], 0)
        via = ways_home(rank, p)
        one = [1 << e for e in (off[0::2] + rest[0::2] + off[1::2] + rest[1::2] if via[1] else off + rest)]
        moves = [(via[h][0], od[2 * q + h], T["ro%d" % p][k], "ri%d" % p) if via[h] else
                 (T.cores[q], od[2 * q + h], to[2 * rank + h], "of%d" % p) for h in range(2) for k, q in enumerate(far)]
        moves += [(T.cores[q], od[2 * q + h], to[2 * rank + h], "on%d" % p) for q in near for h in range(2)]
        send([(c, m, x, y, s) for m, (c, x, y, s) in zip(one, moves)], key, "ri%d" % p, 1)

    def cursors():
        vts(T.cfin[:], T.cur[:], 1.0 / U, 3.0, (A.mult, A.min), curk, ["cfin"], 176)
        dma("y", [(T.cd[:], T.cfin[:])], "dcd", ["cfin"], ["cd"], 0)
        dma("y", [(T.yc[lo:hi, :], T.cfin[lo:hi, :])], "dy", ["cfin", "cd"], [], 0)
        send(to_all(T.cd, T.cr, "ca"), ["cd"], "ca")

    prepare(0)
    for c in range(NC):
        for m in range(2):
            look(0, c, m, LOOK0.split()[c][m])
        mask(c, False)
    olk = ["ol%d" % c for c in range(NC)] + ["olt"]
    dma("s", [(T.l0d[:], T.ol[:])], "dlb", olk, ["l0d"], 130e3)
    send(to_all(T.l0d, T.l0r, "l0a"), ["l0d"], "l0a")
    arrives("pxn", 4 * nn, "pxrn", "pxn", 2 * HOP)
    dma("y", [(T.xi[16 * a:16 * b, RH * h:RH * h + RH], T.pnr[8 * h + a:8 * h + b]) for h in (0, 1) for a, b in nears],
        "dxn", ["pxrn", "w"], ["xi.n"], 540e3)
    for k in (0, 2, 1, 3):
        for q in far:
            straight = k % 2 and not lay[q][2][0]
            arrives("px%d%d" % (k, q), 1, "pxr%d%d" % (k, q), "pxf%d" % (k % 2),
                    (5 if straight else 2 + k % 2 + 2 * len(lay[q][2][k // 2])) * HOP)
            dma("y", [(T.xi[16 * q:16 * q + 16, RQ * k:RQ * k + RQ], T.pxr[8 * k + q])], "dx%d" % k,
                ["pxr%d%d" % (k, q), "w"], ["xi.f%d%d" % (k, q)], 45e3)
    arrives("l0a", 14, "l0r", "l0a", HOP + 1)
    land("s", T.om, T.l0r, T.ol, "dl0", ["l0r"] + olk, "om", 130e3)
    later_lists(1, ["pxr3%d" % q for q in far])
    later_lists(2, ["om"] + ["xi.f3%d" % q for q in far])
    for k in (0, 2, 1, 3):
        op("v", "copy", (T.xf[:, RQ * k:RQ * k + RQ], T.xi[:, RQ * k:RQ * k + RQ]),
           ["xi.own", "xi.n"] + ["xi.f%d%d" % (k, q) for q in far], keys("xf", 44 * k, 44 * k + 59), RQ)
    vts(T.oh[:], T.om[:, 0:512], float(R), None, (A.min,), ["om"], ["oh%d" % c for c in range(NC)], 256)
    thresholds()
    for t in range(3):
        for c in range(NC):
            if t:
                for m in range(2):
                    look(t, c, m, LOOKS.split()[c][m])
                mask(c)
            see(t, c)
        if t:
            places(t)
            rounded()
        for c in range(NC):
            carve(t, c)
        if not t:
            rays()
            places(t)
        if t < 2:
            lists_land(t + 2, "ea%d" % (NC - 2))
            prepare(t + 1)
            for step in range(2):
                for p, (a, b) in enumerate(PIECES):
                    flags(t, step, p, a, b)
                    move(t, step, a, b, (step, p) in GATHERS)
            row_of_w()
        if t == 0:
            later_lists(3, ["w"])
    for p, (a, b) in enumerate(LAST):
        for step in range(2):
            flags(2, step, p, a, b)
            move(2, step, a, b, step == 1 and p in LASTG)
        if p == len(LAST) - 1:
            cursors()
        home(p, a, b)
    for p, (a, b) in enumerate(LAST):
        src, d = T["or%d" % p], slice(16 * a, 16 * b)
        arrives("on%d" % p, 2 * nn, "orn%d" % p, "ri%d" % p, HOP)
        dma("s", [(T.yx[16 * x:16 * y, d], src[2 * x:2 * y]) for x, y in nears], "dz", ["orn%d" % p, "sg110"], [], 0)
        arrives("of%d" % p, 2 * nf, "orf%d" % p, "ri%d" % p, 3 * HOP)
        dma("s", [(T.yx[16 * fa:16 * fb, d], src[2 * fa:2 * fb])], "dz", ["orf%d" % p, "sg110"], [], 0)
    arrives("ca", 14, "cr", "ca", HOP + 1)
    dma("s", [(T.yc[16 * x:16 * y, :], T.cr[x:y]) for x, y in others], "dz", ["cr", "sg110"], [], 0)
    for i in order_of_issue(prog):
        issue[i]()
    waits("g", [(s, cnt[s]) for s in cnt])
